import numpy as np, ml_dtypes
CORES = [23,119,17,113]
N = 4
BF = ml_dtypes.bfloat16
P, CAP, J, W, D, RO = 512, 128, 8, 8192, 3, 9
WT = np.array([1, 3, 7, 13, 21, 35, 49, 67, 85, 107, 129, 155, 181, 211, 241, 253], np.int32)
KA = np.array([17, 101, 263, 389, 547, 701, 859, 1021], np.int32)
def mark(s):
    return np.add.reduce(s * WT[:, None], axis=-2) & 4095
def columns(u, e):
    return ((u * u >> 4)[..., None, :] + KA[:, None] * u[..., None, :] + 811 * e) & (W - 1)
def lanes(rng, v, k):
    return np.minimum((rng.random((N, 8, 16, k), dtype=np.float32) * (v + 1)[:, None, None]).astype(np.int32), v[:, None, None])
def toward(s, r):
    z = np.array(s); z[0] = (s[0] & (64 - N)) + ((s[0] + r - mark(s)) & (N - 1))
    return z
def pack(o, s, c):
    return {"opr": np.ascontiguousarray(o.reshape(N, 128, W)).astype(np.float32).astype(BF), "s0": np.ascontiguousarray(s.reshape(N, 128, P)).astype(np.float32).astype(BF),
            "f0": np.ascontiguousarray(c).astype(np.int32)}
def setup_inputs(rng):
    t = rng.permutation(8); v = np.full(8, 63); v[t[0]] = rng.choice(np.array([1, 3])); v[t[1]] = 15
    span = rng.choice(np.array([40, 100, 200, 400]), (8, 1)); span[t[0]] = 1
    c = (rng.random((N, 8, P)) * (span + 1)).astype(np.int64)
    c = np.where(rng.random((N, 8, P)) < rng.choice(np.array([0.0, 0.1, 0.3]), (N, 8, 1)), 1023, c)
    return pack(lanes(rng, v, W), lanes(rng, v, P), c)
def setup_inputs_spread(rng):
    o = np.minimum((np.exp2(6 * rng.random((N, 8, 1, W))) * rng.random((N, 8, 16, W))).astype(np.int64), 63)
    s = np.minimum((np.exp2(6 * rng.random((N, 8, 1, P))) * rng.random((N, 8, 16, P))).astype(np.int64), 63)
    c = np.minimum(np.exp2(10 * rng.random((N, 8, P))).astype(np.int64) - 1, 1022)
    return pack(o, s, np.where(rng.random((N, 8, P)) < 0.125, 1023, c))
def setup_inputs_ends(rng):
    o = 63 * rng.integers(0, 2, (N, 8, 16, W)); s = 63 * rng.integers(0, 2, (N, 8, 16, P))
    share = rng.permutation(np.array([1.0, 1.0, 1.0, 0.9, 0.7, 0.5, 0.3, 0.1]))
    c = np.where(rng.random((N, 8, P)) < share[:, None], 0, 1023)
    m = 63 * ((np.arange(65536)[:, None] >> np.arange(16)) & 1)
    u = np.arange(4096); free = np.zeros((4096, 16), np.int64)
    free[:, 15] = u // 253; free[:, 4] = (u % 253) // 21; free[:, 0] = (u % 253) % 21
    every = columns(mark(free.T), 0)
    for k, x in ((P - 3, int(np.max(every))), (P // 2, int(np.min(every)))):
        for b in (m, free):
            z = np.nonzero(np.any(columns(mark(b.T), 0) == x, axis=0))[0]
            if len(z):
                s[:, :, :, k] = b[rng.choice(z, (N, 8))]; c[:, :, k] = 0
                break
    s[..., [0, 1, P - 2, P - 1]] = 63; c[..., [0, P - 1]] = 0; c[..., [1, P - 2]] = 1023
    a = columns(mark(np.full((16, 1), 63)), 0)[:, 0]
    o[..., a[0]] = 0; o[..., a[J - 1]] = 63
    return pack(o, s, c)
def setup_inputs_corners(rng):
    t = rng.permutation(8); v = np.full(8, 63); v[t[6]] = 1; v[t[7]] = 7
    o = lanes(rng, v, W); s = lanes(rng, v, P); c = np.full((N, 8, P), 1023); n = CAP // J; big = int(rng.integers(0, N))
    o[:, t[7]] = 0; c[:, t[0]] = 0; c[N - 1, t[2], P - 1] = 0
    c[:, t[6]] = rng.integers(1012, 1024, (N, P)); c[:, t[7]] = rng.integers(0, 101, (N, P))
    a = columns(mark(np.full((16, 1), 63)), 0)[:, 0]
    for q in range(N):
        for k in (3, 4, 5):
            g = int(t[k]); x = rng.integers(0, 16, 16); x[0] = 0
            x[0] = (q + 1 - int(mark(x[:, None])[0])) & (N - 1)
            o[q, g][:, a] = (63 - x)[:, None]; b = 300 - (int(np.add.reduce(x)) >> 2)
            if k == 5: c[q, g] = np.where(rng.random(P) < 0.5, rng.integers(400, 700, P), 1023)
            w = n + k - 3 if k < 5 else n + 1 if q == big else int(rng.integers(0, n + 1))
            p = np.append(P - 1, rng.permutation(P - 1))[:w]
            s[q, g][:, p] = 63; c[q, g, p] = b
            if k == 4: c[q, g, p[-1]] = b + 1
    return pack(o, s, c)
def setup_inputs_edges(rng):
    t = [int(k) for k in rng.permutation(8)]; v = np.full(8, 63); v[t[7]] = 15
    n = CAP // J; r = int(rng.integers(0, N)); big = int(rng.integers(0, N)); top = int(rng.integers(520, 1001))
    o = lanes(rng, v, W); s = lanes(rng, v, P)
    c = (rng.random((N, 8, P)) * rng.choice(np.array([41, 101, 201]), (8, 1))).astype(np.int64)
    c = np.where(rng.random((N, 8, P)) < 0.1, 1023, c)
    o[:, t[:3]] = 0; c[:, t[0]] = rng.integers(1, 201, (N, P)); c[:, t[1:5]] = 1023
    for q in range(N):
        for k in range(3):
            w = n if k == 1 else n + (k == 0) if q == big else int(rng.integers(0, n + 1))
            p = np.append(P - 1, rng.permutation(P - 1))[:w]
            z = toward(s[q, t[k]][:, p], r)
            if k == 0: z = 0 * z
            s[q, t[k]][:, p] = z; h = np.add.reduce(z, axis=0) >> 2
            if k == 0: c[q, t[k], p] = 0
            elif k == 1: c[q, t[k], p] = top + np.arange(q * n, q * n + n) * 8 // (N * n) - 2 * h
            else: c[q, t[k], p] = 1022 - 2 * h
    for k in (3, 4):
        x = t[k]; z = rng.integers(1, 8, 16); z[0] += (2 - int(mark(z[:, None])[0])) & 3
        h = int(np.add.reduce(z)) >> 2; o[:, x] = rng.integers(56, 64, (N, 16, W))
        for e in range(D): o[:, x, :, int(columns(mark(z[:, None]), e)[0, 0])] = 0
        q = rng.permutation(N); a = int(q[0]); p = np.append(P - 1, rng.permutation(P - 1))[:CAP + 1]
        if k == 3: b = int(q[1]); low = 1022 - 3 * h; more = 1
        else: b = a; low = int(rng.integers(850, 911)); more = h
        s[a, x][:, p[1:]] = z[:, None]; c[a, x, p[1:]] = low + more
        s[b, x, :, P - 1] = z; c[b, x, P - 1] = low
    return pack(o, s, c)
def setup_inputs_ties(rng):
    v = rng.permutation(np.array([1, 1, 3, 3, 7, 15, 31, 63])); o = lanes(rng, v, W); s = lanes(rng, v, P)
    c = rng.choice(np.array([0, 5, 9]), (1, 8, 1)) + rng.integers(0, 2, (N, 8, P)) * rng.choice(np.array([0, 1, 3]), (1, 8, 1))
    s[:, 1::2, :, P // 2:] = s[:, 1::2, :, :P // 2]
    c = np.where(rng.random((N, 8, P)) < 0.05, 1023, c)
    x = int(np.nonzero(v == 1)[0][0]); y = int(np.nonzero(v == 3)[0][0])
    o[:, x] = 0; c[:, x] = 1023
    s[:, x] = rng.integers(0, 64, (N, 16, P)); s[:, x, 0] = np.maximum(s[:, x, 0], 4)
    for q in range(N):
        p = np.append(P - 1, rng.permutation(P - 1))[:CAP // J]
        a = np.add.reduce(s[q, x][:, p], axis=0) >> 2
        c[q, x, p] = 1022 - a - rng.integers(0, a)
    z = rng.integers(1, 8, 16); z[0] += (2 - int(mark(z[:, None])[0])) & 3
    a = int(np.add.reduce(z)) >> 2; b = int(rng.integers(850, 931))
    o[:, y] = rng.integers(56, 64, (N, 16, W)); c[:, y] = 1023
    for e in range(D): o[:, y, :, int(columns(mark(z[:, None]), e)[0, 0])] = 0
    q = rng.permutation(N); p = rng.permutation(P)[:CAP]
    s[int(q[0]), y][:, p] = z[:, None]; c[int(q[0]), y, p] = b + a
    s[int(q[1]), y, :, P - 1] = z; c[int(q[1]), y, P - 1] = b
    return pack(o, s, c)
def check_inputs(d):
    bad = []
    for k, lo, hi in (("opr", 0, 63), ("s0", 0, 63), ("f0", 0, 1023)):
        x = np.asarray(d[k]).astype(np.float64)
        if not (np.min(x) >= lo and np.max(x) <= hi): bad.append("range of " + k)
        elif np.any(x != np.floor(x)): bad.append("whole numbers of " + k)
    return bad
def reference(opr, s0, f0):
    o = opr.astype(np.float32).astype(np.int32).reshape(N, 8, 16, W); gi = np.arange(8)
    S = np.zeros((N, 8, D + 1, 16, P), np.int32); F = np.full((N, 8, D + 1, P), 1023, np.int32)
    S[:, :, 0] = s0.astype(np.float32).astype(np.int32).reshape(N, 8, 16, P); F[:, :, 0] = f0
    lo = np.zeros((8, D), np.int32); hi = np.zeros((8, D), np.int32); U = np.full(8, 1023, np.int32); lev = np.zeros(8, np.int32)
    for rnd in range(RO):
        s = S[:, gi, lev]; f = F[:, gi, lev]; low = lo[gi, lev][:, None]
        h = columns(mark(s), lev[:, None, None]).reshape(N, 8, 1, J * P)
        c = np.abs(np.tile(s, (1, 1, 1, J)) - np.take_along_axis(o, h.astype(np.int64), axis=3))
        fc = np.tile(f, (1, 1, J)) + (np.add.reduce(c, axis=2) >> 2); own = mark(c) & (N - 1)
        B = np.full(8, 1023, np.int32)
        for a in range(N):
            x = np.partition(np.where((fc >= low) & (own == a), fc, 4000), CAP, axis=2)[:, :, CAP]
            B = np.minimum(B, np.min(x, axis=0))
        keep = (fc >= low) & (fc < B[:, None])
        m = np.min(np.where(keep, fc, 4000), axis=(0, 2))
        ns = np.zeros((N, 8, 16, P), np.int32); nf = np.full((N, 8, P), 1023, np.int32)
        for a in range(N):
            k = keep & (own == a); place = np.add.accumulate(k, axis=2, dtype=np.int64) - 1
            qi, ji, ci = np.nonzero(k); t = qi * CAP + place[qi, ji, ci]
            ns[a, ji, :, t] = c[qi, ji, :, ci]; nf[a, ji, t] = fc[qi, ji, ci]
        S[:, gi, lev + 1] = ns; F[:, gi, lev + 1] = nf; hi[gi, lev] = B
        U = np.where(lev == D - 1, np.minimum(U, m), U)
        for g in range(8):
            e = int(lev[g])
            if e == D - 1 or m[g] >= U[g]:
                lo[g, e] = max(int(B[g]), int(lo[g, e]) + 1)
                if lo[g, e] >= U[g] and e > 0:
                    lo[g, e] = 0; e -= 1; lo[g, e] = max(int(hi[g, e]), int(lo[g, e]) + 1)
            else:
                e += 1; lo[g, e] = 0
            lev[g] = e
    yl = np.ascontiguousarray(S[:, :, 1:].transpose(0, 1, 3, 2, 4)).reshape(N, 128, D * P)
    yt = np.concatenate([lo, hi, lev[:, None], U[:, None]], axis=1)
    return {"yl": yl.astype(np.float32).astype(BF), "yf": np.ascontiguousarray(F[:, :, 1:]).reshape(N, 8, D * P).astype(np.float32), "yt": np.stack([yt] * N).astype(np.float32)}

@@ -1,0 +1,572 @@
+from concourse.bass import DstId, RemoteDMATransfer
+from concourse.mybir import AluOpType as A, AxisListType, ActivationFunctionType as F
+
+RO = 9
+NSLOT = RO + 2
+KA = [17, 101, 263, 389, 547, 701, 859, 1021]
+WTS = [1, 3, 7, 13, 21, 35, 49, 67, 85, 107, 129, 155, 181, 211, 241, 253]
+CW = 4112
+
+SCRATCH = {"PS": ("psum", [128, 4096], "float32")}
+for _dt, _names in (
+        ("bfloat16", "OPS:8192 CH:4112 FB:4112 DY:4096 SS:512 SF:512 IN0:1024 SC:1024 DD:1024 STEP:1024 IND:4096 CCR:512 MSG:1024 CN:32"
+                     " TLM:128 WMARK:144 WF0:144 WF1:144 SEL4:16 MASKG:16 IDENT:128 ONES:128 TRI:128 SHIFT:128 IMS:128 CS0:128 CS1:128"
+                     " CM:128 QALL:128 LANEG:128 BO:128 BCF:128 BLK:128 TMPA:128 TMPB:128 DIAG:2048 KK:512 RST:512 OWF:256"),
+        ("float16", "KEY:1024 RH:4 BH:4 WT0:160 WT1:160"),
+        ("float32", "BML:144 UF:64 KU:256 KMAT:256 PEN:256 CC:256 CP:256 SG:32 SELC:64 SP:16 TS:4 MT:32 MTT:32 MM:4 ST:16 LT:128"
+                    " COL:32 WROW:48 LQ:16 HM:2 I3:8 PWC:32 K1:32 K2:32 YT:8 PW0:32 PW1:32 PW2:32 RE0:16 WX:192"),
+        ("int32", "FL:512 UI:128 OFP:256 OFM:256 LI:64 I1:256 OW:256 T4:256 CI:160 C5:128 C4:128 CL:128 RF:132 RF2:132 CM3:16 TI:8 WI:4"
+                  " F0:512 FH:512 FD:512 FE:512 FG:512"),
+        ("uint16", "OFU:256 OFS:32 LU:32 LCU:32 REP:16")):
+    for _n in _names.split():
+        _n, _c = _n.split(":")
+        SCRATCH[_n] = ("sbuf", [128, int(_c)], _dt)
+SCRATCH["XF"] = ("sbuf", [128, NSLOT * 1024], "bfloat16")
+for _l in (1, 2, 3):
+    for _n, _c, _dt in (("FS", 512, "bfloat16"), ("FC", 512, "bfloat16"), ("FV", 512, "float32"), ("FA", 512, "bfloat16"),
+                        ("FN", 512, "bfloat16"), ("FO", 64, "uint16"), ("OS", 1024, "bfloat16"), ("OV", 1024, "float32")):
+        SCRATCH[_n + str(_l)] = ("sbuf", [128, _c], _dt)
+
+SEMAPHORES = (["qV", "qS", "qP", "qG", "ld0", "ld1", "ld2", "out", "lsb", "lsd"]
+              + ["bm%d" % r for r in range(RO)] + ["dat%d" % r for r in range(RO)])
+
+
+def rank_program(g, core, T, topo):
+    rank = T.rank_of(core)
+    if rank is None:
+        return
+    cores = list(T.cores)
+    eng = {"V": g.vector, "S": g.scalar, "P": g.tensor, "G": g, "Y": g.sync}
+    qs = {"V": "qV", "S": "qS", "P": "qP", "G": "qG"}
+    cnt, snap, lastw, readers = {}, {}, {}, {}
+    known = {q: {} for q in eng}
+
+    def need(q, toks):
+        best = {}
+        for s, v in toks:
+            if known[q].get(s, 0) < v:
+                best[s] = max(best.get(s, 0), v)
+        for s in sorted(best):
+            v = best[s]
+            if known[q].get(s, 0) < v:
+                eng[q].wait_ge(T.sem[s], v)
+                known[q][s] = v
+                for s2, v2 in snap.get((s, v), {}).items():
+                    known[q][s2] = max(known[q].get(s2, 0), v2)
+
+    def deps(q, r, w):
+        own = qs.get(q)
+        toks = []
+        for k in r:
+            if k in lastw:
+                toks.append(lastw[k])
+            if k[:2] == "ps":
+                toks += [t for t in readers.get(k, {}).items() if t[0] != own]
+        for k in w:
+            k, more = k.rstrip("+"), k[-1] == "+" or k[:2] == "ps"
+            if k in lastw and not (more and lastw[k][0] == own):
+                toks.append(lastw[k])
+            toks += readers.get(k, {}).items()
+        return toks
+
+    def mark(q, tok, r, w):
+        snap[tok] = dict(known[q])
+        for k in r:
+            readers.setdefault(k, {})[tok[0]] = tok[1]
+        for k in w:
+            k = k.rstrip("+")
+            lastw[k] = tok
+            readers[k] = {}
+
+    def do(q, f, r, w):
+        r, w = r.split(), w.split()
+        need(q, deps(q, r, w))
+        s = qs[q]
+        f(eng[q]).then_inc(T.sem[s], 1)
+        cnt[s] = cnt.get(s, 0) + 1
+        mark(q, (s, cnt[s]), r, w)
+
+    def dma(q, sem, pairs, r, w):
+        r, w = r.split(), w.split()
+        need(q, deps(q, r, w))
+        for out, in_ in pairs:
+            eng[q].dma_start(out, in_).then_inc(T.sem[sem], 16)
+            cnt[sem] = cnt.get(sem, 0) + 16
+        mark(q, (sem, cnt[sem]), r, w)
+
+    def V(f, r, w):
+        do("V", f, r, w)
+
+    def ts(r, w, out, i, s1, o0, s2=None, o1=None):
+        if o1 is None:
+            V(lambda e: e.tensor_scalar(out, i, s1, None, o0), r, w)
+        else:
+            V(lambda e: e.tensor_scalar(out, i, s1, s2, o0, o1), r, w)
+
+    def tt(r, w, out, a, b_, op):
+        V(lambda e: e.tensor_tensor(out, a, b_, op), r, w)
+
+    def cp(r, w, out, i):
+        V(lambda e: e.tensor_copy(out, i), r, w)
+
+    def red(r, w, out, i, op):
+        V(lambda e: e.tensor_reduce(out, i, AxisListType.X, op), r, w)
+
+    def fill(w, out, c):
+        V(lambda e: e.memset(out, c), "", w)
+
+    def scan(r, w, out, i):
+        V(lambda e: e.tensor_tensor_scan(out, T.RST[:], i, 0.0, A.mult, A.add), r, w)
+
+    def mm(r, w, out, l, r_, st=True, sp=True):
+        do("P", lambda e: e.matmul(out, l, r_, st, sp), r, w)
+
+    def act(r, w, out, i, fn, **k):
+        do("S", lambda e: e.activation(out, i, fn, **k), r, w)
+
+    def b(k, x, y, st=1):
+        return T.PS[:, k * 512 + x:k * 512 + y:st] if st > 1 else T.PS[:, k * 512 + x:k * 512 + y]
+
+    def plan(src):
+        off = [c for c in cores if topo.chip(c) != topo.chip(src)]
+        on = [c for c in cores if topo.chip(c) == topo.chip(src) and c != src]
+        base = list(topo.engines(src, off[0]))
+        rest = [e for e in topo.engines(src, on[0]) if e not in base]
+        out = {}
+        for cs, es in ((off, base), (on, rest)):
+            p = len(es) // len(cs)
+            for i, c in enumerate(cs):
+                out[c] = es[i * p:(i + 1) * p]
+        return out
+
+    mine = plan(core)
+    arrive = sum(len(plan(c)[core]) for c in cores if c != core)
+
+    def send(name, r, local, src_of, dst, keys):
+        keys = keys.split()
+        need("G", deps("G", keys, []))
+        tr = []
+        for c, en in mine.items():
+            rid, pid, _ = topo.addr(c)
+            tr.append(RemoteDMATransfer(dst_ids=[DstId(rid=rid, pnc=pid)], dma_engine_mask=sum(1 << e for e in en),
+                                        remote_sem=T.sem["%s%d" % (name, r)], srcs=[src_of(cores.index(c))], dsts=[dst]))
+        g.remote_dma_fused(tr, local_sem=T.sem[local])
+        cnt[local] = cnt.get(local, 0) + sum(len(en) for en in mine.values())
+        mark("G", (local, cnt[local]), keys, [])
+        lastw["%s%d" % (name, r)] = ("%s%d" % (name, r), arrive)
+
+    fill("F0", T.F0[:], 0)
+    dma("S", "ld0", [(T.XF[:, q * 256:q * 256 + 128], T.s0[:, q * 128:(q + 1) * 128]) for q in range(4)], "", "XF0s")
+    dma("S", "ld1", [(T.F0[0::16, :], T.f0[:]), (T.F0[1::16, :], T.f0[:])], "", "F0")
+    dma("Y", "ld2", [(T.OPS[:], T.opr[:])], "", "OPS")
+
+    def iota(w, out, pat, base=0, cm=0, small=False):
+        if small:
+            do("G", lambda e: e.iota(out, pat, base, cm, allow_small_or_imprecise_dtypes=True), "", w)
+        else:
+            do("G", lambda e: e.iota(out, pat, base, cm), "", w)
+
+    iota("TI", T.TI[:, 0:1], [[1, 1]], 0, 1)
+    iota("CI", T.CI[:], [[1, 160]])
+    iota("PW0", T.PW0[:], [[256, 4], [16, 8]], small=True)
+    iota("RF", T.RF[:], [[1, 33], [1000, 4]], -3000)
+    iota("CM3", T.CM3[:], [[0, 4], [1, 4]])
+    iota("RE0", T.RE0[:], [[0, 8], [16, 2]], small=True)
+    iota("C4", T.C4[:], [[1, 8], [0, 16]])
+    iota("CL", T.CL[:], [[0, 8], [1, 16]])
+    iota("C5", T.C5[:], [[1, 4], [0, 32]])
+    iota("KK", T.KK[:], [[0, 4], [1, 16], [16, 8]], small=True)
+    iota("PW1", T.PW1[:], [[0, 4], [16, 8]], small=True)
+    iota("PW2", T.PW2[:], [[16, 32]], small=True)
+
+    def C(k):
+        return T.COL[:, k:k + 1]
+    cp("TI", "c0", C(0), T.TI[:, 0:1])
+    for k, sh, an in ((1, 0, 15), (2, 4, 7), (3, 0, 31), (4, 5, 3), (6, 4, 1)):
+        ts("TI", "TI%d" % k, T.TI[:, k:k + 1], T.TI[:, 0:1], sh, A.logical_shift_right, an, A.bitwise_and)
+    for k in (1, 2, 3, 4, 6):
+        cp("TI%d" % k, "c%d" % k, C(k), T.TI[:, k:k + 1])
+    for i in range(16):
+        fill("wr+", T.WROW[:, i:i + 1], WTS[i])
+    ts("CI c1", "wm", T.WROW[:, 16:32], T.CI[:, 0:16], C(1), A.is_equal)
+    tt("wr wm", "wx", T.WROW[:, 32:48], T.WROW[:, 0:16], T.WROW[:, 16:32], A.mult)
+    red("wx", "c7", C(7), T.WROW[:, 32:48], A.add)
+    tt("c0 c1", "c12", C(12), C(0), C(1), A.subtract)
+    ts("c12", "c13", C(13), C(12), 15.0, A.add)
+    ts("CI c13 c7", "WMARK", T.WMARK[:, 0:143], T.CI[:, 0:143], C(13), A.is_equal, C(7), A.mult)
+    ts("PW0 c1", "PWC", T.PWC[:], T.PW0[:], C(1), A.add)
+    ts("RE0 c1", "REP", T.REP[:], T.RE0[:], C(1), A.add)
+    for j in range(8):
+        fill("KMAT+", T.KMAT[:, j * 32:(j + 1) * 32], KA[j])
+    cp("c7", "wi0", T.WI[:, 0:1], C(7))
+    ts("wi0", "wi1", T.WI[:, 1:2], T.WI[:, 0:1], 3, A.bitwise_and)
+    ts("wi1", "c8", C(8), T.WI[:, 1:2], -1024.0, A.mult, 2049.0, A.add)
+    ts("c1", "c9", C(9), C(1), 0.0, A.is_equal, 31.0, A.mult)
+    ts("c1", "c10", C(10), C(1), 3.5, A.is_lt)
+    tt("c9 c10", "c11", C(11), C(9), C(10), A.add)
+    ts("c4", "c14", C(14), C(4), 32.0, A.mult, 31.0, A.add)
+    ts("c6", "c15", C(15), C(6), 1000.0, A.mult)
+    ts("c6", "c16", C(16), C(6), -1000.0, A.mult, 1000.0, A.add)
+    ts("c0", "c17", C(17), C(0), 1.0, A.add)
+    ts("c4", "c5", C(5), C(4), 2.0, A.mult)
+    ts("c5", "c18", C(18), C(5), 1.0, A.add)
+    ts("c3", "c28", C(28), C(3), 1.5, A.is_gt, 1000.0, A.mult)
+    ts("c3 c28 c5", "c19", C(19), C(3), C(28), A.add, C(5), A.add)
+    ts("c1", "c20", C(20), C(1), 0.0, A.is_equal, 32.0, A.mult)
+    ts("RF", "RF2", T.RF2[:], T.RF[:], 3, A.arith_shift_right)
+    WT, WF, CS = (T.WT0, T.WT1), (T.WF0, T.WF1), (T.CS0, T.CS1)
+    for h in (0, 1):
+        tt("c14 c%d" % (15 + h), "c%d" % (21 + h), C(21 + h), C(14), C(15 + h), A.add)
+        tt("c4 c%d" % (15 + h), "c%d" % (23 + h), C(23 + h), C(4), C(15 + h), A.add)
+        ts("c6", "HM+", T.HM[:, h:h + 1], C(6), float(h), A.is_equal)
+        ts("CI c8 c%d" % (21 + h), "WT+", WT[h][:, 0:159], T.CI[:, 0:159], C(21 + h), A.is_equal, C(8), A.mult)
+        ts("RF2 c11 c%d" % (23 + h), "WF+", WF[h][:, 0:132], T.RF2[:], C(23 + h), A.is_equal, C(11), A.mult)
+    ts("F0", "FH", T.FH[:], T.F0[:], 5, A.logical_shift_right)
+    ts("F0", "FD", T.FD[:], T.F0[:], 31, A.bitwise_and)
+    ts("c1", "c26", C(26), C(1), 0.0, A.is_equal)
+    ts("c1", "c27", C(27), C(1), 1.0, A.is_equal)
+    ts("FH c26", "FE", T.FE[:], T.FH[:], C(26), A.mult)
+    ts("FD c27", "FG", T.FG[:], T.FD[:], C(27), A.mult)
+    for q in range(4):
+        tt("FE FG", "XF0c+", T.XF[:, q * 256 + 128:q * 256 + 256], T.FE[:, q * 128:q * 128 + 128], T.FG[:, q * 128:q * 128 + 128], A.add)
+    fill("XF1m", T.XF[:, 1024:2048], 0.0)
+    for q in range(4):
+        x = T.XF[:, 1024 + q * 256 + 128:1024 + q * 256 + 256]
+        ts("XF1m c20", "XF1+", x, x, 0.0, A.mult, C(20), A.add)
+    fill("FBm", T.FB[:], 0.0)
+    ts("FBm c20", "FBz", T.FB[:, 4096:CW], T.FB[:, 4096:CW], 0.0, A.mult, C(20), A.add)
+    ci = T.CI[:, 0:128]
+    ts("C4 c2", "BO", T.BO[:], T.C4[:], C(2), A.is_equal)
+    ts("CL", "TA", T.TMPA[:], T.CL[:], 1.5, A.is_gt)
+    ts("CL", "TB", T.TMPB[:], T.CL[:], 3.5, A.is_lt)
+    tt("TA TB", "L1", T.LANEG[:], T.TMPA[:], T.TMPB[:], A.mult)
+    tt("L1 BO", "TA", T.TMPA[:], T.LANEG[:], T.BO[:], A.mult)
+    ts("CL", "TB", T.TMPB[:], T.CL[:], 1.0, A.add)
+    tt("TA TB", "L1", T.LANEG[:], T.TMPA[:], T.TMPB[:], A.mult)
+    ts("L1", "LANEG", T.LANEG[:], T.LANEG[:], -1.0, A.add)
+    ts("C5 c4", "BLK", T.BLK[:], T.C5[:], C(4), A.is_equal)
+    ts("BLK", "QALL", T.QALL[:], T.BLK[:], 0.0625, A.mult)
+    fill("lo hi last e U", T.ST[:], 0.0)
+    fill("last", T.ST[:, 6:9], 1024.0)
+    fill("U", T.ST[:, 10:11], 1023.0)
+    cp("CI", "I3", T.I3[:, 0:3], T.CI[:, 0:3])
+    ts("CI", "J3", T.I3[:, 4:7], T.CI[:, 0:3], 1.0, A.add)
+    LO, HI, LA, EE, UU = T.ST[:, 0:3], T.ST[:, 3:6], T.ST[:, 6:9], T.ST[:, 9:10], T.ST[:, 10:11]
+    lt = {}
+
+    def L(name, k=1):
+        if name not in lt:
+            lt[name] = (sum(v[1] for v in lt.values()), k)
+        x, k = lt[name]
+        return T.LT[:, x:x + k]
+
+    def L1(name, i):
+        x = lt[name][0] + i
+        return T.LT[:, x:x + 1]
+
+    def derive():
+        ts("J3 e", "oh1", L("oh1", 3), T.I3[:, 4:7], EE, A.is_equal)
+        ts("e", "e1", L("e1"), EE, 1.0, A.add)
+        tt("oh1 last", "sl", L("sl", 3), L("oh1"), LA, A.mult)
+        ts("LANEG e1", "TLM", T.TLM[:], T.LANEG[:], L("e1"), A.is_equal)
+        red("sl", "slot", L("slot"), L("sl"), A.add)
+        ts("e", "e811", L("e811"), EE, 811.0, A.mult)
+        ts("PWC slot", "OFS", T.OFS[:], T.PWC[:], L("slot"), A.add)
+        tt("oh1 hi", "th", L("th", 3), L("oh1"), HI, A.mult)
+        ts("I3 e", "oh", L("oh", 3), T.I3[:, 0:3], EE, A.is_equal)
+        red("th", "th1", L("th1"), L("th"), A.add)
+        tt("oh lo", "ol", L("ol", 3), L("oh"), LO, A.mult)
+        ts("I3 e", "noh", L("noh", 3), T.I3[:, 0:3], EE, A.not_equal)
+        ts("oh th1", "thr", L("thr"), L1("oh", 0), 2000.0, A.mult, L("th1"), A.add)
+        red("ol", "loe", L("loe"), L("ol"), A.add)
+        ts("HM thr", "RH2", T.RH[:, 2:4], T.HM[:], L("thr"), A.mult)
+        ts("HM loe", "RH0", T.RH[:, 0:2], T.HM[:], L("loe"), A.mult)
+
+    derive()
+
+    def search_constants():
+        ts("CI c0", "IDENT", T.IDENT[:], ci, C(0), A.is_equal)
+        ts("CI c4", "SEL4", T.SEL4[:, 0:4], T.CI[:, 0:4], C(4), A.is_equal)
+        ts("CM3 c4", "MASKG", T.MASKG[:], T.CM3[:], C(4), A.not_equal, -8192.0, A.mult)
+        fill("ONES", T.ONES[:], 1.0)
+        fill("MTm", T.MT[:], 3000.0)
+
+    late = [lambda: ts("CI c0", "TA", T.TMPA[:], ci, C(0), A.is_gt),
+            lambda: ts("CI c17", "TB", T.TMPB[:], ci, C(17), A.is_equal),
+            lambda: fill("RSTm", T.RST[:], 1.0),
+            lambda: tt("TA BLK", "TRI", T.TRI[:], T.TMPA[:], T.BLK[:], A.mult),
+            lambda: tt("TB BLK", "SHIFT", T.SHIFT[:], T.TMPB[:], T.BLK[:], A.mult),
+            lambda: V(lambda e: e.memset(T.RST[:, 0::128], 0.0), "RSTm", "RST"),
+            lambda: tt("IDENT SHIFT", "IMS", T.IMS[:], T.IDENT[:], T.SHIFT[:], A.subtract),
+            lambda: ts("C4 c5", "CS", T.CS0[:], T.C4[:], C(5), A.is_equal),
+            lambda: ts("C4 c18", "CS+", T.CS1[:], T.C4[:], C(18), A.is_equal),
+            lambda: ts("C4 c19", "CM", T.CM[:], T.C4[:], C(19), A.is_equal),
+            lambda: fill("CHz", T.CH[:, 4096:CW], 0.0),
+            lambda: ts("CI c1", "LQ", T.LQ[:], T.CI[:, 0:16], C(1), A.is_equal, 128.0, A.mult)]
+    late += [lambda q=q: fill("BMo%d" % q, T.BML[:, q * 16 + rank * 4:q * 16 + rank * 4 + 4], 0.0) for q in range(RO)]
+    late += [lambda q=q: ts("CI c0 LQ", "DIAG+", T.DIAG[:, q * 128:(q + 1) * 128], ci, C(0), A.is_equal, T.LQ[:, q:q + 1], A.mult)
+             for q in range(16)]
+
+    def output_constants():
+        for l in (1, 2, 3):
+            fill("OS%d" % l, T["OS%d" % l][:], 0.0)
+            fill("OV%d" % l, T["OV%d" % l][:], 1023.0)
+        ts("C4 c2", "BCF", T.BCF[:], T.C4[:], C(2), A.is_equal, C(11), A.mult)
+        ts("PW1 c1", "PW1", T.PW1[:], T.PW1[:], C(1), A.add, -128.0, A.mult)
+        ts("PW2 c1", "PW2", T.PW2[:], T.PW2[:], C(1), A.add, 512.0, A.add)
+        ts("PW1", "K1", T.K1[:], T.PW1[:], -513.0 * 128, A.add)
+        ts("PW2", "K2", T.K2[:], T.PW2[:], 16384.0, A.mult)
+
+    xkeys = ["XF0s", "XF0c", "XF1"]
+    SE = T.SELC
+    for r in range(RO):
+        win = (r + 2) * 1024
+        xk = " ".join(xkeys)
+        cp(xk + " OFS", "SS", T.SS[:], T.XF[:, 0:win].indirect(T.OFS[:]))
+        act(xk + " OFS", "SF", T.SF[:], T.XF[:, 128:win].indirect(T.OFS[:]), F.Copy)
+        for q in range(16):
+            mm("WMARK SS", "ps3", b(3, 0, 32), T.WMARK[:, 15 - q:143 - q], T.SS[:, q::16], q == 0, q == 15)
+        mm("TLM SS", "ps4", b(4, 0, 512), T.TLM[:], T.SS[:])
+        u = [T.UI[:, k * 32:(k + 1) * 32] for k in range(4)]
+        cp("ps3", "u0", u[0], b(3, 0, 32))
+        ts("u0", "u1", u[1], u[0], 4095, A.bitwise_and)
+        tt("u1", "u2", u[2], u[1], u[1], A.mult)
+        cp("u1", "uf0", T.UF[:, 0:32], u[1])
+        ts("u2", "u3", u[3], u[2], 4, A.logical_shift_right, 8191, A.bitwise_and)
+        tt("uf0 REP KMAT", "KU", T.KU[:], T.UF[:, 0:32].indirect(T.REP[:]), T.KMAT[:], A.mult)
+        ts("u3 e811", "uf1", T.UF[:, 32:64], u[3], L("e811"), A.add)
+        tt("uf1 REP KU", "OFP", T.OFP[:], T.UF[:, 32:64].indirect(T.REP[:]), T.KU[:], A.add)
+        ts("OFP", "OFM", T.OFM[:], T.OFP[:], 8191, A.bitwise_and)
+        cp("OFM", "OFU", T.OFU[:], T.OFM[:])
+        mm("QALL RH0 RH2", "ps3", b(3, 40, 44), T.QALL[:], T.RH[:])
+        for j in range(8):
+            d = T.DY[:, j * 512:(j + 1) * 512]
+            tt("OPS OFU SS", "DY%d" % j, d, T.OPS[:].indirect(T.OFU[:, j * 32:(j + 1) * 32]), T.SS[:], A.subtract)
+            act("DY%d" % j, "CH%d" % j, T.CH[:, j * 512:(j + 1) * 512], d, F.Abs)
+            for co in range(4 * j, 4 * j + 4):
+                for h in (0, 1):
+                    mm("WT CH%d" % j, "ps%d" % h, b(h, 0, 128), WT[h][:, 31 - co:159 - co], T.CH[:, co * 128:(co + 1) * 128], co == 0, co == 31)
+            if j == 0:
+                ts("ps4", "FL", T.FL[:], b(4, 0, 512), 0.25, A.mult, -0.375, A.add)
+                tt("SF FL FBm", "FB", T.FB[:, 0:512], T.SF[:], T.FL[:], A.add)
+                for h in (0, 1):
+                    for m in range(4):
+                        mm("WF FB", "ps2", b(2, h * 128, h * 128 + 128), WF[h][:, 3 - m:131 - m], T.FB[:, m * 128:(m + 1) * 128], m == 0, m == 3)
+                cp("ps3", "TS", T.TS[:], b(3, 40, 44))
+            if j == 3:
+                for h in (0, 1):
+                    ts("ps2 TS", "PEN+", T.PEN[:, h * 128:h * 128 + 128], b(2, h * 128, h * 128 + 128), T.TS[:, 2 + h:3 + h], A.is_ge, 4000.0, A.mult)
+                tt("ps2 PEN", "ps5", b(5, 0, 256), b(2, 0, 256), T.PEN[:], A.add)
+        if r == 0:
+            search_constants()
+        for h in (0, 1):
+            cp("ps%d" % h, "I1+", T.I1[:, h * 128:h * 128 + 128], b(h, 0, 128))
+        ts("I1", "OW", T.OW[:], T.I1[:], 10, A.arith_shift_right, 3, A.bitwise_and)
+        ts("I1", "T4", T.T4[:], T.I1[:], 1023, A.bitwise_and, 2, A.logical_shift_right)
+        cp("OW", "OWF", T.OWF[:], T.OW[:])
+        for o in range(4):
+            k = 4 if o < 2 else 2
+            act("OWF", "ps%d" % k, b(k, (o % 2) * 256, (o % 2) * 256 + 256), T.OWF[:], F.Square, bias=-64.0 * o, scale=64.0)
+        tt("T4 ps5", "CC", T.CC[:], T.T4[:], b(5, 0, 256), A.add)
+        for h in (0, 1):
+            ts("CC TS", "ps5", b(5, 256 + h * 128, 384 + h * 128), T.CC[:, h * 128:h * 128 + 128], T.TS[:, h:h + 1], A.is_lt, 4000.0, A.mult)
+        tt("CC ps5", "CP", T.CP[:], T.CC[:], b(5, 256, 512), A.add)
+        for h in (0, 1):
+            for o in range(4):
+                k = 4 if o < 2 else 2
+                x = (o % 2) * 256 + h * 128
+                tt("CP ps%d" % k, "KEY%d+" % h, T.KEY[:, h * 512 + o * 128:h * 512 + (o + 1) * 128], T.CP[:, h * 128:h * 128 + 128], b(k, x, x + 128), A.add)
+
+        def dl(h, s):
+            return SE[:, h * 32 + s:h * 32 + s + 1]
+
+        def bs(h, s):
+            return SE[:, h * 32 + 10 + s:h * 32 + 11 + s]
+
+        def vi(h, s):
+            return SE[:, h * 32 + 21 + s:h * 32 + 22 + s]
+
+        for s in range(11):
+            bit = 512 >> s
+            for h in (0, 1):
+                ky, io = T.KEY[:, h * 512:(h + 1) * 512], T.IN0[:, h * 512:(h + 1) * 512]
+                if s > 0:
+                    ts("v%d.%d" % (h, s - 1), "d%d.%d" % (h, s - 1), dl(h, s - 1), vi(h, s - 1), 0.5, A.is_lt, float(512 >> (s - 1)), A.mult)
+                if s == 0:
+                    ts("KEY%d" % h, "IN0%d" % h, io, ky, 512.0, A.is_lt)
+                elif s == 1:
+                    ts("KEY%d d%d.0" % (h, h), "IN0%d" % h, io, ky, dl(h, 0), A.subtract, 256.0, A.is_lt)
+                else:
+                    ts("KEY%d d%d.%d b%d.%d" % (h, h, s - 1, h, s), "IN0%d" % h, io, ky, dl(h, s - 1), A.subtract, bs(h, s), A.is_lt)
+                if s == 10:
+                    continue
+                k = 6 + h
+                pk = "ps%d" % k
+                for o in range(4):
+                    mm("IN0%d SEL4" % h, pk, b(k, o * 4, o * 4 + 4), T.IN0[:, h * 512 + o * 128:h * 512 + (o + 1) * 128], T.SEL4[:, 0:4])
+                act(pk, "CN%d" % h, T.CN[:, h * 16:h * 16 + 16], b(k, 0, 16), F.Copy)
+                mm("IDENT MASKG", pk, b(k, 32, 48), T.IDENT[:], T.MASKG[:], True, False)
+                mm("ONES CN%d" % h, pk, b(k, 32, 48), T.ONES[:], T.CN[:, h * 16:h * 16 + 16], False, True)
+                act(pk, "SG%d v%d.%d" % (h, h, s), T.SG[:, h * 16:h * 16 + 16], b(k, 32, 48), F.Sigmoid, bias=-128.5 * 64, scale=64.0, accum_out=vi(h, s))
+            if s == 0:
+                for h in (0, 1):
+                    red("CP MTm", "MT+", T.MT[:, h:h + 1], T.CP[:, h * 128:h * 128 + 128], A.min)
+                V(lambda e: e.transpose(T.MTT[:], T.MT[:]), "MT MTm", "MTT")
+                red("MTT", "MM0", T.MM[:, 0:1], T.MTT[:], A.min)
+                ts("MM0", "BHm", T.BH[:, 2:3], T.MM[:, 0:1], 2000.0, A.min)
+            for h in (0, 1):
+                if s == 1:
+                    ts("d%d.0" % h, "b%d.2" % h, bs(h, 2), dl(h, 0), 128.0, A.add)
+                elif 2 <= s < 10:
+                    ts("b%d.%d d%d.%d" % (h, s, h, s - 1), "b%d.%d" % (h, s + 1), bs(h, s + 1), bs(h, s), dl(h, s - 1), A.add,
+                       float((bit >> 1) - bit), A.add)
+            for _ in range(4):
+                if s and late:
+                    late.pop(0)()
+        for h in (0, 1):
+            scan("RST IN0%d" % h, "SC%d" % h, T.SC[:, h * 512:(h + 1) * 512], T.IN0[:, h * 512:(h + 1) * 512])
+        for h in (0, 1):
+            ts("d%d.9 b%d.10" % (h, h), "BHb%d" % h, T.BH[:, h:h + 1], dl(h, 9), bs(h, 10), A.add, 0.03125, A.mult)
+        tot = T.SC[:, 127:1024:128]
+        mm("TRI SC0 SC1", "ps3", b(3, 64, 72), T.TRI[:], tot)
+        mm("SHIFT SC0 SC1", "ps3", b(3, 72, 80), T.SHIFT[:], tot)
+        for h in (0, 1):
+            mm("IMS SC%d" % h, "ps%d" % (6 + h), b(6 + h, 0, 512), T.IMS[:], T.SC[:, h * 512:(h + 1) * 512])
+        for h in (0, 1):
+            mm("CS BHb%d" % h, "ps5", b(5, 0, 1), CS[h][:], T.BH[:, h:h + 1], h == 0, h == 1)
+        mm("CM BHm", "ps5", b(5, 1, 2), T.CM[:], T.BH[:, 2:3])
+        cp("ps3", "SP", T.SP[:], b(3, 64, 80))
+        x = r * 16 + rank * 4
+        own = T.BML[:, x:x + 4]
+        cp("ps5", "BMo%d" % r, T.BML[:, x:x + 2], b(5, 0, 2))
+        send("bm", r, "lsb", lambda q: own, own, "BMo%d" % r)
+        for o in range(4):
+            ho = o * 128
+            act("ps6 SP", "DD0%d" % o, T.DD[:, ho:ho + 128], b(6, ho, ho + 128), F.Identity, bias=T.SP[:, 8 + o:9 + o])
+            for h in (0, 1):
+                ts("KK SP", "STEP%d%d" % (h, o), T.STEP[:, h * 512 + ho:h * 512 + ho + 128], T.KK[:, 0:128], T.SP[:, h * 4 + o:h * 4 + o + 1], A.is_ge)
+            ts("ps7 SP", "DD1%d" % o, T.DD[:, 512 + ho:640 + ho], b(7, ho, ho + 128), T.SP[:, 12 + o:13 + o], A.add)
+
+        def place(ph, q):
+            k = (0, 1, 4, 5)[q]
+            for o in (2 * ph, 2 * ph + 1):
+                for h in (0, 1):
+                    ho, x = h * 512 + o * 128, (o % 2) * 256 + h * 128
+                    mm("DD%d%d STEP%d%d" % (h, o, h, o), "ps%d" % k, b(k, x, x + 128), T.DD[32 * q:32 * q + 32, ho:ho + 128],
+                       T.STEP[32 * q:32 * q + 32, ho:ho + 128])
+            for o in (2 * ph, 2 * ph + 1):
+                x = o * 1024 + q * 256
+                tt("ps%d KK" % k, "IND%d+" % o, T.IND[:, x:x + 256], b(k, (o % 2) * 256, (o % 2) * 256 + 256), T.KK[:, 0:256], A.is_le)
+
+        def wrap(o):
+            for a in range(8):
+                c = 96 + a * 4 + o
+                mm("IND%d ONES" % o, "ps3", b(3, c, c + 1), T.IND[:, o * 1024 + a:(o + 1) * 1024:8], T.ONES[:, 0:1], False, o == 3 and a == 7)
+
+        for q in range(4):
+            place(0, q)
+        for a in range(8):
+            for h in (0, 1):
+                mm("CS " + " ".join("STEP%d%d" % (h, o) for o in range(4)), "ps2", b(2, a * 64, a * 64 + 64), CS[h][:],
+                   T.STEP[:, h * 512 + a:(h + 1) * 512:8], h == 0, h == 1)
+        act("ps2", "CCR", T.CCR[:], b(2, 0, 512), F.Copy)
+        for q in range(4):
+            place(1, q)
+        for q in range(16):
+            mm("DIAG CCR", "ps3", b(3, 96, 128), T.DIAG[:, q * 128:(q + 1) * 128], T.CCR[:, q::16], q == 0, False)
+        for o in range(4):
+            wrap(o)
+        bk = "BMo%d bm%d" % (r, r)
+        red(bk, "B", L("B"), T.BML[:, r * 16:r * 16 + 16:4], A.min)
+        red(bk, "M", L("M"), T.BML[:, r * 16 + 1:r * 16 + 16:4], A.min)
+        tt("hi noh", "ha", L("ha", 3), HI, L("noh"), A.mult)
+        tt("last noh", "la", L("la", 3), LA, L("noh"), A.mult)
+        ts("oh", "lb", L("lb", 3), L("oh"), float((r + 2) * 1024), A.mult)
+        ts("M B", "kept", L("kept"), L("M"), L("B"), A.is_lt)
+        ts("oh B", "hb", L("hb", 3), L("oh"), L("B"), A.mult)
+        ts("loe B", "x", L("x"), L("loe"), 1.0, A.add, L("B"), A.max)
+        ts("kept oh", "k2", L("k2"), L("kept"), L1("oh", 2), A.mult, -4000.0, A.mult)
+        tt("la lb", "last", LA, L("la"), L("lb"), A.add)
+        tt("ha hb", "hi", HI, L("ha"), L("hb"), A.add)
+        ts("k2 M", "uc", L("uc"), L("k2"), L("M"), A.add, 4000.0, A.add)
+        tt("uc U", "U", UU, UU, L("uc"), A.min)
+        for o in range(4):
+            ts("ps3", "LI+", T.LI[:, o * 8:o * 8 + 8], b(3, 96 + o, 128, 4), -128.0, A.add)
+        cp("LI", "LU", T.LU[:], T.LI[:, 0:32])
+        ts("LI", "LI2", T.LI[:, 32:64], T.LI[:, 0:32], 4607, A.bitwise_and)
+        cp("LI2", "LCU", T.LCU[:], T.LI[:, 32:64])
+        xo = (r + 2) * 1024 + rank * 256
+        chk = " ".join("CH%d" % j for j in range(8)) + " CHz LU"
+        for o in sorted(range(4), key=lambda o: o == rank):
+            t, x, kk = (T.XF, xo, "XO%d" % r) if o == rank else (T.MSG, o * 256, "MSG")
+            cp(chk, kk + "s+", t[:, x:x + 128], T.CH[:].indirect(T.LU[:, o * 8:o * 8 + 8]))
+            act("FB FBm FBz LCU", kk + "c+", t[:, x + 128:x + 256], T.FB[:].indirect(T.LCU[:, o * 8:o * 8 + 8]), F.Copy)
+        send("dat", r, "lsd", lambda q: T.MSG[:, q * 256:(q + 1) * 256], T.XF[:, xo:xo + 256], "MSGs MSGc")
+        xkeys += ["XO%ds" % r, "XO%dc" % r, "dat%d" % r]
+        ts("M U", "ml", L("ml"), L("M"), UU, A.is_lt)
+        ts("x U", "xu", L("xu"), L("x"), UU, A.is_ge)
+        ts("ml kept noh", "adv0", L("adv0"), L("ml"), L("kept"), A.mult)
+        ts("adv0 noh", "adv", L("adv"), L("adv0"), L1("noh", 2), A.mult)
+        ts("adv", "nadv", L("nadv"), L("adv"), -1.0, A.mult, 1.0, A.add)
+        ts("xu noh nadv", "back", L("back"), L("xu"), L1("noh", 0), A.mult, L("nadv"), A.mult)
+        ts("adv e back", "e", EE, L("adv"), EE, A.add, L("back"), A.subtract)
+        ts("back", "nb", L("nb"), L("back"), -1.0, A.mult, 1.0, A.add)
+        ts("adv loe", "al", L("al"), L("adv"), L("loe"), A.mult)
+        tt("lo noh", "lo0", L("lo0", 3), LO, L("noh"), A.mult)
+        ts("x nadv nb", "y", L("y"), L("x"), L("nadv"), A.mult, L("nb"), A.mult)
+        ts("I3 e", "oq", L("oq", 3), T.I3[:, 0:3], EE, A.is_equal)
+        ts("adv back", "ch", L("ch"), L("adv"), L("back"), A.add)
+        tt("al y", "z", L("z"), L("al"), L("y"), A.add)
+        ts("oq back", "tb", L("tb", 3), L("oq"), L("back"), A.mult)
+        ts("oq ch", "tk", L("tk", 3), L("oq"), L("ch"), A.mult)
+        ts("oh z", "oz", L("oz", 3), L("oh"), L("z"), A.mult)
+        ts("tk", "tn", L("tn", 3), L("tk"), -1.0, A.mult, 1.0, A.add)
+        tt("lo0 oz", "l1", L("l1", 3), L("lo0"), L("oz"), A.add)
+        ts("l1", "l2", L("l2", 3), L("l1"), 1.0, A.add)
+        tt("l1 tn", "l3", L("l3", 3), L("l1"), L("tn"), A.mult)
+        tt("l2 hi", "l4", L("l4", 3), L("l2"), HI, A.max)
+        tt("l4 tb", "l5", L("l5", 3), L("l4"), L("tb"), A.mult)
+        tt("l3 l5", "lo", LO, L("l3"), L("l5"), A.add)
+        if r + 1 < RO:
+            derive()
+        if r == 0:
+            output_constants()
+
+    xk = " ".join(xkeys)
+    win = NSLOT * 1024
+    cp("lo hi", "YT", T.YT[:, 0:6], T.ST[:, 0:6])
+    cp("e U", "YT+", T.YT[:, 6:8], T.ST[:, 9:11])
+    dma("Y", "out", [(T.yt[:], T.YT[0::16, :])], "YT", "yt")
+    for l in (1, 2, 3):
+        ts("PWC last", "FO%d" % l, T["FO%d" % l][:, 0:32], T.PWC[:], T.ST[:, 5 + l:6 + l], A.add)
+    for l in (1, 2, 3):
+        off = T["FO%d" % l][:, 0:32]
+        cp(xk + " FO%d" % l, "FS%d" % l, T["FS%d" % l][:], T.XF[:, 0:win].indirect(off))
+        act(xk + " FO%d" % l, "FC%d" % l, T["FC%d" % l][:], T.XF[:, 128:win].indirect(off), F.Copy)
+        mm("BO FS%d" % l, "ps%d" % l, b(l, 0, 512), T.BO[:], T["FS%d" % l][:])
+        mm("BCF FC%d" % l, "ps%d" % (3 + l), b(3 + l, 0, 512), T.BCF[:], T["FC%d" % l][:])
+    for l in (1, 2, 3):
+        fv, fa, fn = T["FV%d" % l][:], T["FA%d" % l][:], T["FN%d" % l][:]
+        ts("ps%d" % l, "FL", T.FL[:], b(l, 0, 512), 0.25, A.mult, -0.375, A.add)
+        tt("FL ps%d" % (3 + l), "FV%d" % l, fv, T.FL[:], b(3 + l, 0, 512), A.add)
+        ts("FV%d hi" % l, "FA%d" % l, fa, fv, T.ST[:, 2 + l:3 + l], A.is_lt)
+        scan("RST FA%d" % l, "FN%d" % l, fn, fa)
+        k = (7, 0, 3)[l - 1]
+        for i, t in enumerate((fn, fa)):
+            t = T[("FN%d", "FA%d")[i] % l]
+            for q in range(16):
+                mm("DIAG F%s%d" % ("NA"[i], l), "ps%d" % k, b(k, i * 32, i * 32 + 32), T.DIAG[:, q * 128:(q + 1) * 128], t[:, q::16], q == 0, q == 15)
+    for l in (1, 2, 3):
+        k = (7, 0, 3)[l - 1]
+        fo = T["FO%d" % l][:, 32:64]
+        w1, w2 = T.WX[:, l * 64 - 64:l * 64 - 32], T.WX[:, l * 64 - 32:l * 64]
+        tt("ps%d K1" % k, "w1%d" % l, w1, b(k, 0, 32), T.K1[:], A.add)
+        tt("ps%d w1%d" % (k, l), "w2%d" % l, w2, b(k, 32, 64), w1, A.mult)
+        tt("w2%d K2" % l, "w1%d" % l, w1, w2, T.K2[:], A.add)
+        ts("w1%d" % l, "FP%d" % l, fo, w1, 1.0 / 16384, A.mult)
+        o1, o2 = T["OS%d" % l], T["OV%d" % l]
+        cp("FP%d FS%d OS%d" % (l, l, l), "OS%d" % l, o1[:].indirect(fo), T["FS%d" % l][:])
+        dma("Y", "out", [(T.yl[:, (l - 1) * 512:l * 512], o1[:, 0:512])], "OS%d" % l, "yl%d" % l)
+        cp("FP%d FV%d OV%d" % (l, l, l), "OV%d" % l, o2[:].indirect(fo), T["FV%d" % l][:])
+        dma("Y", "out", [(T.yf[:, (l - 1) * 512:l * 512], o2[0::16, 0:512])], "OV%d" % l, "yf%d" % l)
+    need("G", list(cnt.items()) + [("%s%d" % (s, r), arrive) for s in ("bm", "dat") for r in range(RO)])

@@ -6,29 +6,35 @@ NSLOT = RO + 2
 KA = [17, 101, 263, 389, 547, 701, 859, 1021]
 WTS = [1, 3, 7, 13, 21, 35, 49, 67, 85, 107, 129, 155, 181, 211, 241, 253]
 CW = 4112
+OW = 8192 + 1632
+GAP = 2048
+ST_ = 272
+BIG = 32768.0
+M0, M2, M4 = 1.5 * 2 ** 23, 1.5 * 2 ** 13, 1.5 * 2 ** 25
+SSTEP = (1, 3)
 
 SCRATCH = {"PS": ("psum", [128, 4096], "float32")}
 for _dt, _names in (
-        ("bfloat16", "OPS:8192 CH:4112 FB:4112 DY:4096 SS:512 SF:512 IN0:1024 SC:1024 DD:1024 STEP:1024 IND:4096 CCR:512 MSG:1024 CN:32"
-                     " TLM:128 WMARK:144 WF0:144 WF1:144 SEL4:16 MASKG:16 IDENT:128 ONES:128 TRI:128 SHIFT:128 IMS:128 CS0:128 CS1:128"
-                     " CM:128 QALL:128 LANEG:128 BO:128 BCF:128 BLK:128 TMPA:128 TMPB:128 DIAG:2048 KK:512 RST:512 OWF:256"),
-        ("float16", "KEY:1024 RH:4 BH:4 WT0:160 WT1:160"),
-        ("float32", "BML:144 UF:64 KU:256 KMAT:256 PEN:256 CC:256 CP:256 SG:32 SELC:64 SP:16 TS:4 MT:32 MTT:32 MM:4 ST:16 LT:128"
-                    " COL:32 WROW:48 LQ:16 HM:2 I3:8 PWC:32 K1:32 K2:32 YT:8 PW0:32 PW1:32 PW2:32 RE0:16 WX:192"),
-        ("int32", "FL:512 UI:128 OFP:256 OFM:256 LI:64 I1:256 OW:256 T4:256 CI:160 C5:128 C4:128 CL:128 RF:132 RF2:132 CM3:16 TI:8 WI:4"
-                  " F0:512 FH:512 FD:512 FE:512 FG:512"),
-        ("uint16", "OFU:256 OFS:32 LU:32 LCU:32 REP:16")):
+        ("bfloat16", "OPS:%d CH:4112 FB:528 DY:3072 RAW:1024 SS:512 SO:512 SF:512 IN0:1024 BASE:1024 SC:1088 P3:1088 C2:96 IN1:544 S1:544 KWX:272 RS17:272"
+                     " IN2:512 IN3:512 KKP:256 MS:384 MD:384 OO:256 AW:32 C17:16 CN3:16 DL:64 ONE:64 TLM:128 WMARK:144 WMN:144 WMO:144 WPC:144 W15:144 W16:144"
+                     " IDENT:128 IK:512 IM:128 BLK:128 TRIU:128 TRIL:128 LANEG:128 BCF:128 TMPA:128 TMPB:128 RST:512" % OW),
+        ("float16", "WSUM:144 KK:256 PEN:256 PCW:32 CF:32"),
+        ("float32", "BML:144 FA:512 KU:256 KMAT:256 F4:256 JUNK:512 TAU:48 DEL:48 YY:48 BB:4 TF:4 GO:4 PP:32 MH:32 MX:32 MXT:32 MM:8 ST:16 LT:128"
+                    " COL:40 WROW:48 I3:8 PWC:32 K1:32 K2:32 YT:8 PW1:32 PW2:32 RE0:16 WX:192"),
+        ("int32", "FL:512 UI:128 OFP:256 OFM:256 LI:64 CI:160 C4:128 CL:128 TI:16 F0:512 FD:512 FE:512 FG:512"),
+        ("uint16", "OFU:256 RR:256 OFS:32 OFO:32 OF2:32 OF3:32 LU:32 LCU:32 REP:16 REP2:2")):
     for _n in _names.split():
         _n, _c = _n.split(":")
         SCRATCH[_n] = ("sbuf", [128, int(_c)], _dt)
-SCRATCH["XF"] = ("sbuf", [128, NSLOT * 1024], "bfloat16")
+SCRATCH["XS"] = ("sbuf", [128, NSLOT * 512], "bfloat16")
+SCRATCH["XD"] = ("sbuf", [128, NSLOT * 512], "bfloat16")
 for _l in (1, 2, 3):
-    for _n, _c, _dt in (("FS", 512, "bfloat16"), ("FC", 512, "bfloat16"), ("FV", 512, "float32"), ("FA", 512, "bfloat16"),
-                        ("FN", 512, "bfloat16"), ("FO", 64, "uint16"), ("OS", 1024, "bfloat16"), ("OV", 1024, "float32")):
+    for _n, _c, _dt in (("FS", 512, "bfloat16"), ("FC", 512, "bfloat16"), ("FV", 512, "float32"), ("FA", 1024, "bfloat16"),
+                        ("FO", 64, "uint16"), ("OS", 1024, "bfloat16"), ("OV", 1024, "float32")):
         SCRATCH[_n + str(_l)] = ("sbuf", [128, _c], _dt)
 
-SEMAPHORES = (["qV", "qS", "qP", "qG", "ld0", "ld1", "ld2", "out", "lsb", "lsd"]
-              + ["bm%d" % r for r in range(RO)] + ["dat%d" % r for r in range(RO)])
+SEMAPHORES = (["qV", "qS", "qP", "qG", "ld0", "ld1", "ld2", "out", "lsb", "lsa", "lsd"]
+              + ["%s%d" % (s, r) for s in ("bm", "ds", "dd") for r in range(RO)])
 
 
 def rank_program(g, core, T, topo):
@@ -112,11 +118,11 @@ def rank_program(g, core, T, topo):
     def red(r, w, out, i, op):
         V(lambda e: e.tensor_reduce(out, i, AxisListType.X, op), r, w)
 
-    def fill(w, out, c):
-        V(lambda e: e.memset(out, c), "", w)
+    def fill(w, out, c, r=""):
+        V(lambda e: e.memset(out, c), r, w)
 
-    def scan(r, w, out, i):
-        V(lambda e: e.tensor_tensor_scan(out, T.RST[:], i, 0.0, A.mult, A.add), r, w)
+    def scan(r, w, out, a, b_, o0, o1):
+        V(lambda e: e.tensor_tensor_scan(out, a, b_, 0.0, o0, o1), r, w)
 
     def mm(r, w, out, l, r_, st=True, sp=True):
         do("P", lambda e: e.matmul(out, l, r_, st, sp), r, w)
@@ -124,130 +130,103 @@ def rank_program(g, core, T, topo):
     def act(r, w, out, i, fn, **k):
         do("S", lambda e: e.activation(out, i, fn, **k), r, w)
 
-    def b(k, x, y, st=1):
-        return T.PS[:, k * 512 + x:k * 512 + y:st] if st > 1 else T.PS[:, k * 512 + x:k * 512 + y]
+    def b(k, x, y):
+        return T.PS[:, k * 512 + x:k * 512 + y]
 
-    def plan(src):
-        off = [c for c in cores if topo.chip(c) != topo.chip(src)]
-        on = [c for c in cores if topo.chip(c) == topo.chip(src) and c != src]
-        base = list(topo.engines(src, off[0]))
-        rest = [e for e in topo.engines(src, on[0]) if e not in base]
-        out = {}
-        for cs, es in ((off, base), (on, rest)):
-            p = len(es) // len(cs)
-            for i, c in enumerate(cs):
-                out[c] = es[i * p:(i + 1) * p]
-        return out
+    def to_w(r, k, x, n, wt, src, c0, first=True, last=True):
+        for q in range(16):
+            mm(r, "ps%d" % k, b(k, x, x + n), wt[:, 15 - q:143 - q], src[:, c0 + q:c0 + 16 * n:16], first and q == 0, last and q == 15)
 
-    mine = plan(core)
-    arrive = sum(len(plan(c)[core]) for c in cores if c != core)
+    off = [c for c in cores if topo.chip(c) != topo.chip(core)]
+    near = [c for c in cores if topo.chip(c) == topo.chip(core) and c != core][0]
+    far_e = list(topo.engines(core, off[0]))
+    near_e = [e for e in topo.engines(core, near) if e not in far_e]
+    ne = len(far_e) // len(off)
+    lane = {c: far_e[i * ne:(i + 1) * ne] for i, c in enumerate(off)}
+    lane[near] = near_e[:ne]
+    ow = [cores.index(c) for c in off + [near, core]]
+    arrive = ne * (len(cores) - 1)
 
-    def send(name, r, local, src_of, dst, keys):
+    def send(local, parts, keys):
         keys = keys.split()
         need("G", deps("G", keys, []))
         tr = []
-        for c, en in mine.items():
+        for c, en, sem, src, dst in parts:
             rid, pid, _ = topo.addr(c)
             tr.append(RemoteDMATransfer(dst_ids=[DstId(rid=rid, pnc=pid)], dma_engine_mask=sum(1 << e for e in en),
-                                        remote_sem=T.sem["%s%d" % (name, r)], srcs=[src_of(cores.index(c))], dsts=[dst]))
+                                        remote_sem=T.sem[sem], srcs=[src], dsts=[dst]))
+            lastw[sem] = (sem, arrive)
         g.remote_dma_fused(tr, local_sem=T.sem[local])
-        cnt[local] = cnt.get(local, 0) + sum(len(en) for en in mine.values())
+        cnt[local] = cnt.get(local, 0) + ne * len(parts)
         mark("G", (local, cnt[local]), keys, [])
-        lastw["%s%d" % (name, r)] = ("%s%d" % (name, r), arrive)
 
     fill("F0", T.F0[:], 0)
-    dma("S", "ld0", [(T.XF[:, q * 256:q * 256 + 128], T.s0[:, q * 128:(q + 1) * 128]) for q in range(4)], "", "XF0s")
+    dma("S", "ld0", [(T.XS[:, 0:512], T.s0[:])], "", "XS0")
     dma("S", "ld1", [(T.F0[0::16, :], T.f0[:]), (T.F0[1::16, :], T.f0[:])], "", "F0")
-    dma("Y", "ld2", [(T.OPS[:], T.opr[:])], "", "OPS")
+    dma("Y", "ld2", [(T.OPS[:, 0:8192], T.opr[:]), (T.OPS[:, 8192:OW], T.opr[:, 0:OW - 8192])], "", "OPS")
 
-    def iota(w, out, pat, base=0, cm=0, small=False):
+    def iota(w, out, pat, base=0, cm=0, small=True):
         if small:
             do("G", lambda e: e.iota(out, pat, base, cm, allow_small_or_imprecise_dtypes=True), "", w)
         else:
             do("G", lambda e: e.iota(out, pat, base, cm), "", w)
 
-    iota("TI", T.TI[:, 0:1], [[1, 1]], 0, 1)
-    iota("CI", T.CI[:], [[1, 160]])
-    iota("PW0", T.PW0[:], [[256, 4], [16, 8]], small=True)
-    iota("RF", T.RF[:], [[1, 33], [1000, 4]], -3000)
-    iota("CM3", T.CM3[:], [[0, 4], [1, 4]])
-    iota("RE0", T.RE0[:], [[0, 8], [16, 2]], small=True)
-    iota("C4", T.C4[:], [[1, 8], [0, 16]])
-    iota("CL", T.CL[:], [[0, 8], [1, 16]])
-    iota("C5", T.C5[:], [[1, 4], [0, 32]])
-    iota("KK", T.KK[:], [[0, 4], [1, 16], [16, 8]], small=True)
-    iota("PW1", T.PW1[:], [[0, 4], [16, 8]], small=True)
-    iota("PW2", T.PW2[:], [[16, 32]], small=True)
+    iota("TI", T.TI[:, 0:1], [[1, 1]], 0, 1, False)
+    iota("CI", T.CI[:], [[1, 160]], small=False)
+    iota("PW2", T.PW2[:], [[16, 32]])
+    iota("RE0", T.RE0[:], [[0, 8], [16, 2]])
+    iota("C4", T.C4[:], [[1, 8], [0, 16]], small=False)
+    iota("CL", T.CL[:], [[0, 8], [1, 16]], small=False)
+    iota("KWX", T.KWX[:], [[16, 8], [0, 34]])
+    iota("KKP", T.KKP[:], [[0, 2], [1, 128]])
+    iota("C17", T.C17[:], [[17, 2], [0, 8]])
+    iota("CN3", T.CN3[:], [[-256 * 17, 2], [0, 8]], -256)
+    iota("PW1", T.PW1[:], [[0, 4], [16, 8]])
 
     def C(k):
         return T.COL[:, k:k + 1]
-    cp("TI", "c0", C(0), T.TI[:, 0:1])
-    for k, sh, an in ((1, 0, 15), (2, 4, 7), (3, 0, 31), (4, 5, 3), (6, 4, 1)):
-        ts("TI", "TI%d" % k, T.TI[:, k:k + 1], T.TI[:, 0:1], sh, A.logical_shift_right, an, A.bitwise_and)
-    for k in (1, 2, 3, 4, 6):
-        cp("TI%d" % k, "c%d" % k, C(k), T.TI[:, k:k + 1])
+
+    def TI(k):
+        return T.TI[:, k:k + 1]
+    ci = T.CI[:, 0:128]
+    cw = T.CI[:, 0:143]
+    cp("TI", "c0", C(0), TI(0))
+    for k, sh, an in ((1, 0, 15), (2, 4, 7), (3, 4, 1), (4, 0, 7), (5, 3, 1)):
+        ts("TI", "TI%d" % k, TI(k), TI(0), sh, A.logical_shift_right, an, A.bitwise_and)
+    for k in (1, 2, 3):
+        cp("TI%d" % k, "c%d" % k, C(k), TI(k))
     for i in range(16):
         fill("wr+", T.WROW[:, i:i + 1], WTS[i])
     ts("CI c1", "wm", T.WROW[:, 16:32], T.CI[:, 0:16], C(1), A.is_equal)
     tt("wr wm", "wx", T.WROW[:, 32:48], T.WROW[:, 0:16], T.WROW[:, 16:32], A.mult)
     red("wx", "c7", C(7), T.WROW[:, 32:48], A.add)
-    tt("c0 c1", "c12", C(12), C(0), C(1), A.subtract)
-    ts("c12", "c13", C(13), C(12), 15.0, A.add)
-    ts("CI c13 c7", "WMARK", T.WMARK[:, 0:143], T.CI[:, 0:143], C(13), A.is_equal, C(7), A.mult)
-    ts("PW0 c1", "PWC", T.PWC[:], T.PW0[:], C(1), A.add)
+    ts("c2", "c13", C(13), C(2), 16.0, A.mult, 15.0, A.add)
+    ts("CI c13 c7", "WMARK", T.WMARK[:, 0:143], cw, C(13), A.is_equal, C(7), A.mult)
+    ts("PW2 c1", "PWC", T.PWC[:], T.PW2[:], C(1), A.add)
     ts("RE0 c1", "REP", T.REP[:], T.RE0[:], C(1), A.add)
     for j in range(8):
         fill("KMAT+", T.KMAT[:, j * 32:(j + 1) * 32], KA[j])
-    cp("c7", "wi0", T.WI[:, 0:1], C(7))
-    ts("wi0", "wi1", T.WI[:, 1:2], T.WI[:, 0:1], 3, A.bitwise_and)
-    ts("wi1", "c8", C(8), T.WI[:, 1:2], -1024.0, A.mult, 2049.0, A.add)
-    ts("c1", "c9", C(9), C(1), 0.0, A.is_equal, 31.0, A.mult)
-    ts("c1", "c10", C(10), C(1), 3.5, A.is_lt)
-    tt("c9 c10", "c11", C(11), C(9), C(10), A.add)
-    ts("c4", "c14", C(14), C(4), 32.0, A.mult, 31.0, A.add)
-    ts("c6", "c15", C(15), C(6), 1000.0, A.mult)
-    ts("c6", "c16", C(16), C(6), -1000.0, A.mult, 1000.0, A.add)
-    ts("c0", "c17", C(17), C(0), 1.0, A.add)
-    ts("c4", "c5", C(5), C(4), 2.0, A.mult)
-    ts("c5", "c18", C(18), C(5), 1.0, A.add)
-    ts("c3", "c28", C(28), C(3), 1.5, A.is_gt, 1000.0, A.mult)
-    ts("c3 c28 c5", "c19", C(19), C(3), C(28), A.add, C(5), A.add)
-    ts("c1", "c20", C(20), C(1), 0.0, A.is_equal, 32.0, A.mult)
-    ts("RF", "RF2", T.RF2[:], T.RF[:], 3, A.arith_shift_right)
-    WT, WF, CS = (T.WT0, T.WT1), (T.WF0, T.WF1), (T.CS0, T.CS1)
-    for h in (0, 1):
-        tt("c14 c%d" % (15 + h), "c%d" % (21 + h), C(21 + h), C(14), C(15 + h), A.add)
-        tt("c4 c%d" % (15 + h), "c%d" % (23 + h), C(23 + h), C(4), C(15 + h), A.add)
-        ts("c6", "HM+", T.HM[:, h:h + 1], C(6), float(h), A.is_equal)
-        ts("CI c8 c%d" % (21 + h), "WT+", WT[h][:, 0:159], T.CI[:, 0:159], C(21 + h), A.is_equal, C(8), A.mult)
-        ts("RF2 c11 c%d" % (23 + h), "WF+", WF[h][:, 0:132], T.RF2[:], C(23 + h), A.is_equal, C(11), A.mult)
-    ts("F0", "FH", T.FH[:], T.F0[:], 5, A.logical_shift_right)
+    ts("c1", "c26", C(26), C(1), 0.0, A.is_equal, 4.0, A.mult)
+    ts("c1", "c27", C(27), C(1), 1.0, A.is_equal, 4.0, A.mult)
+    ts("c1", "c28", C(28), C(1), 15.0, A.is_equal, 4.0, A.mult)
+    ts("c26 c28", "c20", C(20), C(26), 32.0, A.mult, C(28), A.add)
+    ts("F0", "FL", T.FL[:], T.F0[:], 5, A.logical_shift_right)
     ts("F0", "FD", T.FD[:], T.F0[:], 31, A.bitwise_and)
-    ts("c1", "c26", C(26), C(1), 0.0, A.is_equal)
-    ts("c1", "c27", C(27), C(1), 1.0, A.is_equal)
-    ts("FH c26", "FE", T.FE[:], T.FH[:], C(26), A.mult)
-    ts("FD c27", "FG", T.FG[:], T.FD[:], C(27), A.mult)
-    for q in range(4):
-        tt("FE FG", "XF0c+", T.XF[:, q * 256 + 128:q * 256 + 256], T.FE[:, q * 128:q * 128 + 128], T.FG[:, q * 128:q * 128 + 128], A.add)
-    fill("XF1m", T.XF[:, 1024:2048], 0.0)
-    for q in range(4):
-        x = T.XF[:, 1024 + q * 256 + 128:1024 + q * 256 + 256]
-        ts("XF1m c20", "XF1+", x, x, 0.0, A.mult, C(20), A.add)
-    fill("FBm", T.FB[:], 0.0)
-    ts("FBm c20", "FBz", T.FB[:, 4096:CW], T.FB[:, 4096:CW], 0.0, A.mult, C(20), A.add)
-    ci = T.CI[:, 0:128]
-    ts("C4 c2", "BO", T.BO[:], T.C4[:], C(2), A.is_equal)
+    ts("FL c26", "FE", T.FE[:], T.FL[:], C(26), A.mult)
+    ts("FD c27 c28", "FG", T.FG[:], T.FD[:], C(27), A.mult, C(28), A.add)
+    tt("FE FG", "XD0", T.XD[:, 0:512], T.FE[:], T.FG[:], A.add)
+    fill("XS1", T.XS[:, 512:1024], 0.0)
+    ts("XS1 c20", "XD1", T.XD[:, 512:1024], T.XS[:, 512:1024], C(20), A.add)
+    ts("C4 c2", "BLK", T.BLK[:], T.C4[:], C(2), A.is_equal)
     ts("CL", "TA", T.TMPA[:], T.CL[:], 1.5, A.is_gt)
     ts("CL", "TB", T.TMPB[:], T.CL[:], 3.5, A.is_lt)
     tt("TA TB", "L1", T.LANEG[:], T.TMPA[:], T.TMPB[:], A.mult)
-    tt("L1 BO", "TA", T.TMPA[:], T.LANEG[:], T.BO[:], A.mult)
+    tt("L1 BLK", "TA", T.TMPA[:], T.LANEG[:], T.BLK[:], A.mult)
     ts("CL", "TB", T.TMPB[:], T.CL[:], 1.0, A.add)
     tt("TA TB", "L1", T.LANEG[:], T.TMPA[:], T.TMPB[:], A.mult)
     ts("L1", "LANEG", T.LANEG[:], T.LANEG[:], -1.0, A.add)
-    ts("C5 c4", "BLK", T.BLK[:], T.C5[:], C(4), A.is_equal)
-    ts("BLK", "QALL", T.QALL[:], T.BLK[:], 0.0625, A.mult)
     fill("lo hi last e U", T.ST[:], 0.0)
-    fill("last", T.ST[:, 6:9], 1024.0)
+    fill("last", T.ST[:, 6:9], 512.0)
     fill("U", T.ST[:, 10:11], 1023.0)
     cp("CI", "I3", T.I3[:, 0:3], T.CI[:, 0:3])
     ts("CI", "J3", T.I3[:, 4:7], T.CI[:, 0:3], 1.0, A.add)
@@ -265,13 +244,10 @@ def rank_program(g, core, T, topo):
         return T.LT[:, x:x + 1]
 
     def derive():
-        ts("J3 e", "oh1", L("oh1", 3), T.I3[:, 4:7], EE, A.is_equal)
         ts("e", "e1", L("e1"), EE, 1.0, A.add)
-        tt("oh1 last", "sl", L("sl", 3), L("oh1"), LA, A.mult)
+        ts("J3 e", "oh1", L("oh1", 3), T.I3[:, 4:7], EE, A.is_equal)
         ts("LANEG e1", "TLM", T.TLM[:], T.LANEG[:], L("e1"), A.is_equal)
-        red("sl", "slot", L("slot"), L("sl"), A.add)
         ts("e", "e811", L("e811"), EE, 811.0, A.mult)
-        ts("PWC slot", "OFS", T.OFS[:], T.PWC[:], L("slot"), A.add)
         tt("oh1 hi", "th", L("th", 3), L("oh1"), HI, A.mult)
         ts("I3 e", "oh", L("oh", 3), T.I3[:, 0:3], EE, A.is_equal)
         red("th", "th1", L("th1"), L("th"), A.add)
@@ -279,248 +255,321 @@ def rank_program(g, core, T, topo):
         ts("I3 e", "noh", L("noh", 3), T.I3[:, 0:3], EE, A.not_equal)
         ts("oh th1", "thr", L("thr"), L1("oh", 0), 2000.0, A.mult, L("th1"), A.add)
         red("ol", "loe", L("loe"), L("ol"), A.add)
-        ts("HM thr", "RH2", T.RH[:, 2:4], T.HM[:], L("thr"), A.mult)
-        ts("HM loe", "RH0", T.RH[:, 0:2], T.HM[:], L("loe"), A.mult)
 
+    cp("PWC", "OFS", T.OFS[:], T.PWC[:])
+    fill("slot", L("slot"), 0.0)
     derive()
+    ts("CI c0", "IDENT", T.IDENT[:], ci, C(0), A.is_equal)
+    ts("BLK c28", "TA", T.TMPA[:], T.BLK[:], C(28), A.mult, -0.09375, A.mult)
+    tt("IDENT TA", "IM", T.IM[:], T.IDENT[:], T.TMPA[:], A.add)
+    cp("c7", "wi0", TI(8), C(7))
+    ts("wi0", "wi1", TI(9), TI(8), 3, A.bitwise_and)
+    ts("wi1", "c8", C(8), TI(9), -1.0 / 4096, A.mult, 1026.0 / 4096, A.add)
+    ts("c1", "c9", C(9), C(1), 0.0, A.is_equal, 31.0, A.mult)
+    ts("c1", "c10", C(10), C(1), 3.5, A.is_lt)
+    ts("c9 c10", "c11", C(11), C(9), C(10), A.add, 0.25, A.mult)
+    ts("CI c13 c8", "WSUM", T.WSUM[:, 0:143], cw, C(13), A.is_equal, C(8), A.mult)
+    ts("CI c13 c11", "WPC", T.WPC[:, 0:143], cw, C(13), A.is_equal, C(11), A.mult)
+    INEG, I45, IG, I16 = [T.IK[:, k * 128:k * 128 + 128] for k in range(4)]
+    for nm, t, v in (("INEG", INEG, -1.0), ("I45", I45, 45.0), ("IG", IG, GAP * 4096.0), ("I16", I16, 16.0)):
+        ts("IDENT", nm, t, T.IDENT[:], v, A.mult)
+    fill("DL", T.DL[:], -71.0 / 8192)
+    fill("ONE", T.ONE[:], 1.0)
+    ts("XS1 c20", "FBz", T.FB[:, 512:528], T.XS[:, 512:528], C(20), A.add)
+    for i in range(4):
+        fill("GO+", T.GO[:, i:i + 1], float(GAP * ow[i]))
+    ts("GO", "t0", T.TAU[:, 0:4], T.GO[:], 512.0, A.add)
+    zero = ow.index(0)
 
-    def search_constants():
-        ts("CI c0", "IDENT", T.IDENT[:], ci, C(0), A.is_equal)
-        ts("CI c4", "SEL4", T.SEL4[:, 0:4], T.CI[:, 0:4], C(4), A.is_equal)
-        ts("CM3 c4", "MASKG", T.MASKG[:], T.CM3[:], C(4), A.not_equal, -8192.0, A.mult)
-        fill("ONES", T.ONES[:], 1.0)
-        fill("MTm", T.MT[:], 3000.0)
-
-    late = [lambda: ts("CI c0", "TA", T.TMPA[:], ci, C(0), A.is_gt),
-            lambda: ts("CI c17", "TB", T.TMPB[:], ci, C(17), A.is_equal),
-            lambda: fill("RSTm", T.RST[:], 1.0),
-            lambda: tt("TA BLK", "TRI", T.TRI[:], T.TMPA[:], T.BLK[:], A.mult),
-            lambda: tt("TB BLK", "SHIFT", T.SHIFT[:], T.TMPB[:], T.BLK[:], A.mult),
-            lambda: V(lambda e: e.memset(T.RST[:, 0::128], 0.0), "RSTm", "RST"),
-            lambda: tt("IDENT SHIFT", "IMS", T.IMS[:], T.IDENT[:], T.SHIFT[:], A.subtract),
-            lambda: ts("C4 c5", "CS", T.CS0[:], T.C4[:], C(5), A.is_equal),
-            lambda: ts("C4 c18", "CS+", T.CS1[:], T.C4[:], C(18), A.is_equal),
-            lambda: ts("C4 c19", "CM", T.CM[:], T.C4[:], C(19), A.is_equal),
+    late = [lambda: ts("CI", "TA", T.TMPA[:, 0:32], T.CI[:, 0:32], 15.5, A.is_gt),
+            lambda: ts("TA c3", "MH", T.MH[:], T.TMPA[:, 0:32], C(3), A.not_equal, 20000.0, A.mult),
+            lambda: fill("BASE%d" % zero, T.BASE[:, zero * 256:zero * 256 + 256], 0.0),
+            lambda: fill("SCz", T.SC[:], 0.0),
+            lambda: fill("P3z", T.P3[:], 0.0),
+            lambda: fill("RSm", T.RS17[:], 1.0),
+            lambda: fill("RS17", T.RS17[:, 0::17], 0.0, "RSm"),
+            lambda: ts("KWX c1", "KWX", T.KWX[:], T.KWX[:], C(1), A.add),
+            lambda: fill("KWX", T.KWX[:, 16::17], -1024.0),
+            lambda: ts("CI c0", "TB", T.TMPB[:], ci, C(0), A.is_ge),
+            lambda: tt("TB BLK", "TRIU", T.TRIU[:], T.TMPB[:], T.BLK[:], A.mult),
+            lambda: tt("TRIU BLK", "TRIL", T.TRIL[:], T.BLK[:], T.TRIU[:], A.subtract),
+            lambda: ts("c1", "c12", C(12), C(1), 14.5, A.is_lt),
+            lambda: ts("CI c13 c12", "W15", T.W15[:, 0:143], cw, C(13), A.is_equal, C(12), A.mult),
+            lambda: ts("CI c13", "W16", T.W16[:, 0:143], cw, C(13), A.is_equal),
             lambda: fill("CHz", T.CH[:, 4096:CW], 0.0),
-            lambda: ts("CI c1", "LQ", T.LQ[:], T.CI[:, 0:16], C(1), A.is_equal, 128.0, A.mult)]
-    late += [lambda q=q: fill("BMo%d" % q, T.BML[:, q * 16 + rank * 4:q * 16 + rank * 4 + 4], 0.0) for q in range(RO)]
-    late += [lambda q=q: ts("CI c0 LQ", "DIAG+", T.DIAG[:, q * 128:(q + 1) * 128], ci, C(0), A.is_equal, T.LQ[:, q:q + 1], A.mult)
-             for q in range(16)]
+            lambda: ts("TI4", "c14", C(14), TI(4), 34.0, A.mult, 16.0, A.add),
+            lambda: ts("TI5 c14", "REP2", T.REP2[:, 0:1], TI(5), 17.0, A.mult, C(14), A.add),
+            lambda: fill("BMz+", T.BML[:, rank * 4 + 2::16], 0.0),
+            lambda: fill("BMz+", T.BML[:, rank * 4 + 3::16], 0.0)]
 
     def output_constants():
+        fill("RSTm", T.RST[:], 1.0)
+        fill("RST", T.RST[:, 0::128], 0.0, "RSTm")
         for l in (1, 2, 3):
             fill("OS%d" % l, T["OS%d" % l][:], 0.0)
             fill("OV%d" % l, T["OV%d" % l][:], 1023.0)
-        ts("C4 c2", "BCF", T.BCF[:], T.C4[:], C(2), A.is_equal, C(11), A.mult)
-        ts("PW1 c1", "PW1", T.PW1[:], T.PW1[:], C(1), A.add, -128.0, A.mult)
-        ts("PW2 c1", "PW2", T.PW2[:], T.PW2[:], C(1), A.add, 512.0, A.add)
-        ts("PW1", "K1", T.K1[:], T.PW1[:], -513.0 * 128, A.add)
-        ts("PW2", "K2", T.K2[:], T.PW2[:], 16384.0, A.mult)
+        ts("BLK c11", "BCF", T.BCF[:], T.BLK[:], C(11), A.mult)
+        ts("PW1 c1", "PW1", T.PW1[:], T.PW1[:], C(1), A.add, -16.0, A.mult)
+        ts("PW1", "K1", T.K1[:], T.PW1[:], -513.0 * 16, A.add)
+        ts("PWC", "K2", T.K2[:], T.PWC[:], 512.0, A.add, 256.0, A.mult)
 
-    xkeys = ["XF0s", "XF0c", "XF1"]
-    SE = T.SELC
+    skeys, dkeys = ["XS0", "XS1"], ["XD0", "XD1"]
     for r in range(RO):
-        win = (r + 2) * 1024
-        xk = " ".join(xkeys)
-        cp(xk + " OFS", "SS", T.SS[:], T.XF[:, 0:win].indirect(T.OFS[:]))
-        act(xk + " OFS", "SF", T.SF[:], T.XF[:, 128:win].indirect(T.OFS[:]), F.Copy)
-        for q in range(16):
-            mm("WMARK SS", "ps3", b(3, 0, 32), T.WMARK[:, 15 - q:143 - q], T.SS[:, q::16], q == 0, q == 15)
-        mm("TLM SS", "ps4", b(4, 0, 512), T.TLM[:], T.SS[:])
+        win = (r + 2) * 512
+        cp(" ".join(skeys) + " OFS", "SS", T.SS[:], T.XS[:, 0:win].indirect(T.OFS[:]))
+        if r == 0:
+            to_w("WMARK XS0", 7, 0, 32, T.WMARK, T.XS, 0)
+        else:
+            to_w("WMN " + " ".join(skeys[-2:]), 7, 0, 32, T.WMN, T.XS, win - 512, False, True)
+        act(" ".join(dkeys) + " OFS", "SF", T.SF[:], T.XD[:, 0:win].indirect(T.OFS[:]), F.Copy)
+        mm("TLM SS", "ps6", b(6, 0, 512), T.TLM[:], T.SS[:], True, False)
+        mm("IM SF", "ps6", b(6, 0, 512), T.IM[:], T.SF[:], False, True)
+        act("ps6", "FA", T.FA[:], b(6, 0, 512), F.Identity, bias=M4)
+        act("FA", "FB", T.FB[:, 0:512], T.FA[:], F.Identity, bias=-M4)
         u = [T.UI[:, k * 32:(k + 1) * 32] for k in range(4)]
-        cp("ps3", "u0", u[0], b(3, 0, 32))
+        cp("ps7", "u0", u[0], b(7, 0, 32))
         ts("u0", "u1", u[1], u[0], 4095, A.bitwise_and)
         tt("u1", "u2", u[2], u[1], u[1], A.mult)
-        cp("u1", "uf0", T.UF[:, 0:32], u[1])
-        ts("u2", "u3", u[3], u[2], 4, A.logical_shift_right, 8191, A.bitwise_and)
-        tt("uf0 REP KMAT", "KU", T.KU[:], T.UF[:, 0:32].indirect(T.REP[:]), T.KMAT[:], A.mult)
-        ts("u3 e811", "uf1", T.UF[:, 32:64], u[3], L("e811"), A.add)
-        tt("uf1 REP KU", "OFP", T.OFP[:], T.UF[:, 32:64].indirect(T.REP[:]), T.KU[:], A.add)
+        tt("u1 REP KMAT", "KU", T.KU[:], u[1].indirect(T.REP[:]), T.KMAT[:], A.mult)
+        ts("u2", "u3", u[3], u[2], 4, A.logical_shift_right)
+        tt("u3 REP KU", "OFP", T.OFP[:], u[3].indirect(T.REP[:]), T.KU[:], A.add)
         ts("OFP", "OFM", T.OFM[:], T.OFP[:], 8191, A.bitwise_and)
-        cp("OFM", "OFU", T.OFU[:], T.OFM[:])
-        mm("QALL RH0 RH2", "ps3", b(3, 40, 44), T.QALL[:], T.RH[:])
-        for j in range(8):
-            d = T.DY[:, j * 512:(j + 1) * 512]
-            tt("OPS OFU SS", "DY%d" % j, d, T.OPS[:].indirect(T.OFU[:, j * 32:(j + 1) * 32]), T.SS[:], A.subtract)
-            act("DY%d" % j, "CH%d" % j, T.CH[:, j * 512:(j + 1) * 512], d, F.Abs)
-            for co in range(4 * j, 4 * j + 4):
-                for h in (0, 1):
-                    mm("WT CH%d" % j, "ps%d" % h, b(h, 0, 128), WT[h][:, 31 - co:159 - co], T.CH[:, co * 128:(co + 1) * 128], co == 0, co == 31)
-            if j == 0:
-                ts("ps4", "FL", T.FL[:], b(4, 0, 512), 0.25, A.mult, -0.375, A.add)
-                tt("SF FL FBm", "FB", T.FB[:, 0:512], T.SF[:], T.FL[:], A.add)
-                for h in (0, 1):
-                    for m in range(4):
-                        mm("WF FB", "ps2", b(2, h * 128, h * 128 + 128), WF[h][:, 3 - m:131 - m], T.FB[:, m * 128:(m + 1) * 128], m == 0, m == 3)
-                cp("ps3", "TS", T.TS[:], b(3, 40, 44))
-            if j == 3:
-                for h in (0, 1):
-                    ts("ps2 TS", "PEN+", T.PEN[:, h * 128:h * 128 + 128], b(2, h * 128, h * 128 + 128), T.TS[:, 2 + h:3 + h], A.is_ge, 4000.0, A.mult)
-                tt("ps2 PEN", "ps5", b(5, 0, 256), b(2, 0, 256), T.PEN[:], A.add)
-        if r == 0:
-            search_constants()
-        for h in (0, 1):
-            cp("ps%d" % h, "I1+", T.I1[:, h * 128:h * 128 + 128], b(h, 0, 128))
-        ts("I1", "OW", T.OW[:], T.I1[:], 10, A.arith_shift_right, 3, A.bitwise_and)
-        ts("I1", "T4", T.T4[:], T.I1[:], 1023, A.bitwise_and, 2, A.logical_shift_right)
-        cp("OW", "OWF", T.OWF[:], T.OW[:])
-        for o in range(4):
-            k = 4 if o < 2 else 2
-            act("OWF", "ps%d" % k, b(k, (o % 2) * 256, (o % 2) * 256 + 256), T.OWF[:], F.Square, bias=-64.0 * o, scale=64.0)
-        tt("T4 ps5", "CC", T.CC[:], T.T4[:], b(5, 0, 256), A.add)
-        for h in (0, 1):
-            ts("CC TS", "ps5", b(5, 256 + h * 128, 384 + h * 128), T.CC[:, h * 128:h * 128 + 128], T.TS[:, h:h + 1], A.is_lt, 4000.0, A.mult)
-        tt("CC ps5", "CP", T.CP[:], T.CC[:], b(5, 256, 512), A.add)
-        for h in (0, 1):
-            for o in range(4):
-                k = 4 if o < 2 else 2
-                x = (o % 2) * 256 + h * 128
-                tt("CP ps%d" % k, "KEY%d+" % h, T.KEY[:, h * 512 + o * 128:h * 512 + (o + 1) * 128], T.CP[:, h * 128:h * 128 + 128], b(k, x, x + 128), A.add)
+        ts("OFM e811", "OFU", T.OFU[:], T.OFM[:], L("e811"), A.add)
+        to_w("WPC FB", 7, 32, 32, T.WPC, T.FB, 0)
 
-        def dl(h, s):
-            return SE[:, h * 32 + s:h * 32 + s + 1]
+        def opj(j, x=0, y=512):
+            return T.OPS[:].indirect(T.OFU[:, j * 32 + x // 16:j * 32 + y // 16])
 
-        def bs(h, s):
-            return SE[:, h * 32 + 10 + s:h * 32 + 11 + s]
+        def vg(j, x=0, y=512):
+            tt("OPS OFU SS", "DY%d.%d" % (j, x), T.DY[:, j * 512 + x:j * 512 + y], opj(j, x, y), T.SS[:, x:y], A.subtract)
 
-        def vi(h, s):
-            return SE[:, h * 32 + 21 + s:h * 32 + 22 + s]
+        def ab(j, x=0, y=512):
+            if j < 6:
+                act("DY%d.%d" % (j, x), "CH%d+" % j, T.CH[:, j * 512 + x:j * 512 + y], T.DY[:, j * 512 + x:j * 512 + y], F.Abs)
+            else:
+                act("ps%d" % (j - 2), "CH%d" % j, T.CH[:, j * 512:j * 512 + 512], b(j - 2, 0, 512), F.Abs)
 
-        for s in range(11):
-            bit = 512 >> s
-            for h in (0, 1):
-                ky, io = T.KEY[:, h * 512:(h + 1) * 512], T.IN0[:, h * 512:(h + 1) * 512]
-                if s > 0:
-                    ts("v%d.%d" % (h, s - 1), "d%d.%d" % (h, s - 1), dl(h, s - 1), vi(h, s - 1), 0.5, A.is_lt, float(512 >> (s - 1)), A.mult)
-                if s == 0:
-                    ts("KEY%d" % h, "IN0%d" % h, io, ky, 512.0, A.is_lt)
-                elif s == 1:
-                    ts("KEY%d d%d.0" % (h, h), "IN0%d" % h, io, ky, dl(h, 0), A.subtract, 256.0, A.is_lt)
-                else:
-                    ts("KEY%d d%d.%d b%d.%d" % (h, h, s - 1, h, s), "IN0%d" % h, io, ky, dl(h, s - 1), A.subtract, bs(h, s), A.is_lt)
-                if s == 10:
-                    continue
-                k = 6 + h
-                pk = "ps%d" % k
-                for o in range(4):
-                    mm("IN0%d SEL4" % h, pk, b(k, o * 4, o * 4 + 4), T.IN0[:, h * 512 + o * 128:h * 512 + (o + 1) * 128], T.SEL4[:, 0:4])
-                act(pk, "CN%d" % h, T.CN[:, h * 16:h * 16 + 16], b(k, 0, 16), F.Copy)
-                mm("IDENT MASKG", pk, b(k, 32, 48), T.IDENT[:], T.MASKG[:], True, False)
-                mm("ONES CN%d" % h, pk, b(k, 32, 48), T.ONES[:], T.CN[:, h * 16:h * 16 + 16], False, True)
-                act(pk, "SG%d v%d.%d" % (h, h, s), T.SG[:, h * 16:h * 16 + 16], b(k, 32, 48), F.Sigmoid, bias=-128.5 * 64, scale=64.0, accum_out=vi(h, s))
+        def sg(j):
+            raw = T.RAW[:, (j - 6) * 512:(j - 5) * 512]
+            act("OPS OFU", "RAW%d" % j, raw, opj(j), F.Copy)
+            mm("INEG SS", "ps%d" % (j - 2), b(j - 2, 0, 512), INEG, T.SS[:], True, False)
+            mm("IDENT RAW%d" % j, "ps%d" % (j - 2), b(j - 2, 0, 512), T.IDENT[:], raw, False, True)
+
+        def sums(k):
+            mm("I45 DL", "ps%d" % k, b(k, 0, 64), I45, T.DL[:], True, False)
+            for h in (0, 32):
+                mm("IDENT PCW", "ps%d" % k, b(k, h, h + 32), T.IDENT[:], T.PCW[:], False, False)
+            to_w("WSUM CH%d CH%d" % (2 * k, 2 * k + 1), k, 0, 64, T.WSUM, T.CH, k * 1024, False, True)
+
+        def keys(k):
+            s = slice(k * 64, k * 64 + 64)
+            pk = "ps%d" % k
+            ts(pk, "F4%d" % k, T.F4[:, s], b(k, 0, 64), M2, A.add, M2, A.subtract)
+            ts(pk, "KK%d" % k, T.KK[:, s], b(k, 0, 64), M0, A.add, M0, A.subtract)
+            tt(pk + " F4%d" % k, "OO%d" % k, T.OO[:, s], b(k, 0, 64), T.F4[:, s], A.subtract)
+            ts("KK%d loe" % k, "PEN%d" % k, T.PEN[:, s], T.KK[:, s], L("loe"), A.is_lt, 8192.0, A.mult)
+            mm("IDENT KK%d" % k, pk, b(k, 64, 128), T.IDENT[:], T.KK[:, s], True, False)
+            mm("IG OO%d" % k, pk, b(k, 64, 128), IG, T.OO[:, s], False, False)
+            mm("IDENT PEN%d" % k, pk, b(k, 64, 128), T.IDENT[:], T.PEN[:, s], False, True)
+
+        def key16(k):
+            s = slice(k * 64, k * 64 + 64)
+            ts("ps%d" % k, "RR+", T.RR[:, s], b(k, 64, 128), 1.5 * GAP, A.add)
+            mm("IDENT KK%d" % k, "ps6", b(6, k * 64, k * 64 + 64), T.IDENT[:], T.KK[:, s], True, False)
+            mm("IDENT PEN%d" % k, "ps6", b(6, k * 64, k * 64 + 64), T.IDENT[:], T.PEN[:, s], False, True)
+
+        vg(0), sg(6), ab(0), vg(1)
+        ts("ps7 thr", "PP", T.PP[:], b(7, 32, 64), L("thr"), A.is_ge, 1023.0, A.mult)
+        sg(7), ab(1), vg(2)
+        tt("ps7 PP", "PCW", T.PCW[:], b(7, 32, 64), T.PP[:], A.max)
+        sums(0), ab(6), ab(2), vg(3), ab(7), sums(3), ab(3), sums(1), vg(4), ab(4)
+        vg(5, 0, 256), ab(5, 0, 256), vg(5, 256, 512), ab(5, 256, 512)
+        keys(0), keys(3), sums(2), keys(1), key16(0), key16(3), key16(1), keys(2), key16(2)
+
+        def col(t, i, s):
+            return t[:, 4 * s + i:4 * s + i + 1]
+
+        def count(i, k, src, key, w, out, scale, bias, rk=""):
+            for n in range(4):
+                mm("BLK " + key, "ps%d" % k, b(k, 128, 192), T.BLK[:], src[:, i * 256 + n * 64:i * 256 + n * 64 + 64], n == 0, n == 3)
+            act("ps%d %s" % (k, rk), "JUNK%d %s" % (i, w), T.JUNK[:, i * 64:i * 64 + 64], b(k, 128, 192), F.Identity, bias=bias, scale=scale, accum_out=out)
+
+        def step(i, s):
+            hi_, lo_ = (256.0 / 2 ** s, -256.0 / 2 ** s) if s < 9 else (0.0, -1.0)
+            if on_s(i, s):
+                n = int(hi_)
+                act("ONE y%d.%d" % (i, s), "JUNK%d d%d.%d" % (4 + i, i, s), T.JUNK[:, 256 + i * 64:256 + i * 64 + n], T.ONE[:, 0:n], F.Sign,
+                    scale=col(T.YY, i, s), accum_out=col(T.DEL, i, s))
+            else:
+                ts("y%d.%d" % (i, s), "d%d.%d" % (i, s), col(T.DEL, i, s), col(T.YY, i, s), hi_, A.min, lo_, A.max)
+
+        def on_s(i, s):
+            return i in SSTEP and 2 <= s < 9
+
+        def compare(i, s):
+            io = T.IN0[:, i * 256:i * 256 + 256]
+            t0 = GAP * ow[i] + 512.0
             if s == 0:
-                for h in (0, 1):
-                    red("CP MTm", "MT+", T.MT[:, h:h + 1], T.CP[:, h * 128:h * 128 + 128], A.min)
-                V(lambda e: e.transpose(T.MTT[:], T.MT[:]), "MT MTm", "MTT")
-                red("MTT", "MM0", T.MM[:, 0:1], T.MTT[:], A.min)
-                ts("MM0", "BHm", T.BH[:, 2:3], T.MM[:, 0:1], 2000.0, A.min)
-            for h in (0, 1):
-                if s == 1:
-                    ts("d%d.0" % h, "b%d.2" % h, bs(h, 2), dl(h, 0), 128.0, A.add)
-                elif 2 <= s < 10:
-                    ts("b%d.%d d%d.%d" % (h, s, h, s - 1), "b%d.%d" % (h, s + 1), bs(h, s + 1), bs(h, s), dl(h, s - 1), A.add,
-                       float((bit >> 1) - bit), A.add)
-            for _ in range(4):
-                if s and late:
-                    late.pop(0)()
-        for h in (0, 1):
-            scan("RST IN0%d" % h, "SC%d" % h, T.SC[:, h * 512:(h + 1) * 512], T.IN0[:, h * 512:(h + 1) * 512])
-        for h in (0, 1):
-            ts("d%d.9 b%d.10" % (h, h), "BHb%d" % h, T.BH[:, h:h + 1], dl(h, 9), bs(h, 10), A.add, 0.03125, A.mult)
-        tot = T.SC[:, 127:1024:128]
-        mm("TRI SC0 SC1", "ps3", b(3, 64, 72), T.TRI[:], tot)
-        mm("SHIFT SC0 SC1", "ps3", b(3, 72, 80), T.SHIFT[:], tot)
-        for h in (0, 1):
-            mm("IMS SC%d" % h, "ps%d" % (6 + h), b(6 + h, 0, 512), T.IMS[:], T.SC[:, h * 512:(h + 1) * 512])
-        for h in (0, 1):
-            mm("CS BHb%d" % h, "ps5", b(5, 0, 1), CS[h][:], T.BH[:, h:h + 1], h == 0, h == 1)
-        mm("CM BHm", "ps5", b(5, 1, 2), T.CM[:], T.BH[:, 2:3])
-        cp("ps3", "SP", T.SP[:], b(3, 64, 80))
+                ts("RR", "IN%d" % i, io, T.RR[:], t0, A.is_lt)
+            else:
+                prev = t0 if s == 1 else col(T.TAU, i, s - 1)
+                ts("RR d%d.%d t%d" % (i, s - 1, s - 1), "IN%d" % i, io, T.RR[:], col(T.DEL, i, s - 1), A.subtract, prev, A.is_lt)
+            if s < 10:
+                count(i, i, T.IN0, "IN%d" % i, "y%d.%d" % (i, s), col(T.YY, i, s), -BIG, T.BB[:, i:i + 1] if ow[i] else BIG * 128.5 / 64, "BB%d" % i)
+                if on_s(i, s):
+                    step(i, s)
+            else:
+                x = i * ST_ + 16
+                scan("IN%d BASE%d SCz" % (i, i), "SC%d" % i, T.SC[:, x:x + 256], io, T.BASE[:, i * 256:i * 256 + 256], A.add, A.subtract)
+
+        def level(s):
+            dk = " ".join("d%d.%d" % (i, s - 1) for i in range(4))
+            tt(dk + " t%d" % (s - 1), "t%d" % s, T.TAU[:, 4 * s:4 * s + 4], T.TAU[:, 4 * s - 4:4 * s], T.DEL[:, 4 * s - 4:4 * s], A.add)
+
         x = r * 16 + rank * 4
         own = T.BML[:, x:x + 4]
-        cp("ps5", "BMo%d" % r, T.BML[:, x:x + 2], b(5, 0, 2))
-        send("bm", r, "lsb", lambda q: own, own, "BMo%d" % r)
-        for o in range(4):
-            ho = o * 128
-            act("ps6 SP", "DD0%d" % o, T.DD[:, ho:ho + 128], b(6, ho, ho + 128), F.Identity, bias=T.SP[:, 8 + o:9 + o])
-            for h in (0, 1):
-                ts("KK SP", "STEP%d%d" % (h, o), T.STEP[:, h * 512 + ho:h * 512 + ho + 128], T.KK[:, 0:128], T.SP[:, h * 4 + o:h * 4 + o + 1], A.is_ge)
-            ts("ps7 SP", "DD1%d" % o, T.DD[:, 512 + ho:640 + ho], b(7, ho, ho + 128), T.SP[:, 12 + o:13 + o], A.add)
+        extra = [lambda: red("ps6", "MM0", T.MM[:, 0:1], b(6, 0, 256), A.min),
+                 lambda: ts("MM0 MH", "MX", T.MX[:], T.MH[:], T.MM[:, 0:1], A.add),
+                 lambda: V(lambda e: e.transpose(T.MXT[:], T.MX[:]), "MX", "MXT"),
+                 lambda: red("MXT", "BMm%d" % r, T.BML[:, x + 1:x + 2], T.MXT[:], A.min)]
+        for n, i in enumerate([i for i in range(4) if ow[i]]):
+            ts("RR", "BASE%d" % i, T.BASE[:, i * 256:i * 256 + 256], T.RR[:], float(GAP * ow[i]), A.is_lt)
+            count(i, (4, 5, 7)[n], T.BASE, "BASE%d" % i, "BB%d" % i, T.BB[:, i:i + 1], BIG / 64, BIG * 128.5 / 4096)
 
-        def place(ph, q):
-            k = (0, 1, 4, 5)[q]
-            for o in (2 * ph, 2 * ph + 1):
-                for h in (0, 1):
-                    ho, x = h * 512 + o * 128, (o % 2) * 256 + h * 128
-                    mm("DD%d%d STEP%d%d" % (h, o, h, o), "ps%d" % k, b(k, x, x + 128), T.DD[32 * q:32 * q + 32, ho:ho + 128],
-                       T.STEP[32 * q:32 * q + 32, ho:ho + 128])
-            for o in (2 * ph, 2 * ph + 1):
-                x = o * 1024 + q * 256
-                tt("ps%d KK" % k, "IND%d+" % o, T.IND[:, x:x + 256], b(k, (o % 2) * 256, (o % 2) * 256 + 256), T.KK[:, 0:256], A.is_le)
+        def place1(h):
+            sck = "SC%d SC%d SCz" % (2 * h, 2 * h + 1)
+            z = h * 544
+            for c in range(8):
+                mm("BLK " + sck, "ps%d" % (4 + h), b(4 + h, c * 34, c * 34 + 34), T.BLK[:], T.SC[:, z + 15:z + 544:16])
+            to_w("W16 " + sck, 6 + h, 0, 34, T.W16, T.SC, z)
+            act("ps%d" % (6 + h), "C2%d" % h, T.C2[:, h * 48:h * 48 + 34], b(6 + h, 0, 34), F.Copy)
+            for i in (0, 1):
+                y = z + i * ST_ + 16
+                mm("TRIU " + sck, "ps%d" % h, b(h, i * 256, i * 256 + 256), T.TRIU[:], T.SC[:, y:y + 256], True, False)
+                mm("TRIL " + sck, "ps%d" % h, b(h, i * 256, i * 256 + 256), T.TRIL[:], T.SC[:, y - 1:y + 255], False, True)
+            for i in (0, 1):
+                y = z + i * ST_ + 16
+                act("ps%d P3z" % h, "P3%d+" % h, T.P3[:, y:y + 256], b(h, i * 256, i * 256 + 256), F.Copy)
 
-        def wrap(o):
-            for a in range(8):
-                c = 96 + a * 4 + o
-                mm("IND%d ONES" % o, "ps3", b(3, c, c + 1), T.IND[:, o * 1024 + a:(o + 1) * 1024:8], T.ONES[:, 0:1], False, o == 3 and a == 7)
+        def hs(t, h, n=16):
+            return t[:, h * n:h * n + n]
 
-        for q in range(4):
-            place(0, q)
-        for a in range(8):
-            for h in (0, 1):
-                mm("CS " + " ".join("STEP%d%d" % (h, o) for o in range(4)), "ps2", b(2, a * 64, a * 64 + 64), CS[h][:],
-                   T.STEP[:, h * 512 + a:(h + 1) * 512:8], h == 0, h == 1)
-        act("ps2", "CCR", T.CCR[:], b(2, 0, 512), F.Copy)
-        for q in range(4):
-            place(1, q)
-        for q in range(16):
-            mm("DIAG CCR", "ps3", b(3, 96, 128), T.DIAG[:, q * 128:(q + 1) * 128], T.CCR[:, q::16], q == 0, False)
-        for o in range(4):
-            wrap(o)
-        bk = "BMo%d bm%d" % (r, r)
+        def place2(h):
+            return [lambda: tt("ps%d KWX" % (4 + h), "IN1%d" % h, hs(T.IN1, h, 272), b(4 + h, 0, 272), T.KWX[:], A.is_le),
+                    lambda: scan("RS17 IN1%d" % h, "S1%d" % h, hs(T.S1, h, 272), T.RS17[:], hs(T.IN1, h, 272), A.mult, A.add),
+                    lambda: tt("S1%d REP2 C17" % h, "AW%d" % h, hs(T.AW, h), hs(T.S1, h, 272).indirect(T.REP2[:, 0:1]), T.C17[:], A.add),
+                    lambda: cp("AW%d" % h, "OF2%d" % h, hs(T.OF2, h), hs(T.AW, h))]
+
+        def place3(h):
+            tt("C2%d OF2%d KKP" % (h, h), "IN2%d" % h, hs(T.IN2, h, 256), T.C2[:, h * 48:h * 48 + 34].indirect(hs(T.OF2, h)), T.KKP[:], A.is_le)
+            mm("I16 AW%d" % h, "ps%d" % (2 + h), b(2 + h, 0, 16), I16, hs(T.AW, h), True, False)
+            to_w("W15 IN2%d" % h, 2 + h, 0, 16, T.W15, T.IN2, h * 256, False, True)
+
+        def place4(h):
+            cp("ps%d" % (2 + h), "OF3%d" % h, hs(T.OF3, h), b(2 + h, 0, 16))
+            cp("ps%d" % (2 + h), "CF%d" % h, hs(T.CF, h), b(2 + h, 0, 16))
+            tt("P3%d P3z OF3%d KKP" % (h, h), "IN3%d" % h, hs(T.IN3, h, 256), hs(T.P3, h, 544).indirect(hs(T.OF3, h)), T.KKP[:], A.is_le)
+            mm("IDENT CN3", "ps%d" % (4 + h), b(4 + h, 0, 16), T.IDENT[:], T.CN3[:], True, False)
+            mm("I16 CF%d" % h, "ps%d" % (4 + h), b(4 + h, 0, 16), I16, hs(T.CF, h), False, False)
+            to_w("W16 IN3%d" % h, 4 + h, 0, 16, T.W16, T.IN3, h * 256, False, True)
+
+        xo = (r + 2) * 512 + rank * 128
+        chk = " ".join("CH%d" % j for j in range(8)) + " CHz"
+
+        def place5(h):
+            cp("ps%d" % (4 + h), "LU%d" % h, hs(T.LU, h), b(4 + h, 0, 16))
+            cp("ps%d" % (4 + h), "LI%d" % h, hs(T.LI, h), b(4 + h, 0, 16))
+            if h == 0:
+                cp(chk + " LU0", "MS0", T.MS[:, 0:256], T.CH[:].indirect(hs(T.LU, 0)))
+            else:
+                cp(chk + " LU1", "MS1", T.MS[:, 256:384], T.CH[:].indirect(hs(T.LU, 2, 8)))
+            ts("LI%d" % h, "LJ%d" % h, hs(T.LI, 2 + h), hs(T.LI, h), 4607, A.bitwise_and)
+            if h == 1:
+                cp(chk + " LU1", "XSo%d" % r, T.XS[:, xo:xo + 128], T.CH[:].indirect(hs(T.LU, 3, 8)))
+            ts("LJ%d" % h, "LCU%d" % h, hs(T.LCU, h), hs(T.LI, 2 + h), 512.0, A.min)
+            if h == 0:
+                act("FB FBz LCU0", "MD0", T.MD[:, 0:256], T.FB[:].indirect(hs(T.LCU, 0)), F.Copy)
+            else:
+                act("FB FBz LCU1", "MD1", T.MD[:, 256:384], T.FB[:].indirect(hs(T.LCU, 2, 8)), F.Copy)
+                act("FB FBz LCU1", "XDo%d" % r, T.XD[:, xo:xo + 128], T.FB[:].indirect(hs(T.LCU, 3, 8)), F.Copy)
+
+        for s in range(11):
+            for i in range(4):
+                if s and not on_s(i, s - 1):
+                    step(i, s - 1)
+                compare(i, s)
+                if s == 10 and i % 2:
+                    place1(i // 2)
+            if 0 < s < 10:
+                level(s)
+            for _ in range(3):
+                if late:
+                    late.pop(0)()
+            if s > 3 and extra:
+                extra.pop(0)()
+        pa, pb = place2(0), place2(1)
+        pa[0](), level(10), pa[1]()
+        tt("t10 GO", "TB4", T.MM[:, 4:8], T.TAU[:, 40:44], T.GO[:], A.subtract)
+        pa[2](), pb[0](), pa[3]()
+        red("TB4", "BMb%d" % r, T.BML[:, x:x + 1], T.MM[:, 4:8], A.min)
+        send("lsb", [(c, lane[c], "bm%d" % r, own, own) for c in lane], "BMb%d BMm%d BMz" % (r, r))
+        place3(0)
+        pb[1](), pb[2]()
+        ts("oh", "lb", L("lb", 3), L("oh"), float((r + 2) * 512), A.mult)
+        pb[3]()
+        tt("last noh", "la", L("la", 3), LA, L("noh"), A.mult)
+        place3(1)
+        place4(0)
+        tt("hi noh", "ha", L("ha", 3), HI, L("noh"), A.mult)
+        tt("last oh1", "sl", L("sl", 2), T.ST[:, 6:8], T.LT[:, lt["oh1"][0] + 1:lt["oh1"][0] + 3], A.mult)
+        place4(1)
+        place5(0)
+        send("lsa", [(c, lane[c], "ds%d" % r, hs(T.MS, i, 128), T.XS[:, xo:xo + 128]) for i, c in enumerate(off)], "MS0")
+        place5(1)
+        send("lsd", [(near, near_e[ne:2 * ne], "ds%d" % r, hs(T.MS, 2, 128), T.XS[:, xo:xo + 128])]
+             + [(c, lane[c], "dd%d" % r, hs(T.MD, i, 128), T.XD[:, xo:xo + 128]) for i, c in enumerate(off + [near])], "MS1 MD0 MD1")
+        bk = "BMb%d BMm%d bm%d" % (r, r, r)
         red(bk, "B", L("B"), T.BML[:, r * 16:r * 16 + 16:4], A.min)
         red(bk, "M", L("M"), T.BML[:, r * 16 + 1:r * 16 + 16:4], A.min)
-        tt("hi noh", "ha", L("ha", 3), HI, L("noh"), A.mult)
-        tt("last noh", "la", L("la", 3), LA, L("noh"), A.mult)
-        ts("oh", "lb", L("lb", 3), L("oh"), float((r + 2) * 1024), A.mult)
-        ts("M B", "kept", L("kept"), L("M"), L("B"), A.is_lt)
-        ts("oh B", "hb", L("hb", 3), L("oh"), L("B"), A.mult)
+        red("sl", "sb", L("sb"), L("sl"), A.add)
+        tt("B U", "mn", L("mn"), L("B"), UU, A.min)
         ts("loe B", "x", L("x"), L("loe"), 1.0, A.add, L("B"), A.max)
-        ts("kept oh", "k2", L("k2"), L("kept"), L1("oh", 2), A.mult, -4000.0, A.mult)
-        tt("la lb", "last", LA, L("la"), L("lb"), A.add)
-        tt("ha hb", "hi", HI, L("ha"), L("hb"), A.add)
-        ts("k2 M", "uc", L("uc"), L("k2"), L("M"), A.add, 4000.0, A.add)
-        tt("uc U", "U", UU, UU, L("uc"), A.min)
-        for o in range(4):
-            ts("ps3", "LI+", T.LI[:, o * 8:o * 8 + 8], b(3, 96 + o, 128, 4), -128.0, A.add)
-        cp("LI", "LU", T.LU[:], T.LI[:, 0:32])
-        ts("LI", "LI2", T.LI[:, 32:64], T.LI[:, 0:32], 4607, A.bitwise_and)
-        cp("LI2", "LCU", T.LCU[:], T.LI[:, 32:64])
-        xo = (r + 2) * 1024 + rank * 256
-        chk = " ".join("CH%d" % j for j in range(8)) + " CHz LU"
-        for o in sorted(range(4), key=lambda o: o == rank):
-            t, x, kk = (T.XF, xo, "XO%d" % r) if o == rank else (T.MSG, o * 256, "MSG")
-            cp(chk, kk + "s+", t[:, x:x + 128], T.CH[:].indirect(T.LU[:, o * 8:o * 8 + 8]))
-            act("FB FBm FBz LCU", kk + "c+", t[:, x + 128:x + 256], T.FB[:].indirect(T.LCU[:, o * 8:o * 8 + 8]), F.Copy)
-        send("dat", r, "lsd", lambda q: T.MSG[:, q * 256:(q + 1) * 256], T.XF[:, xo:xo + 256], "MSGs MSGc")
-        xkeys += ["XO%ds" % r, "XO%dc" % r, "dat%d" % r]
-        ts("M U", "ml", L("ml"), L("M"), UU, A.is_lt)
-        ts("x U", "xu", L("xu"), L("x"), UU, A.is_ge)
-        ts("ml kept noh", "adv0", L("adv0"), L("ml"), L("kept"), A.mult)
-        ts("adv0 noh", "adv", L("adv"), L("adv0"), L1("noh", 2), A.mult)
-        ts("adv", "nadv", L("nadv"), L("adv"), -1.0, A.mult, 1.0, A.add)
-        ts("xu noh nadv", "back", L("back"), L("xu"), L1("noh", 0), A.mult, L("nadv"), A.mult)
+        ts("M B oh", "k2", L("k2"), L("M"), L("B"), A.is_lt, L1("oh", 2), A.mult)
+        ts("M mn oh", "nadv", L("nadv"), L("M"), L("mn"), A.is_ge, L1("oh", 2), A.max)
+        ts("x U noh", "xu", L("xu"), L("x"), UU, A.is_ge, L1("noh", 0), A.mult)
+        tt("sb slot", "sd", L("sd"), L("sb"), L("slot"), A.subtract)
+        ts("xu nadv k2", "back", L("back"), L("xu"), L("nadv"), A.mult, L("k2"), A.max)
+        ts("nadv", "adv", L("adv"), L("nadv"), -1.0, A.mult, 1.0, A.add)
+        if r + 1 < RO:
+            ts("back sd slot", "so", L("so"), L("back"), L("sd"), A.mult, L("slot"), A.add)
+            ts("WMARK nadv", "WMO", T.WMO[:, 0:143], T.WMARK[:, 0:143], L("nadv"), A.mult)
+            ts("PWC so", "OFO", T.OFO[:], T.PWC[:], L("so"), A.add)
+            act(" ".join(skeys) + " OFO", "SO", T.SO[:], T.XS[:, 0:win].indirect(T.OFO[:]), F.Copy)
+            ts("adv", "an", L("an"), L("adv"), float((r + 2) * 512), A.mult)
+            ts("WMARK adv", "WMN", T.WMN[:, 0:143], T.WMARK[:, 0:143], L("adv"), A.mult)
+            ts("so nadv an", "slot", L("slot"), L("so"), L("nadv"), A.mult, L("an"), A.add)
+            to_w("WMO SO", 7, 0, 32, T.WMO, T.SO, 0, True, False)
         ts("adv e back", "e", EE, L("adv"), EE, A.add, L("back"), A.subtract)
-        ts("back", "nb", L("nb"), L("back"), -1.0, A.mult, 1.0, A.add)
-        ts("adv loe", "al", L("al"), L("adv"), L("loe"), A.mult)
+        if r + 1 < RO:
+            ts("PWC slot", "OFS", T.OFS[:], T.PWC[:], L("slot"), A.add)
+        skeys += ["XSo%d" % r, "ds%d" % r]
+        dkeys += ["XDo%d" % r, "dd%d" % r]
+        ts("oh B", "hb", L("hb", 3), L("oh"), L("B"), A.mult)
+        ts("k2 M", "uc", L("uc"), L("k2"), -4000.0, A.mult, L("M"), A.add)
         tt("lo noh", "lo0", L("lo0", 3), LO, L("noh"), A.mult)
-        ts("x nadv nb", "y", L("y"), L("x"), L("nadv"), A.mult, L("nb"), A.mult)
+        tt("ha hb", "hi", HI, L("ha"), L("hb"), A.add)
+        ts("uc U", "U", UU, L("uc"), 4000.0, A.add, UU, A.min)
+        tt("la lb", "last", LA, L("la"), L("lb"), A.add)
+        ts("adv loe", "al", L("al"), L("adv"), L("loe"), A.mult)
+        ts("back", "nb", L("nb"), L("back"), -1.0, A.mult, 1.0, A.add)
         ts("I3 e", "oq", L("oq", 3), T.I3[:, 0:3], EE, A.is_equal)
         ts("adv back", "ch", L("ch"), L("adv"), L("back"), A.add)
-        tt("al y", "z", L("z"), L("al"), L("y"), A.add)
+        ts("x nadv nb", "y", L("y"), L("x"), L("nadv"), A.mult, L("nb"), A.mult)
         ts("oq back", "tb", L("tb", 3), L("oq"), L("back"), A.mult)
         ts("oq ch", "tk", L("tk", 3), L("oq"), L("ch"), A.mult)
-        ts("oh z", "oz", L("oz", 3), L("oh"), L("z"), A.mult)
+        tt("al y", "z", L("z"), L("al"), L("y"), A.add)
         ts("tk", "tn", L("tn", 3), L("tk"), -1.0, A.mult, 1.0, A.add)
+        ts("oh z", "oz", L("oz", 3), L("oh"), L("z"), A.mult)
         tt("lo0 oz", "l1", L("l1", 3), L("lo0"), L("oz"), A.add)
         ts("l1", "l2", L("l2", 3), L("l1"), 1.0, A.add)
         tt("l1 tn", "l3", L("l3", 3), L("l1"), L("tn"), A.mult)
@@ -532,30 +581,26 @@ def rank_program(g, core, T, topo):
         if r == 0:
             output_constants()
 
-    xk = " ".join(xkeys)
-    win = NSLOT * 1024
     cp("lo hi", "YT", T.YT[:, 0:6], T.ST[:, 0:6])
     cp("e U", "YT+", T.YT[:, 6:8], T.ST[:, 9:11])
     dma("Y", "out", [(T.yt[:], T.YT[0::16, :])], "YT", "yt")
     for l in (1, 2, 3):
         ts("PWC last", "FO%d" % l, T["FO%d" % l][:, 0:32], T.PWC[:], T.ST[:, 5 + l:6 + l], A.add)
     for l in (1, 2, 3):
-        off = T["FO%d" % l][:, 0:32]
-        cp(xk + " FO%d" % l, "FS%d" % l, T["FS%d" % l][:], T.XF[:, 0:win].indirect(off))
-        act(xk + " FO%d" % l, "FC%d" % l, T["FC%d" % l][:], T.XF[:, 128:win].indirect(off), F.Copy)
-        mm("BO FS%d" % l, "ps%d" % l, b(l, 0, 512), T.BO[:], T["FS%d" % l][:])
+        o_ = T["FO%d" % l][:, 0:32]
+        cp(" ".join(skeys) + " FO%d" % l, "FS%d" % l, T["FS%d" % l][:], T.XS[:].indirect(o_))
+        act(" ".join(dkeys) + " FO%d" % l, "FC%d" % l, T["FC%d" % l][:], T.XD[:].indirect(o_), F.Copy)
+        mm("BLK FS%d" % l, "ps%d" % l, b(l, 0, 512), T.BLK[:], T["FS%d" % l][:])
         mm("BCF FC%d" % l, "ps%d" % (3 + l), b(3 + l, 0, 512), T.BCF[:], T["FC%d" % l][:])
     for l in (1, 2, 3):
-        fv, fa, fn = T["FV%d" % l][:], T["FA%d" % l][:], T["FN%d" % l][:]
+        fv, fa, fn = T["FV%d" % l][:], T["FA%d" % l][:, 0:512], T["FA%d" % l][:, 512:1024]
         ts("ps%d" % l, "FL", T.FL[:], b(l, 0, 512), 0.25, A.mult, -0.375, A.add)
         tt("FL ps%d" % (3 + l), "FV%d" % l, fv, T.FL[:], b(3 + l, 0, 512), A.add)
         ts("FV%d hi" % l, "FA%d" % l, fa, fv, T.ST[:, 2 + l:3 + l], A.is_lt)
-        scan("RST FA%d" % l, "FN%d" % l, fn, fa)
+        scan("RST FA%d" % l, "FN%d" % l, fn, T.RST[:], fa, A.mult, A.add)
         k = (7, 0, 3)[l - 1]
-        for i, t in enumerate((fn, fa)):
-            t = T[("FN%d", "FA%d")[i] % l]
-            for q in range(16):
-                mm("DIAG F%s%d" % ("NA"[i], l), "ps%d" % k, b(k, i * 32, i * 32 + 32), T.DIAG[:, q * 128:(q + 1) * 128], t[:, q::16], q == 0, q == 15)
+        to_w("W16 FN%d" % l, k, 0, 32, T.W16, T["FA%d" % l], 512)
+        to_w("W16 FA%d" % l, k, 32, 32, T.W16, T["FA%d" % l], 0)
     for l in (1, 2, 3):
         k = (7, 0, 3)[l - 1]
         fo = T["FO%d" % l][:, 32:64]
@@ -563,10 +608,10 @@ def rank_program(g, core, T, topo):
         tt("ps%d K1" % k, "w1%d" % l, w1, b(k, 0, 32), T.K1[:], A.add)
         tt("ps%d w1%d" % (k, l), "w2%d" % l, w2, b(k, 32, 64), w1, A.mult)
         tt("w2%d K2" % l, "w1%d" % l, w1, w2, T.K2[:], A.add)
-        ts("w1%d" % l, "FP%d" % l, fo, w1, 1.0 / 16384, A.mult)
+        ts("w1%d" % l, "FP%d" % l, fo, w1, 1.0 / 256, A.mult)
         o1, o2 = T["OS%d" % l], T["OV%d" % l]
         cp("FP%d FS%d OS%d" % (l, l, l), "OS%d" % l, o1[:].indirect(fo), T["FS%d" % l][:])
         dma("Y", "out", [(T.yl[:, (l - 1) * 512:l * 512], o1[:, 0:512])], "OS%d" % l, "yl%d" % l)
         cp("FP%d FV%d OV%d" % (l, l, l), "OV%d" % l, o2[:].indirect(fo), T["FV%d" % l][:])
         dma("Y", "out", [(T.yf[:, (l - 1) * 512:l * 512], o2[0::16, 0:512])], "OV%d" % l, "yf%d" % l)
-    need("G", list(cnt.items()) + [("%s%d" % (s, r), arrive) for s in ("bm", "dat") for r in range(RO)])
+    need("G", list(cnt.items()) + [("%s%d" % (s, r), arrive) for s in ("bm", "ds", "dd") for r in range(RO)])

@@ -7,7 +7,7 @@ KA = [17, 101, 263, 389, 547, 701, 859, 1021]
 WTS = [1, 3, 7, 13, 21, 35, 49, 67, 85, 107, 129, 155, 181, 211, 241, 253]
 CW = 4112
 OW = 8192 + 1632
-GAP = 2048
+GAP = 1024
 ST_ = 272
 BIG = 32768.0
 M0, M2, M4 = 1.5 * 2 ** 23, 1.5 * 2 ** 13, 1.5 * 2 ** 25
@@ -16,24 +16,22 @@ SSTEP = (1, 3)
 SCRATCH = {"PS": ("psum", [128, 4096], "float32")}
 for _dt, _names in (
         ("bfloat16", "OPS:%d CH:4112 FB:528 DY:3072 RAW:1024 SS:512 SO:512 SF:512 IN0:1024 BASE:1024 SC:1088 P3:1088 C2:96 IN1:544 S1:544 KWX:272 RS17:272"
-                     " IN2:512 IN3:512 KKP:256 MS:384 MD:384 OO:256 AW:32 C17:16 CN3:16 DL:64 ONE:64 TLM:128 WMARK:144 WMN:144 WMO:144 WPC:144 W15:144 W16:144"
-                     " IDENT:128 IK:512 IM:128 BLK:128 TRIU:128 TRIL:128 LANEG:128 BCF:128 TMPA:128 TMPB:128 RST:512" % OW),
-        ("float16", "WSUM:144 KK:256 PEN:256 PCW:32 CF:32"),
-        ("float32", "BML:144 FA:512 KU:256 KMAT:256 F4:256 JUNK:512 TAU:48 DEL:48 YY:48 BB:4 TF:4 GO:4 PP:32 MH:32 MX:32 MXT:32 MM:8 ST:16 LT:128"
-                    " COL:40 WROW:48 I3:8 PWC:32 K1:32 K2:32 YT:8 PW1:32 PW2:32 RE0:16 WX:192"),
-        ("int32", "FL:512 UI:128 OFP:256 OFM:256 LI:64 CI:160 C4:128 CL:128 TI:16 F0:512 FD:512 FE:512 FG:512"),
-        ("uint16", "OFU:256 RR:256 OFS:32 OFO:32 OF2:32 OF3:32 LU:32 LCU:32 REP:16 REP2:2")):
+                     " IN2:512 IN3:512 KKP:512 MS:384 MD:384 OO:256 AW:32 C17:16 CN3:16 DL:64 ONE:272 TLM:128 WMARK:144 WMN:144 WMO:144 WPC:144 W15:144 W16:144"
+                     " IDENT:128 IK:512 IM:128 BLK:128 TRIU:128 TRIL:128 LANEG:128 TMPA:128 CL:128"
+                     " TL4:128 NTRIL:128 WE:144 KW8:256 RS8:256 C8:32 FS:1056 FC:1024 FX:1584 LV:64 SV:64 P3X:64 I8:512 S8:512 AX:64 I3X:1024"
+                     " CS:1024 CD:1024 DG:640 LC:384 OS:1536" % OW),
+        ("float16", "WSUM:144 KK:256 PEN:512 RR:256 PCW:32 CF:32"),
+        ("float32", "BML:144 FA:512 KU:256 KMAT:256 F4:256 JUNK:768 TAU:48 DEL:48 YY:48 BB:4 GO:4 PP:32 MH:32 MX:32 MXT:32 MM:12 ST:16 LT:160"
+                    " COL:40 WROW:48 I3:8 PWC:32 YT:8 PW2:32 RE0:16 OV:512"),
+        ("int32", "FL:512 UI:128 OFP:256 OFM:256 LI:64 CI:160 C4:128 TI:16 F0:512"),
+        ("uint16", "OFU:256 OFS:32 OFO:32 OF2:32 OF3:32 LU:32 LCU:32 REP:16 REP2:2 REP3:2 OFX:64 OX:64 LX:64")):
     for _n in _names.split():
         _n, _c = _n.split(":")
         SCRATCH[_n] = ("sbuf", [128, int(_c)], _dt)
 SCRATCH["XS"] = ("sbuf", [128, NSLOT * 512], "bfloat16")
 SCRATCH["XD"] = ("sbuf", [128, NSLOT * 512], "bfloat16")
-for _l in (1, 2, 3):
-    for _n, _c, _dt in (("FS", 512, "bfloat16"), ("FC", 512, "bfloat16"), ("FV", 512, "float32"), ("FA", 1024, "bfloat16"),
-                        ("FO", 64, "uint16"), ("OS", 1024, "bfloat16"), ("OV", 1024, "float32")):
-        SCRATCH[_n + str(_l)] = ("sbuf", [128, _c], _dt)
 
-SEMAPHORES = (["qV", "qS", "qP", "qG", "ld0", "ld1", "ld2", "out", "lsb", "lsa", "lsd"]
+SEMAPHORES = (["qV", "qS", "qP", "qG", "ld0", "ld1", "ld2", "ld3", "out", "lsb", "lsa", "lsd"]
               + ["%s%d" % (s, r) for s in ("bm", "ds", "dd") for r in range(RO)])
 
 
@@ -130,8 +128,20 @@ def rank_program(g, core, T, topo):
     def act(r, w, out, i, fn, **k):
         do("S", lambda e: e.activation(out, i, fn, **k), r, w)
 
+    def iota(w, out, pat, base=0, cm=0, small=True):
+        if small:
+            do("G", lambda e: e.iota(out, pat, base, cm, allow_small_or_imprecise_dtypes=True), "", w)
+        else:
+            do("G", lambda e: e.iota(out, pat, base, cm), "", w)
+
+    def pick(r, w, out, i, pat, op, other, base, cm):
+        do("G", lambda e: e.affine_select(out, i, pat, op, other, base, cm), r, w)
+
     def b(k, x, y):
         return T.PS[:, k * 512 + x:k * 512 + y]
+
+    def hs(t, h, n=16):
+        return t[:, h * n:h * n + n]
 
     def to_w(r, k, x, n, wt, src, c0, first=True, last=True):
         for q in range(16):
@@ -145,6 +155,7 @@ def rank_program(g, core, T, topo):
     lane = {c: far_e[i * ne:(i + 1) * ne] for i, c in enumerate(off)}
     lane[near] = near_e[:ne]
     ow = [cores.index(c) for c in off + [near, core]]
+    low = [float(GAP * (o - 2)) for o in ow]
     arrive = ne * (len(cores) - 1)
 
     def send(local, parts, keys):
@@ -160,28 +171,20 @@ def rank_program(g, core, T, topo):
         cnt[local] = cnt.get(local, 0) + ne * len(parts)
         mark("G", (local, cnt[local]), keys, [])
 
-    fill("F0", T.F0[:], 0)
     dma("S", "ld0", [(T.XS[:, 0:512], T.s0[:])], "", "XS0")
+    dma("Y", "ld2", [(T.OPS[:, 0:8192], T.opr[:])], "", "OPS")
+    fill("F0", T.F0[:], 0)
     dma("S", "ld1", [(T.F0[0::16, :], T.f0[:]), (T.F0[1::16, :], T.f0[:])], "", "F0")
-    dma("Y", "ld2", [(T.OPS[:, 0:8192], T.opr[:]), (T.OPS[:, 8192:OW], T.opr[:, 0:OW - 8192])], "", "OPS")
-
-    def iota(w, out, pat, base=0, cm=0, small=True):
-        if small:
-            do("G", lambda e: e.iota(out, pat, base, cm, allow_small_or_imprecise_dtypes=True), "", w)
-        else:
-            do("G", lambda e: e.iota(out, pat, base, cm), "", w)
+    dma("Y", "ld3", [(T.OPS[:, 8192:OW], T.opr[:, 0:OW - 8192])], "", "OPX")
 
     iota("TI", T.TI[:, 0:1], [[1, 1]], 0, 1, False)
     iota("CI", T.CI[:], [[1, 160]], small=False)
     iota("PW2", T.PW2[:], [[16, 32]])
     iota("RE0", T.RE0[:], [[0, 8], [16, 2]])
     iota("C4", T.C4[:], [[1, 8], [0, 16]], small=False)
-    iota("CL", T.CL[:], [[0, 8], [1, 16]], small=False)
-    iota("KWX", T.KWX[:], [[16, 8], [0, 34]])
-    iota("KKP", T.KKP[:], [[0, 2], [1, 128]])
-    iota("C17", T.C17[:], [[17, 2], [0, 8]])
-    iota("CN3", T.CN3[:], [[-256 * 17, 2], [0, 8]], -256)
-    iota("PW1", T.PW1[:], [[0, 4], [16, 8]])
+    for j in range(8):
+        iota("KMAT+", hs(T.KMAT, j, 32), [[0, 32]], KA[j])
+    iota("CL", T.CL[:], [[0, 8], [1, 16]], 1)
 
     def C(k):
         return T.COL[:, k:k + 1]
@@ -190,46 +193,75 @@ def rank_program(g, core, T, topo):
         return T.TI[:, k:k + 1]
     ci = T.CI[:, 0:128]
     cw = T.CI[:, 0:143]
-    cp("TI", "c0", C(0), TI(0))
+    for i in range(16):
+        fill("wr+", T.WROW[:, i:i + 1], WTS[i])
+    fill("ONE", T.ONE[:], 1.0)
     for k, sh, an in ((1, 0, 15), (2, 4, 7), (3, 4, 1), (4, 0, 7), (5, 3, 1)):
         ts("TI", "TI%d" % k, TI(k), TI(0), sh, A.logical_shift_right, an, A.bitwise_and)
     for k in (1, 2, 3):
         cp("TI%d" % k, "c%d" % k, C(k), TI(k))
-    for i in range(16):
-        fill("wr+", T.WROW[:, i:i + 1], WTS[i])
     ts("CI c1", "wm", T.WROW[:, 16:32], T.CI[:, 0:16], C(1), A.is_equal)
-    tt("wr wm", "wx", T.WROW[:, 32:48], T.WROW[:, 0:16], T.WROW[:, 16:32], A.mult)
-    red("wx", "c7", C(7), T.WROW[:, 32:48], A.add)
     ts("c2", "c13", C(13), C(2), 16.0, A.mult, 15.0, A.add)
-    ts("CI c13 c7", "WMARK", T.WMARK[:, 0:143], cw, C(13), A.is_equal, C(7), A.mult)
-    ts("PW2 c1", "PWC", T.PWC[:], T.PW2[:], C(1), A.add)
+    tt("wr wm", "wx", T.WROW[:, 32:48], T.WROW[:, 0:16], T.WROW[:, 16:32], A.mult)
     ts("RE0 c1", "REP", T.REP[:], T.RE0[:], C(1), A.add)
-    for j in range(8):
-        fill("KMAT+", T.KMAT[:, j * 32:(j + 1) * 32], KA[j])
-    ts("c1", "c26", C(26), C(1), 0.0, A.is_equal, 4.0, A.mult)
+    red("wx", "c7", C(7), T.WROW[:, 32:48], A.add)
+    ts("c1", "c26", C(26), C(1), 0.0, A.is_equal)
+    ts("CI c13 c7", "WMARK", T.WMARK[:, 0:143], cw, C(13), A.is_equal, C(7), A.mult)
+    to_w("WMARK XS0", 7, 0, 32, T.WMARK, T.XS, 0)
     ts("c1", "c27", C(27), C(1), 1.0, A.is_equal, 4.0, A.mult)
     ts("c1", "c28", C(28), C(1), 15.0, A.is_equal, 4.0, A.mult)
-    ts("c26 c28", "c20", C(20), C(26), 32.0, A.mult, C(28), A.add)
-    ts("F0", "FL", T.FL[:], T.F0[:], 5, A.logical_shift_right)
-    ts("F0", "FD", T.FD[:], T.F0[:], 31, A.bitwise_and)
-    ts("FL c26", "FE", T.FE[:], T.FL[:], C(26), A.mult)
-    ts("FD c27 c28", "FG", T.FG[:], T.FD[:], C(27), A.mult, C(28), A.add)
-    tt("FE FG", "XD0", T.XD[:, 0:512], T.FE[:], T.FG[:], A.add)
-    fill("XS1", T.XS[:, 512:1024], 0.0)
-    ts("XS1 c20", "XD1", T.XD[:, 512:1024], T.XS[:, 512:1024], C(20), A.add)
+    ts("c26 c28", "c20", C(20), C(26), 128.0, A.mult, C(28), A.add)
+    ts("c27", "c21", C(21), C(27), -32.0, A.mult)
+    ts("c26 c21", "c22", C(22), C(26), 4.0, A.mult, C(21), A.add)
+    ts("c1", "c10", C(10), C(1), 4.5, A.is_lt)
+    ts("c26 c10", "c9", C(9), C(26), 31.0, A.mult, C(10), A.add)
+    cp("c7", "wi0", TI(8), C(7))
+    ts("c9", "c11", C(11), C(9), 0.25, A.mult)
+    ts("wi0", "wi1", TI(9), TI(8), 3, A.bitwise_and)
+    ts("CI c13 c11", "WPC", T.WPC[:, 0:143], cw, C(13), A.is_equal, C(11), A.mult)
+    ts("wi1", "c8", C(8), TI(9), -1.0 / 4096, A.mult, 1026.0 / 4096, A.add)
     ts("C4 c2", "BLK", T.BLK[:], T.C4[:], C(2), A.is_equal)
-    ts("CL", "TA", T.TMPA[:], T.CL[:], 1.5, A.is_gt)
-    ts("CL", "TB", T.TMPB[:], T.CL[:], 3.5, A.is_lt)
-    tt("TA TB", "L1", T.LANEG[:], T.TMPA[:], T.TMPB[:], A.mult)
-    tt("L1 BLK", "TA", T.TMPA[:], T.LANEG[:], T.BLK[:], A.mult)
-    ts("CL", "TB", T.TMPB[:], T.CL[:], 1.0, A.add)
-    tt("TA TB", "L1", T.LANEG[:], T.TMPA[:], T.TMPB[:], A.mult)
-    ts("L1", "LANEG", T.LANEG[:], T.LANEG[:], -1.0, A.add)
+    ts("CI c13 c8", "WSUM", T.WSUM[:, 0:143], cw, C(13), A.is_equal, C(8), A.mult)
+    ts("F0", "FL", T.FL[:], T.F0[:], 5, A.logical_shift_right)
+    ts("F0 c27 c28", "ps6", b(6, 0, 512), T.F0[:], C(27), A.mult, C(28), A.add)
+    ts("FL c22", "FA", T.FA[:], T.FL[:], C(22), A.mult)
+    fill("XS1", T.XS[:, 512:1024], 0.0)
+    tt("FA ps6", "XD0", T.XD[:, 0:512], T.FA[:], b(6, 0, 512), A.add)
+    act("XS1 c20", "XD1", T.XD[:, 512:1024], T.XS[:, 512:1024], F.Identity, bias=C(20))
+    act("XS1 c20", "FBz", T.FB[:, 512:528], T.XS[:, 512:528], F.Identity, bias=C(20))
     fill("lo hi last e U", T.ST[:], 0.0)
+    fill("DL", T.DL[:], -71.0 / 8192)
     fill("last", T.ST[:, 6:9], 512.0)
     fill("U", T.ST[:, 10:11], 1023.0)
     cp("CI", "I3", T.I3[:, 0:3], T.CI[:, 0:3])
     ts("CI", "J3", T.I3[:, 4:7], T.CI[:, 0:3], 1.0, A.add)
+    for i in range(4):
+        fill("GO+", T.GO[:, i:i + 1], low[i])
+    pick("ONE", "IDENT", T.IDENT[:], T.ONE[:, 0:128], [[-1, 128]], A.is_equal, 0.0, 0, 1)
+    INEG, I45, IG, I16 = [hs(T.IK, k, 128) for k in range(4)]
+    for nm, t, v in (("INEG", INEG, -1.0), ("I45", I45, 45.0), ("IG", IG, GAP * 4096.0), ("I16", I16, 16.0)):
+        act("IDENT", nm, t, T.IDENT[:], F.Identity, scale=v)
+    zero = ow.index(0)
+    iota("BASE%d" % zero, hs(T.BASE, zero, 256), [[0, 256]])
+    for i in range(4):
+        iota("SCz+", T.SC[:, i * ST_:i * ST_ + 16], [[0, 16]])
+        iota("P3z+", T.P3[:, i * ST_:i * ST_ + 16], [[0, 16]])
+    iota("CHz", T.CH[:, 4096:CW], [[0, 16]])
+    iota("KWX", T.KWX[:], [[16, 8], [0, 34]])
+    iota("KKP", T.KKP[:], [[0, 4], [1, 128]])
+    iota("C17", T.C17[:], [[17, 2], [0, 8]])
+    iota("CN3", T.CN3[:], [[-256 * 17, 2], [0, 8]], -256)
+    pick("ONE", "RS17", T.RS17[:], T.ONE[:], [[0, 16], [1, 17]], A.is_gt, 0.0, 0, 0)
+    pick("BLK", "TRIU", T.TRIU[:], T.BLK[:], [[1, 128]], A.is_ge, 0.0, 0, -1)
+    pick("BLK", "TRIL", T.TRIL[:], T.BLK[:], [[-1, 128]], A.is_gt, 0.0, 0, 1)
+    for k in (2, 3):
+        iota("BMz+", T.BML[:, rank * 4 + k::16], [[0, RO]])
+    iota("KW8", T.KW8[:], [[16, 8], [0, 32]])
+    iota("C8", T.C8[:], [[8, 4], [0, 8]])
+    pick("ONE", "RS8", T.RS8[:], T.ONE[:, 0:256], [[0, 32], [1, 8]], A.is_gt, 0.0, 0, 0)
+    for n in (0, 1):
+        iota("FSz+", T.FS[:, n * 528 + 512:n * 528 + 528], [[0, 16]])
+
     LO, HI, LA, EE, UU = T.ST[:, 0:3], T.ST[:, 3:6], T.ST[:, 6:9], T.ST[:, 9:10], T.ST[:, 10:11]
     lt = {}
 
@@ -239,94 +271,146 @@ def rank_program(g, core, T, topo):
         x, k = lt[name]
         return T.LT[:, x:x + k]
 
-    def L1(name, i):
+    def L1(name, i, n=1):
         x = lt[name][0] + i
-        return T.LT[:, x:x + 1]
+        return T.LT[:, x:x + n]
 
-    def derive():
-        ts("e", "e1", L("e1"), EE, 1.0, A.add)
-        ts("J3 e", "oh1", L("oh1", 3), T.I3[:, 4:7], EE, A.is_equal)
-        ts("LANEG e1", "TLM", T.TLM[:], T.LANEG[:], L("e1"), A.is_equal)
-        ts("e", "e811", L("e811"), EE, 811.0, A.mult)
-        tt("oh1 hi", "th", L("th", 3), L("oh1"), HI, A.mult)
+    def derive(first):
         ts("I3 e", "oh", L("oh", 3), T.I3[:, 0:3], EE, A.is_equal)
-        red("th", "th1", L("th1"), L("th"), A.add)
+        ts("J3 e", "oh1", L("oh1", 3), T.I3[:, 4:7], EE, A.is_equal)
+        if not first:
+            ts("oh e", "e1", L("e1"), L1("oh", 0), 97.0, A.mult, EE, A.add)
+        ts("e", "e811", L("e811"), EE, 811.0, A.mult)
+        if not first:
+            ts("LANEG e1", "TLM", T.TLM[:], T.LANEG[:], -2.0, A.add, L("e1"), A.is_equal)
+        tt("oh1 hi", "th", L("th", 3), L("oh1"), HI, A.mult)
         tt("oh lo", "ol", L("ol", 3), L("oh"), LO, A.mult)
+        red("th", "th1", L("th1"), L("th"), A.add)
         ts("I3 e", "noh", L("noh", 3), T.I3[:, 0:3], EE, A.not_equal)
-        ts("oh th1", "thr", L("thr"), L1("oh", 0), 2000.0, A.mult, L("th1"), A.add)
         red("ol", "loe", L("loe"), L("ol"), A.add)
+        ts("oh th1", "thr", L("thr"), L1("oh", 0), 2000.0, A.mult, L("th1"), A.add)
 
-    cp("PWC", "OFS", T.OFS[:], T.PWC[:])
     fill("slot", L("slot"), 0.0)
-    derive()
-    ts("CI c0", "IDENT", T.IDENT[:], ci, C(0), A.is_equal)
-    ts("BLK c28", "TA", T.TMPA[:], T.BLK[:], C(28), A.mult, -0.09375, A.mult)
-    tt("IDENT TA", "IM", T.IM[:], T.IDENT[:], T.TMPA[:], A.add)
-    cp("c7", "wi0", TI(8), C(7))
-    ts("wi0", "wi1", TI(9), TI(8), 3, A.bitwise_and)
-    ts("wi1", "c8", C(8), TI(9), -1.0 / 4096, A.mult, 1026.0 / 4096, A.add)
-    ts("c1", "c9", C(9), C(1), 0.0, A.is_equal, 31.0, A.mult)
-    ts("c1", "c10", C(10), C(1), 3.5, A.is_lt)
-    ts("c9 c10", "c11", C(11), C(9), C(10), A.add, 0.25, A.mult)
-    ts("CI c13 c8", "WSUM", T.WSUM[:, 0:143], cw, C(13), A.is_equal, C(8), A.mult)
-    ts("CI c13 c11", "WPC", T.WPC[:, 0:143], cw, C(13), A.is_equal, C(11), A.mult)
-    INEG, I45, IG, I16 = [T.IK[:, k * 128:k * 128 + 128] for k in range(4)]
-    for nm, t, v in (("INEG", INEG, -1.0), ("I45", I45, 45.0), ("IG", IG, GAP * 4096.0), ("I16", I16, 16.0)):
-        ts("IDENT", nm, t, T.IDENT[:], v, A.mult)
-    fill("DL", T.DL[:], -71.0 / 8192)
-    fill("ONE", T.ONE[:], 1.0)
-    ts("XS1 c20", "FBz", T.FB[:, 512:528], T.XS[:, 512:528], C(20), A.add)
-    for i in range(4):
-        fill("GO+", T.GO[:, i:i + 1], float(GAP * ow[i]))
-    ts("GO", "t0", T.TAU[:, 0:4], T.GO[:], 512.0, A.add)
-    zero = ow.index(0)
+    derive(True)
 
-    late = [lambda: ts("CI", "TA", T.TMPA[:, 0:32], T.CI[:, 0:32], 15.5, A.is_gt),
-            lambda: ts("TA c3", "MH", T.MH[:], T.TMPA[:, 0:32], C(3), A.not_equal, 20000.0, A.mult),
-            lambda: fill("BASE%d" % zero, T.BASE[:, zero * 256:zero * 256 + 256], 0.0),
-            lambda: fill("SCz", T.SC[:], 0.0),
-            lambda: fill("P3z", T.P3[:], 0.0),
-            lambda: fill("RSm", T.RS17[:], 1.0),
-            lambda: fill("RS17", T.RS17[:, 0::17], 0.0, "RSm"),
-            lambda: ts("KWX c1", "KWX", T.KWX[:], T.KWX[:], C(1), A.add),
-            lambda: fill("KWX", T.KWX[:, 16::17], -1024.0),
-            lambda: ts("CI c0", "TB", T.TMPB[:], ci, C(0), A.is_ge),
-            lambda: tt("TB BLK", "TRIU", T.TRIU[:], T.TMPB[:], T.BLK[:], A.mult),
-            lambda: tt("TRIU BLK", "TRIL", T.TRIL[:], T.BLK[:], T.TRIU[:], A.subtract),
-            lambda: ts("c1", "c12", C(12), C(1), 14.5, A.is_lt),
-            lambda: ts("CI c13 c12", "W15", T.W15[:, 0:143], cw, C(13), A.is_equal, C(12), A.mult),
-            lambda: ts("CI c13", "W16", T.W16[:, 0:143], cw, C(13), A.is_equal),
-            lambda: fill("CHz", T.CH[:, 4096:CW], 0.0),
-            lambda: ts("TI4", "c14", C(14), TI(4), 34.0, A.mult, 16.0, A.add),
-            lambda: ts("TI5 c14", "REP2", T.REP2[:, 0:1], TI(5), 17.0, A.mult, C(14), A.add),
-            lambda: fill("BMz+", T.BML[:, rank * 4 + 2::16], 0.0),
-            lambda: fill("BMz+", T.BML[:, rank * 4 + 3::16], 0.0)]
+    def more_constants():
+        ts("GO", "t0", T.TAU[:, 0:4], T.GO[:], 512.0, A.add)
+        ts("CI", "TA", T.TMPA[:, 0:32], T.CI[:, 0:32], 15.5, A.is_gt)
+        ts("c1", "c12", C(12), C(1), 14.5, A.is_lt)
+        ts("TA c3", "MH", T.MH[:], T.TMPA[:, 0:32], C(3), A.not_equal, 20000.0, A.mult)
+        ts("CI c13 c12", "W15", T.W15[:, 0:143], cw, C(13), A.is_equal, C(12), A.mult)
+        ts("CI c13", "W16", T.W16[:, 0:143], cw, C(13), A.is_equal)
+        ts("TI4", "c14", C(14), TI(4), 34.0, A.mult, 16.0, A.add)
+        ts("PW2 c1", "PWC", T.PWC[:], T.PW2[:], C(1), A.add)
+        ts("TI5 c14", "REP2", T.REP2[:, 0:1], TI(5), 17.0, A.mult, C(14), A.add)
+        ts("BLK c28", "TA", T.TMPA[:], T.BLK[:], C(28), A.mult, -0.09375, A.mult)
+        tt("CL BLK", "LANEG", T.LANEG[:], T.CL[:], T.BLK[:], A.mult)
+        tt("IDENT TA", "IM", T.IM[:], T.IDENT[:], T.TMPA[:], A.add)
 
-    def output_constants():
-        fill("RSTm", T.RST[:], 1.0)
-        fill("RST", T.RST[:, 0::128], 0.0, "RSTm")
-        for l in (1, 2, 3):
-            fill("OS%d" % l, T["OS%d" % l][:], 0.0)
-            fill("OV%d" % l, T["OV%d" % l][:], 1023.0)
-        ts("BLK c11", "BCF", T.BCF[:], T.BLK[:], C(11), A.mult)
-        ts("PW1 c1", "PW1", T.PW1[:], T.PW1[:], C(1), A.add, -16.0, A.mult)
-        ts("PW1", "K1", T.K1[:], T.PW1[:], -513.0 * 16, A.add)
-        ts("PWC", "K2", T.K2[:], T.PWC[:], 512.0, A.add, 256.0, A.mult)
+    late = [lambda: ts("KWX c1", "KWX", T.KWX[:], T.KWX[:], C(1), A.add),
+            lambda: fill("KWX", T.KWX[:, 16::17], -1024.0)]
+    spare = [lambda: ts("KW8 c1", "KW8", T.KW8[:], T.KW8[:], C(1), A.add),
+             lambda: fill("KW8", T.KW8[:, 7::8], -1024.0),
+             lambda: ts("LANEG", "TL4", T.TL4[:], T.LANEG[:], 5.0, A.is_equal),
+             lambda: ts("TRIL", "NTRIL", T.NTRIL[:], T.TRIL[:], -1.0, A.mult),
+             lambda: ts("c28 c12", "c16", C(16), C(28), 128.0, A.mult, C(12), A.add),
+             lambda: ts("CI c13 c16", "WE", T.WE[:, 0:143], cw, C(13), A.is_equal, C(16), A.mult),
+             lambda: ts("TI4", "c17", C(17), TI(4), 32.0, A.mult, 7.0, A.add),
+             lambda: ts("TI5 c17", "c18", C(18), TI(5), 8.0, A.mult, C(17), A.add),
+             lambda: ts("CI c18", "REP3", T.REP3[:], T.CI[:, 0:2], 16.0, A.mult, C(18), A.add),
+             lambda: ts("XS1 c20", "FXz+", T.FX[:, 512:528], T.XS[:, 512:528], C(20), A.add),
+             lambda: ts("XS1 c20", "FXz+", T.FX[:, 1040:1056], T.XS[:, 512:528], C(20), A.add)]
+
+    def pick3(name, x, i, j, sel):
+        u, v = T.ST[:, x + i:x + i + 1], T.ST[:, x + j:x + j + 1]
+        tt("last hi", name + "d", L(name + "d"), v, u, A.subtract)
+        ts("last hi oh %sd" % name, name, L(name), L(name + "d"), sel, A.mult, u, A.add)
+
+    def old_where():
+        for n, (i, k) in enumerate(((0, 0), (2, 2))):
+            pick3("sx%d" % n, 6, i, 1, L1("oh", k))
+            pick3("hx%d" % n, 3, i, 1, L1("oh", k))
+            ts("PWC sx%d" % n, "OFX%d" % n, hs(T.OFX, n, 32), T.PWC[:], L("sx%d" % n), A.add)
+        ts("oh c2", "lc0", L("lc0"), L1("oh", 0), 32.0, A.mult, C(2), A.add)
+        ts("noh", "lcx", L("lcx"), L1("noh", 2), 32.0, A.mult, 32.0, A.add)
+        ts("e c2", "lc2", L("lc2"), EE, 32.0, A.mult, C(2), A.add)
+        tt("lcx c2", "lc1", L("lc1"), L("lcx"), C(2), A.add)
+        for n in range(3):
+            ts("lc%d CI c11" % n, "LC%d" % n, hs(T.LC, n, 128), ci, L("lc%d" % n), A.is_equal, C(11), A.mult)
+
+    def old_take(sk, dk, win):
+        for n in (0, 1):
+            act(dk + " OFX%d" % n, "FC%d" % n, hs(T.FC, n, 512), T.XD[:, 0:win].indirect(hs(T.OFX, n, 32)), F.Copy)
+        act(sk + " OFX0", "FS0", T.FS[:, 0:512], T.XS[:, 0:win].indirect(hs(T.OFX, 0, 32)), F.Copy)
+
+    def old_front(sk, win):
+        cp(sk + " OFX1", "FS1", T.FS[:, 528:1040], T.XS[:, 0:win].indirect(hs(T.OFX, 1, 32)))
+        for n in (0, 1):
+            mm("TL4 FS%d" % n, "ps%d" % n, b(n, 0, 512), T.TL4[:], T.FS[:, n * 528:n * 528 + 512], True, False)
+            mm("IM FC%d" % n, "ps%d" % n, b(n, 0, 512), T.IM[:], hs(T.FC, n, 512), False, True)
+        for k, sel in enumerate((L1("oh", 0), L1("oh", 1), L1("oh", 2), L1("noh", 0), L1("noh", 2))):
+            act("IDENT oh noh", "DG%d" % k, DG[k], T.IDENT[:], F.Identity, scale=sel)
+        for n in (0, 1):
+            ts("ps%d" % n, "FX%d" % n, T.FX[:, n * 528:n * 528 + 512], b(n, 0, 512), M4, A.add, M4, A.subtract)
+            to_w("WPC FX%d" % n, 2 + n, 0, 32, T.WPC, T.FX, n * 528)
+        for n in (0, 1):
+            ts("ps%d hx%d" % (2 + n, n), "LV%d" % n, hs(T.LV, n, 32), b(2 + n, 0, 32), L("hx%d" % n), A.is_lt)
+        for n in (0, 1):
+            sv = hs(T.SV, n, 32)
+            scan("RS8 LV%d" % n, "SV%d" % n, sv, T.RS8[:, 0:32], hs(T.LV, n, 32), A.mult, A.add)
+            for c in range(8):
+                mm("BLK SV%d" % n, "ps%d" % (6 + n), b(6 + n, c * 32, c * 32 + 32), T.BLK[:], sv)
+            mm("BLK SV%d" % n, "ps%d" % (4 + n), b(4 + n, 0, 32), T.BLK[:], sv, True, False)
+            mm("NTRIL LV%d" % n, "ps%d" % (4 + n), b(4 + n, 0, 32), T.NTRIL[:], hs(T.LV, n, 32), False, True)
+            act("ps%d" % (4 + n), "P3X%d" % n, hs(T.P3X, n, 32), b(4 + n, 0, 32), F.Copy)
+        for n in (0, 1):
+            tt("ps%d KW8" % (6 + n), "I8%d" % n, hs(T.I8, n, 256), b(6 + n, 0, 256), T.KW8[:], A.is_le)
+        for n in (0, 1):
+            scan("RS8 I8%d" % n, "S8%d" % n, hs(T.S8, n, 256), T.RS8[:], hs(T.I8, n, 256), A.mult, A.add)
+        for n in (0, 1):
+            tt("S8%d REP3 C8" % n, "AX%d" % n, hs(T.AX, n, 32), hs(T.S8, n, 256).indirect(T.REP3[:]), T.C8[:], A.add)
+        for n in (0, 1):
+            cp("AX%d" % n, "OX%d" % n, hs(T.OX, n, 32), hs(T.AX, n, 32))
+
+    DG = [hs(T.DG, k, 128) for k in range(5)]
+    parts = ((1, 3, 0), (2, 0, 0), (2, 2, 1), (3, 4, 1))
+
+    def old_back():
+        for n in (0, 1):
+            tt("P3X%d OX%d KKP" % (n, n), "I3X%d" % n, hs(T.I3X, n, 512), hs(T.P3X, n, 32).indirect(hs(T.OX, n, 32)), T.KKP[:], A.is_le)
+            mm("I16 AX%d" % n, "ps%d" % (6 + n), b(6 + n, 0, 32), I16, hs(T.AX, n, 32), True, False)
+            to_w("WE I3X%d" % n, 6 + n, 0, 32, T.WE, T.I3X, n * 512, False, True)
+
+    def old_list(n):
+        ts("ps%d" % (6 + n), "LX%d" % n, hs(T.LX, n, 32), b(6 + n, 0, 32), 512.0, A.min)
+        if n == 0:
+            act("FS0 FSz LX0", "CS0", hs(T.CS, 0, 512), hs(T.FS, 0, 528).indirect(hs(T.LX, 0, 32)), F.Copy)
+        act("FX%d FXz LX%d" % (n, n), "CD%d" % n, hs(T.CD, n, 512), hs(T.FX, n, 528).indirect(hs(T.LX, n, 32)), F.Copy)
+
+    def old_put():
+        cp("FS1 FSz LX1", "CS1", hs(T.CS, 1, 512), hs(T.FS, 1, 528).indirect(hs(T.LX, 1, 32)))
+        for i, (l, k, n) in enumerate(parts):
+            mm("DG%d CS%d" % (k, n), "ps%d" % l, b(l, 0, 512), DG[k], hs(T.CS, n, 512), i != 2, False)
+        for n in (0, 1):
+            mm("LC%d CD%d" % (n, n), "ps4", b(4, 0, 512), hs(T.LC, n, 128), hs(T.CD, n, 512), n == 0, False)
 
     skeys, dkeys = ["XS0", "XS1"], ["XD0", "XD1"]
     for r in range(RO):
         win = (r + 2) * 512
-        cp(" ".join(skeys) + " OFS", "SS", T.SS[:], T.XS[:, 0:win].indirect(T.OFS[:]))
+        end = r + 1 == RO
         if r == 0:
-            to_w("WMARK XS0", 7, 0, 32, T.WMARK, T.XS, 0)
+            SS, FB, ssk, fbk, opk, OPS = T.XS[:, 0:512], T.XD, "XS0", "XD0 XD1", "OPS", T.OPS[:, 0:8192]
         else:
+            SS, FB, ssk, fbk, opk, OPS = T.SS[:], T.FB, "SS", "FB FBz", "OPS OPX", T.OPS[:]
+            cp(" ".join(skeys) + " OFS", "SS", SS, T.XS[:, 0:win].indirect(T.OFS[:]))
             to_w("WMN " + " ".join(skeys[-2:]), 7, 0, 32, T.WMN, T.XS, win - 512, False, True)
-        act(" ".join(dkeys) + " OFS", "SF", T.SF[:], T.XD[:, 0:win].indirect(T.OFS[:]), F.Copy)
-        mm("TLM SS", "ps6", b(6, 0, 512), T.TLM[:], T.SS[:], True, False)
-        mm("IM SF", "ps6", b(6, 0, 512), T.IM[:], T.SF[:], False, True)
-        act("ps6", "FA", T.FA[:], b(6, 0, 512), F.Identity, bias=M4)
-        act("FA", "FB", T.FB[:, 0:512], T.FA[:], F.Identity, bias=-M4)
-        u = [T.UI[:, k * 32:(k + 1) * 32] for k in range(4)]
+            act(" ".join(dkeys) + " OFS", "SF", T.SF[:], T.XD[:, 0:win].indirect(T.OFS[:]), F.Copy)
+            mm("TLM SS", "ps6", b(6, 0, 512), T.TLM[:], SS, True, False)
+            mm("IM SF", "ps6", b(6, 0, 512), T.IM[:], T.SF[:], False, True)
+            act("ps6", "FA", T.FA[:], b(6, 0, 512), F.Identity, bias=M4)
+            act("FA", "FB", T.FB[:, 0:512], T.FA[:], F.Identity, bias=-M4)
+        sst = T.XS if r == 0 else T.SS
+        u = [hs(T.UI, k, 32) for k in range(4)]
         cp("ps7", "u0", u[0], b(7, 0, 32))
         ts("u0", "u1", u[1], u[0], 4095, A.bitwise_and)
         tt("u1", "u2", u[2], u[1], u[1], A.mult)
@@ -335,24 +419,26 @@ def rank_program(g, core, T, topo):
         tt("u3 REP KU", "OFP", T.OFP[:], u[3].indirect(T.REP[:]), T.KU[:], A.add)
         ts("OFP", "OFM", T.OFM[:], T.OFP[:], 8191, A.bitwise_and)
         ts("OFM e811", "OFU", T.OFU[:], T.OFM[:], L("e811"), A.add)
-        to_w("WPC FB", 7, 32, 32, T.WPC, T.FB, 0)
+        to_w("WPC " + fbk, 7, 32, 32, T.WPC, FB, 0)
+        if r == 0:
+            more_constants()
 
         def opj(j, x=0, y=512):
-            return T.OPS[:].indirect(T.OFU[:, j * 32 + x // 16:j * 32 + y // 16])
+            return OPS.indirect(T.OFU[:, j * 32 + x // 16:j * 32 + y // 16])
 
         def vg(j, x=0, y=512):
-            tt("OPS OFU SS", "DY%d.%d" % (j, x), T.DY[:, j * 512 + x:j * 512 + y], opj(j, x, y), T.SS[:, x:y], A.subtract)
+            tt(opk + " OFU " + ssk, "DY%d.%d" % (j, x), T.DY[:, j * 512 + x:j * 512 + y], opj(j, x, y), sst[:, x:y], A.subtract)
 
         def ab(j, x=0, y=512):
             if j < 6:
                 act("DY%d.%d" % (j, x), "CH%d+" % j, T.CH[:, j * 512 + x:j * 512 + y], T.DY[:, j * 512 + x:j * 512 + y], F.Abs)
             else:
-                act("ps%d" % (j - 2), "CH%d" % j, T.CH[:, j * 512:j * 512 + 512], b(j - 2, 0, 512), F.Abs)
+                act("ps%d" % (j - 2), "CH%d" % j, hs(T.CH, j, 512), b(j - 2, 0, 512), F.Abs)
 
         def sg(j):
-            raw = T.RAW[:, (j - 6) * 512:(j - 5) * 512]
-            act("OPS OFU", "RAW%d" % j, raw, opj(j), F.Copy)
-            mm("INEG SS", "ps%d" % (j - 2), b(j - 2, 0, 512), INEG, T.SS[:], True, False)
+            raw = hs(T.RAW, j - 6, 512)
+            act(opk + " OFU", "RAW%d" % j, raw, opj(j), F.Copy)
+            mm("INEG " + ssk, "ps%d" % (j - 2), b(j - 2, 0, 512), INEG, SS, True, False)
             mm("IDENT RAW%d" % j, "ps%d" % (j - 2), b(j - 2, 0, 512), T.IDENT[:], raw, False, True)
 
         def sums(k):
@@ -362,21 +448,22 @@ def rank_program(g, core, T, topo):
             to_w("WSUM CH%d CH%d" % (2 * k, 2 * k + 1), k, 0, 64, T.WSUM, T.CH, k * 1024, False, True)
 
         def keys(k):
-            s = slice(k * 64, k * 64 + 64)
-            pk = "ps%d" % k
-            ts(pk, "F4%d" % k, T.F4[:, s], b(k, 0, 64), M2, A.add, M2, A.subtract)
-            ts(pk, "KK%d" % k, T.KK[:, s], b(k, 0, 64), M0, A.add, M0, A.subtract)
-            tt(pk + " F4%d" % k, "OO%d" % k, T.OO[:, s], b(k, 0, 64), T.F4[:, s], A.subtract)
-            ts("KK%d loe" % k, "PEN%d" % k, T.PEN[:, s], T.KK[:, s], L("loe"), A.is_lt, 8192.0, A.mult)
-            mm("IDENT KK%d" % k, pk, b(k, 64, 128), T.IDENT[:], T.KK[:, s], True, False)
-            mm("IG OO%d" % k, pk, b(k, 64, 128), IG, T.OO[:, s], False, False)
-            mm("IDENT PEN%d" % k, pk, b(k, 64, 128), T.IDENT[:], T.PEN[:, s], False, True)
+            pk, x, y = "ps%d" % k, b(k, 0, 64), b(k, 64, 128)
+            kk, p0, p1 = hs(T.KK, k, 64), hs(T.PEN, k, 64), hs(T.PEN, 4 + k, 64)
+            ts(pk, "F4%d" % k, hs(T.F4, k, 64), x, M2, A.add, M2, A.subtract)
+            ts(pk, "KK%d" % k, kk, x, M0, A.add, M0, A.subtract)
+            tt(pk + " F4%d" % k, "OO%d" % k, hs(T.OO, k, 64), x, hs(T.F4, k, 64), A.subtract)
+            ts("KK%d loe" % k, "PEN%d" % k, p0, kk, L("loe"), A.is_lt, 8192.0, A.mult)
+            ts("KK%d" % k, "PEM%d" % k, p1, kk, float(GAP), A.is_ge, 8192.0, A.mult)
+            mm("IDENT KK%d" % k, pk, y, T.IDENT[:], kk, True, False)
+            mm("IG OO%d" % k, pk, y, IG, hs(T.OO, k, 64), False, False)
+            mm("IDENT PEN%d" % k, pk, y, T.IDENT[:], p0, False, False)
+            mm("IDENT PEM%d" % k, pk, y, T.IDENT[:], p1, False, True)
 
         def key16(k):
-            s = slice(k * 64, k * 64 + 64)
-            ts("ps%d" % k, "RR+", T.RR[:, s], b(k, 64, 128), 1.5 * GAP, A.add)
-            mm("IDENT KK%d" % k, "ps6", b(6, k * 64, k * 64 + 64), T.IDENT[:], T.KK[:, s], True, False)
-            mm("IDENT PEN%d" % k, "ps6", b(6, k * 64, k * 64 + 64), T.IDENT[:], T.PEN[:, s], False, True)
+            ts("ps%d" % k, "RR+", hs(T.RR, k, 64), b(k, 64, 128), -0.5 * GAP, A.add)
+            mm("IDENT KK%d" % k, "ps6", b(6, k * 64, k * 64 + 64), T.IDENT[:], hs(T.KK, k, 64), True, False)
+            mm("IDENT PEN%d" % k, "ps6", b(6, k * 64, k * 64 + 64), T.IDENT[:], hs(T.PEN, k, 64), False, True)
 
         vg(0), sg(6), ab(0), vg(1)
         ts("ps7 thr", "PP", T.PP[:], b(7, 32, 64), L("thr"), A.is_ge, 1023.0, A.mult)
@@ -384,6 +471,8 @@ def rank_program(g, core, T, topo):
         tt("ps7 PP", "PCW", T.PCW[:], b(7, 32, 64), T.PP[:], A.max)
         sums(0), ab(6), ab(2), vg(3), ab(7), sums(3), ab(3), sums(1), vg(4), ab(4)
         vg(5, 0, 256), ab(5, 0, 256), vg(5, 256, 512), ab(5, 256, 512)
+        if end:
+            old_take(" ".join(skeys), " ".join(dkeys), win)
         keys(0), keys(3), sums(2), keys(1), key16(0), key16(3), key16(1), keys(2), key16(2)
 
         def col(t, i, s):
@@ -391,49 +480,55 @@ def rank_program(g, core, T, topo):
 
         def count(i, k, src, key, w, out, scale, bias, rk=""):
             for n in range(4):
-                mm("BLK " + key, "ps%d" % k, b(k, 128, 192), T.BLK[:], src[:, i * 256 + n * 64:i * 256 + n * 64 + 64], n == 0, n == 3)
-            act("ps%d %s" % (k, rk), "JUNK%d %s" % (i, w), T.JUNK[:, i * 64:i * 64 + 64], b(k, 128, 192), F.Identity, bias=bias, scale=scale, accum_out=out)
+                mm("BLK " + key, "ps%d" % k, b(k, 128, 192), T.BLK[:], hs(src, 4 * i + n, 64), n == 0, n == 3)
+            act("ps%d %s" % (k, rk), "JUNK%d %s" % (i, w), hs(T.JUNK, i, 64), b(k, 128, 192), F.Identity, bias=bias, scale=scale, accum_out=out)
+
+        def on_s(i, s):
+            return i in SSTEP and 1 <= s < 9
 
         def step(i, s):
             hi_, lo_ = (256.0 / 2 ** s, -256.0 / 2 ** s) if s < 9 else (0.0, -1.0)
             if on_s(i, s):
                 n = int(hi_)
-                act("ONE y%d.%d" % (i, s), "JUNK%d d%d.%d" % (4 + i, i, s), T.JUNK[:, 256 + i * 64:256 + i * 64 + n], T.ONE[:, 0:n], F.Sign,
+                act("ONE y%d.%d" % (i, s), "JUNK%d d%d.%d" % (4 + i, i, s), T.JUNK[:, 256 + i * 128:256 + i * 128 + n], T.ONE[:, 0:n], F.Sign,
                     scale=col(T.YY, i, s), accum_out=col(T.DEL, i, s))
             else:
                 ts("y%d.%d" % (i, s), "d%d.%d" % (i, s), col(T.DEL, i, s), col(T.YY, i, s), hi_, A.min, lo_, A.max)
 
-        def on_s(i, s):
-            return i in SSTEP and 2 <= s < 9
-
         def compare(i, s):
-            io = T.IN0[:, i * 256:i * 256 + 256]
-            t0 = GAP * ow[i] + 512.0
+            io = hs(T.IN0, i, 256)
             if s == 0:
-                ts("RR", "IN%d" % i, io, T.RR[:], t0, A.is_lt)
+                ts("RR", "IN%d" % i, io, T.RR[:], low[i] + 512.0, A.is_lt)
+            elif s == 10 and end:
+                ts("RR TG", "IN%d" % i, io, T.RR[:], T.MM[:, 8 + i:9 + i], A.is_lt)
             else:
-                prev = t0 if s == 1 else col(T.TAU, i, s - 1)
-                ts("RR d%d.%d t%d" % (i, s - 1, s - 1), "IN%d" % i, io, T.RR[:], col(T.DEL, i, s - 1), A.subtract, prev, A.is_lt)
+                ts("RR d%d.%d t%d" % (i, s - 1, s - 1), "IN%d" % i, io, T.RR[:], col(T.DEL, i, s - 1), A.subtract, col(T.TAU, i, s - 1), A.is_lt)
             if s < 10:
                 count(i, i, T.IN0, "IN%d" % i, "y%d.%d" % (i, s), col(T.YY, i, s), -BIG, T.BB[:, i:i + 1] if ow[i] else BIG * 128.5 / 64, "BB%d" % i)
                 if on_s(i, s):
                     step(i, s)
-            else:
-                x = i * ST_ + 16
-                scan("IN%d BASE%d SCz" % (i, i), "SC%d" % i, T.SC[:, x:x + 256], io, T.BASE[:, i * 256:i * 256 + 256], A.add, A.subtract)
+
+        def prefix(i):
+            x = i * ST_ + 16
+            scan("IN%d BASE%d SCz" % (i, i), "SC%d" % i, T.SC[:, x:x + 256], hs(T.IN0, i, 256), hs(T.BASE, i, 256), A.add, A.subtract)
 
         def level(s):
             dk = " ".join("d%d.%d" % (i, s - 1) for i in range(4))
-            tt(dk + " t%d" % (s - 1), "t%d" % s, T.TAU[:, 4 * s:4 * s + 4], T.TAU[:, 4 * s - 4:4 * s], T.DEL[:, 4 * s - 4:4 * s], A.add)
+            tt(dk + " t%d" % (s - 1), "t%d" % s, hs(T.TAU, s, 4), hs(T.TAU, s - 1, 4), hs(T.DEL, s - 1, 4), A.add)
 
         x = r * 16 + rank * 4
         own = T.BML[:, x:x + 4]
+        bk = "BMb%d BMm%d bm%d" % (r, r, r)
         extra = [lambda: red("ps6", "MM0", T.MM[:, 0:1], b(6, 0, 256), A.min),
                  lambda: ts("MM0 MH", "MX", T.MX[:], T.MH[:], T.MM[:, 0:1], A.add),
                  lambda: V(lambda e: e.transpose(T.MXT[:], T.MX[:]), "MX", "MXT"),
                  lambda: red("MXT", "BMm%d" % r, T.BML[:, x + 1:x + 2], T.MXT[:], A.min)]
+        bound = [lambda: level(10),
+                 lambda: tt("t10 GO", "TB4", T.MM[:, 4:8], hs(T.TAU, 10, 4), T.GO[:], A.subtract),
+                 lambda: red("TB4", "BMb%d" % r, T.BML[:, x:x + 1], T.MM[:, 4:8], A.min),
+                 lambda: send("lsb", [(c, lane[c], "bm%d" % r, own, own) for c in lane], "BMb%d BMm%d BMz" % (r, r))]
         for n, i in enumerate([i for i in range(4) if ow[i]]):
-            ts("RR", "BASE%d" % i, T.BASE[:, i * 256:i * 256 + 256], T.RR[:], float(GAP * ow[i]), A.is_lt)
+            ts("RR", "BASE%d" % i, hs(T.BASE, i, 256), T.RR[:], low[i], A.is_lt)
             count(i, (4, 5, 7)[n], T.BASE, "BASE%d" % i, "BB%d" % i, T.BB[:, i:i + 1], BIG / 64, BIG * 128.5 / 4096)
 
         def place1(h):
@@ -451,9 +546,6 @@ def rank_program(g, core, T, topo):
                 y = z + i * ST_ + 16
                 act("ps%d P3z" % h, "P3%d+" % h, T.P3[:, y:y + 256], b(h, i * 256, i * 256 + 256), F.Copy)
 
-        def hs(t, h, n=16):
-            return t[:, h * n:h * n + n]
-
         def place2(h):
             return [lambda: tt("ps%d KWX" % (4 + h), "IN1%d" % h, hs(T.IN1, h, 272), b(4 + h, 0, 272), T.KWX[:], A.is_le),
                     lambda: scan("RS17 IN1%d" % h, "S1%d" % h, hs(T.S1, h, 272), T.RS17[:], hs(T.IN1, h, 272), A.mult, A.add),
@@ -461,20 +553,21 @@ def rank_program(g, core, T, topo):
                     lambda: cp("AW%d" % h, "OF2%d" % h, hs(T.OF2, h), hs(T.AW, h))]
 
         def place3(h):
-            tt("C2%d OF2%d KKP" % (h, h), "IN2%d" % h, hs(T.IN2, h, 256), T.C2[:, h * 48:h * 48 + 34].indirect(hs(T.OF2, h)), T.KKP[:], A.is_le)
+            tt("C2%d OF2%d KKP" % (h, h), "IN2%d" % h, hs(T.IN2, h, 256), T.C2[:, h * 48:h * 48 + 34].indirect(hs(T.OF2, h)), T.KKP[:, 0:256], A.is_le)
             mm("I16 AW%d" % h, "ps%d" % (2 + h), b(2 + h, 0, 16), I16, hs(T.AW, h), True, False)
             to_w("W15 IN2%d" % h, 2 + h, 0, 16, T.W15, T.IN2, h * 256, False, True)
 
         def place4(h):
             cp("ps%d" % (2 + h), "OF3%d" % h, hs(T.OF3, h), b(2 + h, 0, 16))
             cp("ps%d" % (2 + h), "CF%d" % h, hs(T.CF, h), b(2 + h, 0, 16))
-            tt("P3%d P3z OF3%d KKP" % (h, h), "IN3%d" % h, hs(T.IN3, h, 256), hs(T.P3, h, 544).indirect(hs(T.OF3, h)), T.KKP[:], A.is_le)
+            tt("P3%d P3z OF3%d KKP" % (h, h), "IN3%d" % h, hs(T.IN3, h, 256), hs(T.P3, h, 544).indirect(hs(T.OF3, h)), T.KKP[:, 0:256], A.is_le)
             mm("IDENT CN3", "ps%d" % (4 + h), b(4 + h, 0, 16), T.IDENT[:], T.CN3[:], True, False)
             mm("I16 CF%d" % h, "ps%d" % (4 + h), b(4 + h, 0, 16), I16, hs(T.CF, h), False, False)
             to_w("W16 IN3%d" % h, 4 + h, 0, 16, T.W16, T.IN3, h * 256, False, True)
 
         xo = (r + 2) * 512 + rank * 128
         chk = " ".join("CH%d" % j for j in range(8)) + " CHz"
+        fbw = FB[:, 0:528]
 
         def place5(h):
             cp("ps%d" % (4 + h), "LU%d" % h, hs(T.LU, h), b(4 + h, 0, 16))
@@ -488,69 +581,85 @@ def rank_program(g, core, T, topo):
                 cp(chk + " LU1", "XSo%d" % r, T.XS[:, xo:xo + 128], T.CH[:].indirect(hs(T.LU, 3, 8)))
             ts("LJ%d" % h, "LCU%d" % h, hs(T.LCU, h), hs(T.LI, 2 + h), 512.0, A.min)
             if h == 0:
-                act("FB FBz LCU0", "MD0", T.MD[:, 0:256], T.FB[:].indirect(hs(T.LCU, 0)), F.Copy)
+                act(fbk + " LCU0", "MD0", T.MD[:, 0:256], fbw.indirect(hs(T.LCU, 0)), F.Copy)
             else:
-                act("FB FBz LCU1", "MD1", T.MD[:, 256:384], T.FB[:].indirect(hs(T.LCU, 2, 8)), F.Copy)
-                act("FB FBz LCU1", "XDo%d" % r, T.XD[:, xo:xo + 128], T.FB[:].indirect(hs(T.LCU, 3, 8)), F.Copy)
+                act(fbk + " LCU1", "MD1", T.MD[:, 256:384], fbw.indirect(hs(T.LCU, 2, 8)), F.Copy)
+                act(fbk + " LCU1", "XDo%d" % r, T.XD[:, xo:xo + 128], fbw.indirect(hs(T.LCU, 3, 8)), F.Copy)
 
         for s in range(11):
+            if s == 10 and end:
+                for i in range(4):
+                    step(i, 9)
+                while bound:
+                    bound.pop(0)()
+                old_front(" ".join(skeys), win)
+                red(bk, "B", L("B"), T.BML[:, r * 16:r * 16 + 16:4], A.min)
+                ts("GO B", "TG", T.MM[:, 8:12], T.GO[:], L("B"), A.add)
+            if s == 10:
+                for h in (0, 1):
+                    for f in ([] if end else [lambda i: step(i, 9)]) + [lambda i: compare(i, 10), prefix]:
+                        f(2 * h), f(2 * h + 1)
+                    place1(h)
+                break
             for i in range(4):
                 if s and not on_s(i, s - 1):
                     step(i, s - 1)
                 compare(i, s)
-                if s == 10 and i % 2:
-                    place1(i // 2)
-            if 0 < s < 10:
+            if s:
                 level(s)
-            for _ in range(3):
-                if late:
-                    late.pop(0)()
+            if late:
+                late.pop(0)()
             if s > 3 and extra:
                 extra.pop(0)()
         pa, pb = place2(0), place2(1)
-        pa[0](), level(10), pa[1]()
-        tt("t10 GO", "TB4", T.MM[:, 4:8], T.TAU[:, 40:44], T.GO[:], A.subtract)
-        pa[2](), pb[0](), pa[3]()
-        red("TB4", "BMb%d" % r, T.BML[:, x:x + 1], T.MM[:, 4:8], A.min)
-        send("lsb", [(c, lane[c], "bm%d" % r, own, own) for c in lane], "BMb%d BMm%d BMz" % (r, r))
+        for f in (pa, bound, pa, bound, pa, pb, pa, bound, bound):
+            if f:
+                f.pop(0)()
         place3(0)
-        pb[1](), pb[2]()
-        ts("oh", "lb", L("lb", 3), L("oh"), float((r + 2) * 512), A.mult)
-        pb[3]()
-        tt("last noh", "la", L("la", 3), LA, L("noh"), A.mult)
+        pb[0](), pb[1]()
+        tt("hi noh", "ha", L("ha", 3), HI, L("noh"), A.mult)
+        pb[2]()
+        tt("last oh1", "sl", L("sl", 2), T.ST[:, 6:8], L1("oh1", 1, 2), A.mult)
         place3(1)
         place4(0)
-        tt("hi noh", "ha", L("ha", 3), HI, L("noh"), A.mult)
-        tt("last oh1", "sl", L("sl", 2), T.ST[:, 6:8], T.LT[:, lt["oh1"][0] + 1:lt["oh1"][0] + 3], A.mult)
         place4(1)
         place5(0)
         send("lsa", [(c, lane[c], "ds%d" % r, hs(T.MS, i, 128), T.XS[:, xo:xo + 128]) for i, c in enumerate(off)], "MS0")
         place5(1)
         send("lsd", [(near, near_e[ne:2 * ne], "ds%d" % r, hs(T.MS, 2, 128), T.XS[:, xo:xo + 128])]
              + [(c, lane[c], "dd%d" % r, hs(T.MD, i, 128), T.XD[:, xo:xo + 128]) for i, c in enumerate(off + [near])], "MS1 MD0 MD1")
-        bk = "BMb%d BMm%d bm%d" % (r, r, r)
-        red(bk, "B", L("B"), T.BML[:, r * 16:r * 16 + 16:4], A.min)
+        if end:
+            old_back()
+            old_list(0)
+        else:
+            red(bk, "B", L("B"), T.BML[:, r * 16:r * 16 + 16:4], A.min)
         red(bk, "M", L("M"), T.BML[:, r * 16 + 1:r * 16 + 16:4], A.min)
-        red("sl", "sb", L("sb"), L("sl"), A.add)
+        if not end:
+            red("sl", "sb", L("sb"), L("sl"), A.add)
         tt("B U", "mn", L("mn"), L("B"), UU, A.min)
         ts("loe B", "x", L("x"), L("loe"), 1.0, A.add, L("B"), A.max)
         ts("M B oh", "k2", L("k2"), L("M"), L("B"), A.is_lt, L1("oh", 2), A.mult)
         ts("M mn oh", "nadv", L("nadv"), L("M"), L("mn"), A.is_ge, L1("oh", 2), A.max)
         ts("x U noh", "xu", L("xu"), L("x"), UU, A.is_ge, L1("noh", 0), A.mult)
-        tt("sb slot", "sd", L("sd"), L("sb"), L("slot"), A.subtract)
+        if end:
+            old_list(1)
+        else:
+            tt("sb slot", "sd", L("sd"), L("sb"), L("slot"), A.subtract)
         ts("xu nadv k2", "back", L("back"), L("xu"), L("nadv"), A.mult, L("k2"), A.max)
         ts("nadv", "adv", L("adv"), L("nadv"), -1.0, A.mult, 1.0, A.add)
-        if r + 1 < RO:
+        if not end:
+            act("WMARK nadv", "WMO", T.WMO[:, 0:143], T.WMARK[:, 0:143], F.Identity, scale=L("nadv"))
             ts("back sd slot", "so", L("so"), L("back"), L("sd"), A.mult, L("slot"), A.add)
-            ts("WMARK nadv", "WMO", T.WMO[:, 0:143], T.WMARK[:, 0:143], L("nadv"), A.mult)
-            ts("PWC so", "OFO", T.OFO[:], T.PWC[:], L("so"), A.add)
-            act(" ".join(skeys) + " OFO", "SO", T.SO[:], T.XS[:, 0:win].indirect(T.OFO[:]), F.Copy)
             ts("adv", "an", L("an"), L("adv"), float((r + 2) * 512), A.mult)
-            ts("WMARK adv", "WMN", T.WMN[:, 0:143], T.WMARK[:, 0:143], L("adv"), A.mult)
+            ts("PWC so", "OFO", T.OFO[:], T.PWC[:], L("so"), A.add)
+            act("WMARK adv", "WMN", T.WMN[:, 0:143], T.WMARK[:, 0:143], F.Identity, scale=L("adv"))
+            act(" ".join(skeys) + " OFO", "SO", T.SO[:], T.XS[:, 0:win].indirect(T.OFO[:]), F.Copy)
             ts("so nadv an", "slot", L("slot"), L("so"), L("nadv"), A.mult, L("an"), A.add)
             to_w("WMO SO", 7, 0, 32, T.WMO, T.SO, 0, True, False)
         ts("adv e back", "e", EE, L("adv"), EE, A.add, L("back"), A.subtract)
-        if r + 1 < RO:
+        if end:
+            old_put()
+        else:
             ts("PWC slot", "OFS", T.OFS[:], T.PWC[:], L("slot"), A.add)
         skeys += ["XSo%d" % r, "ds%d" % r]
         dkeys += ["XDo%d" % r, "dd%d" % r]
@@ -559,9 +668,13 @@ def rank_program(g, core, T, topo):
         tt("lo noh", "lo0", L("lo0", 3), LO, L("noh"), A.mult)
         tt("ha hb", "hi", HI, L("ha"), L("hb"), A.add)
         ts("uc U", "U", UU, L("uc"), 4000.0, A.add, UU, A.min)
-        tt("la lb", "last", LA, L("la"), L("lb"), A.add)
+        if not end:
+            ts("oh", "lb", L("lb", 3), L("oh"), float((r + 2) * 512), A.mult)
+            tt("last noh", "la", L("la", 3), LA, L("noh"), A.mult)
         ts("adv loe", "al", L("al"), L("adv"), L("loe"), A.mult)
         ts("back", "nb", L("nb"), L("back"), -1.0, A.mult, 1.0, A.add)
+        if not end:
+            tt("la lb", "last", LA, L("la"), L("lb"), A.add)
         ts("I3 e", "oq", L("oq", 3), T.I3[:, 0:3], EE, A.is_equal)
         ts("adv back", "ch", L("ch"), L("adv"), L("back"), A.add)
         ts("x nadv nb", "y", L("y"), L("x"), L("nadv"), A.mult, L("nb"), A.mult)
@@ -576,42 +689,32 @@ def rank_program(g, core, T, topo):
         tt("l2 hi", "l4", L("l4", 3), L("l2"), HI, A.max)
         tt("l4 tb", "l5", L("l5", 3), L("l4"), L("tb"), A.mult)
         tt("l3 l5", "lo", LO, L("l3"), L("l5"), A.add)
-        if r + 1 < RO:
-            derive()
-        if r == 0:
-            output_constants()
+        if not end:
+            derive(False)
+        if r + 2 == RO:
+            old_where()
+        for _ in range(2):
+            if spare:
+                spare.pop(0)()
 
     cp("lo hi", "YT", T.YT[:, 0:6], T.ST[:, 0:6])
     cp("e U", "YT+", T.YT[:, 6:8], T.ST[:, 9:11])
     dma("Y", "out", [(T.yt[:], T.YT[0::16, :])], "YT", "yt")
+    xs, xd, sk, dk = hs(T.XS, NSLOT - 1, 512), hs(T.XD, NSLOT - 1, 512), " ".join(skeys[-2:]), " ".join(dkeys[-2:])
+    mm("TL4 " + sk, "ps5", b(5, 0, 512), T.TL4[:], xs, True, False)
     for l in (1, 2, 3):
-        ts("PWC last", "FO%d" % l, T["FO%d" % l][:, 0:32], T.PWC[:], T.ST[:, 5 + l:6 + l], A.add)
+        mm("DG%d %s" % (l - 1, sk), "ps%d" % l, b(l, 0, 512), DG[l - 1], xs, False, True)
+    mm("IM " + dk, "ps5", b(5, 0, 512), T.IM[:], xd, False, True)
     for l in (1, 2, 3):
-        o_ = T["FO%d" % l][:, 0:32]
-        cp(" ".join(skeys) + " FO%d" % l, "FS%d" % l, T["FS%d" % l][:], T.XS[:].indirect(o_))
-        act(" ".join(dkeys) + " FO%d" % l, "FC%d" % l, T["FC%d" % l][:], T.XD[:].indirect(o_), F.Copy)
-        mm("BLK FS%d" % l, "ps%d" % l, b(l, 0, 512), T.BLK[:], T["FS%d" % l][:])
-        mm("BCF FC%d" % l, "ps%d" % (3 + l), b(3 + l, 0, 512), T.BCF[:], T["FC%d" % l][:])
-    for l in (1, 2, 3):
-        fv, fa, fn = T["FV%d" % l][:], T["FA%d" % l][:, 0:512], T["FA%d" % l][:, 512:1024]
-        ts("ps%d" % l, "FL", T.FL[:], b(l, 0, 512), 0.25, A.mult, -0.375, A.add)
-        tt("FL ps%d" % (3 + l), "FV%d" % l, fv, T.FL[:], b(3 + l, 0, 512), A.add)
-        ts("FV%d hi" % l, "FA%d" % l, fa, fv, T.ST[:, 2 + l:3 + l], A.is_lt)
-        scan("RST FA%d" % l, "FN%d" % l, fn, T.RST[:], fa, A.mult, A.add)
-        k = (7, 0, 3)[l - 1]
-        to_w("W16 FN%d" % l, k, 0, 32, T.W16, T["FA%d" % l], 512)
-        to_w("W16 FA%d" % l, k, 32, 32, T.W16, T["FA%d" % l], 0)
-    for l in (1, 2, 3):
-        k = (7, 0, 3)[l - 1]
-        fo = T["FO%d" % l][:, 32:64]
-        w1, w2 = T.WX[:, l * 64 - 64:l * 64 - 32], T.WX[:, l * 64 - 32:l * 64]
-        tt("ps%d K1" % k, "w1%d" % l, w1, b(k, 0, 32), T.K1[:], A.add)
-        tt("ps%d w1%d" % (k, l), "w2%d" % l, w2, b(k, 32, 64), w1, A.mult)
-        tt("w2%d K2" % l, "w1%d" % l, w1, w2, T.K2[:], A.add)
-        ts("w1%d" % l, "FP%d" % l, fo, w1, 1.0 / 256, A.mult)
-        o1, o2 = T["OS%d" % l], T["OV%d" % l]
-        cp("FP%d FS%d OS%d" % (l, l, l), "OS%d" % l, o1[:].indirect(fo), T["FS%d" % l][:])
-        dma("Y", "out", [(T.yl[:, (l - 1) * 512:l * 512], o1[:, 0:512])], "OS%d" % l, "yl%d" % l)
-        cp("FP%d FV%d OV%d" % (l, l, l), "OV%d" % l, o2[:].indirect(fo), T["FV%d" % l][:])
-        dma("Y", "out", [(T.yf[:, (l - 1) * 512:l * 512], o2[0::16, 0:512])], "OV%d" % l, "yf%d" % l)
+        o = hs(T.OS, l - 1, 512)
+        if l == 2:
+            cp("ps2", "OS2", o, b(2, 0, 512))
+        else:
+            act("ps%d" % l, "OS%d" % l, o, b(l, 0, 512), F.Copy)
+    dma("S", "out", [(T.yl[:], T.OS[:])], "OS1 OS2 OS3", "yl")
+    fx = T.FX[:, 1056:1568]
+    ts("ps5", "FX2", fx, b(5, 0, 512), M4, A.add, M4, A.subtract)
+    mm("LC2 FX2", "ps4", b(4, 0, 512), hs(T.LC, 2, 128), fx, False, True)
+    ts("ps4", "OV", T.OV[:], b(4, 0, 512), 1023.0, A.min)
+    dma("Y", "out", [(T.yf[:, l * 512:l * 512 + 512], T.OV[32 * l:32 * l + 8, :]) for l in range(3)], "OV", "yf")
     need("G", list(cnt.items()) + [("%s%d" % (s, r), arrive) for s in ("bm", "ds", "dd") for r in range(RO)])

from concourse.bass import DstId, RemoteDMATransfer
from concourse.mybir import AluOpType as A, AxisListType, ActivationFunctionType as F

RO = 9
NSLOT = RO + 2
KA = [17, 101, 263, 389, 547, 701, 859, 1021]
WTS = [1, 3, 7, 13, 21, 35, 49, 67, 85, 107, 129, 155, 181, 211, 241, 253]
CW = 4112
OW = 8192 + 1632
GAP = 1024
ST_ = 272
BIG = 32768.0
M0, M2, M4 = 1.5 * 2 ** 23, 1.5 * 2 ** 13, 1.5 * 2 ** 25
SSTEP = (1, 3)

SCRATCH = {"PS": ("psum", [128, 4096], "float32")}
for _dt, _names in (
        ("bfloat16", "OPS:%d CH:4112 FB:528 DY:3072 RAW:1024 SS:512 SO:512 SF:512 IN0:1024 BASE:1024 SC:1088 P3:1088 C2:96 IN1:544 S1:544 KWX:272 RS17:272"
                     " IN2:512 IN3:512 KKP:512 MS:384 MD:384 OO:256 AW:32 C17:16 CN3:16 DL:64 ONE:272 TLM:128 WMARK:144 WMN:144 WMO:144 WPC:144 W15:144 W16:144"
                     " IDENT:128 IK:512 IM:128 BLK:128 TRIU:128 TRIL:128 LANEG:128 TMPA:128 CL:128"
                     " TL4:128 NTRIL:128 WE:144 KW8:256 RS8:256 C8:32 FS:1056 FC:1024 FX:1584 LV:64 SV:64 P3X:64 I8:512 S8:512 AX:64 I3X:1024"
                     " CS:1024 CD:1024 DG:640 LC:384 OS:1536" % OW),
        ("float16", "WSUM:144 KK:256 PEN:512 RR:256 PCW:32 CF:32"),
        ("float32", "BML:144 FA:512 KU:256 KMAT:256 F4:256 JUNK:768 TAU:48 DEL:48 YY:48 BB:4 GO:4 PP:32 MH:32 MX:32 MXT:32 MM:12 ST:16 LT:160"
                    " COL:40 WROW:48 I3:8 PWC:32 YT:8 PW2:32 RE0:16 OV:512"),
        ("int32", "FL:512 UI:128 OFP:256 OFM:256 LI:64 CI:160 C4:128 TI:16 F0:512"),
        ("uint16", "OFU:256 OFS:32 OFO:32 OF2:32 OF3:32 LU:32 LCU:32 REP:16 REP2:2 REP3:2 OFX:64 OX:64 LX:64")):
    for _n in _names.split():
        _n, _c = _n.split(":")
        SCRATCH[_n] = ("sbuf", [128, int(_c)], _dt)
SCRATCH["XS"] = ("sbuf", [128, NSLOT * 512], "bfloat16")
SCRATCH["XD"] = ("sbuf", [128, NSLOT * 512], "bfloat16")

SEMAPHORES = (["qV", "qS", "qP", "qG", "ld0", "ld1", "ld2", "ld3", "out", "lsb", "lsa", "lsd"]
              + ["%s%d" % (s, r) for s in ("bm", "ds", "dd") for r in range(RO)])


def rank_program(g, core, T, topo):
    rank = T.rank_of(core)
    if rank is None:
        return
    cores = list(T.cores)
    eng = {"V": g.vector, "S": g.scalar, "P": g.tensor, "G": g, "Y": g.sync}
    qs = {"V": "qV", "S": "qS", "P": "qP", "G": "qG"}
    cnt, snap, lastw, readers = {}, {}, {}, {}
    known = {q: {} for q in eng}

    def need(q, toks):
        best = {}
        for s, v in toks:
            if known[q].get(s, 0) < v:
                best[s] = max(best.get(s, 0), v)
        for s in sorted(best):
            v = best[s]
            if known[q].get(s, 0) < v:
                eng[q].wait_ge(T.sem[s], v)
                known[q][s] = v
                for s2, v2 in snap.get((s, v), {}).items():
                    known[q][s2] = max(known[q].get(s2, 0), v2)

    def deps(q, r, w):
        own = qs.get(q)
        toks = []
        for k in r:
            if k in lastw:
                toks.append(lastw[k])
            if k[:2] == "ps":
                toks += [t for t in readers.get(k, {}).items() if t[0] != own]
        for k in w:
            k, more = k.rstrip("+"), k[-1] == "+" or k[:2] == "ps"
            if k in lastw and not (more and lastw[k][0] == own):
                toks.append(lastw[k])
            toks += readers.get(k, {}).items()
        return toks

    def mark(q, tok, r, w):
        snap[tok] = dict(known[q])
        for k in r:
            readers.setdefault(k, {})[tok[0]] = tok[1]
        for k in w:
            k = k.rstrip("+")
            lastw[k] = tok
            readers[k] = {}

    def do(q, f, r, w):
        r, w = r.split(), w.split()
        need(q, deps(q, r, w))
        s = qs[q]
        f(eng[q]).then_inc(T.sem[s], 1)
        cnt[s] = cnt.get(s, 0) + 1
        mark(q, (s, cnt[s]), r, w)

    def dma(q, sem, pairs, r, w):
        r, w = r.split(), w.split()
        need(q, deps(q, r, w))
        for out, in_ in pairs:
            eng[q].dma_start(out, in_).then_inc(T.sem[sem], 16)
            cnt[sem] = cnt.get(sem, 0) + 16
        mark(q, (sem, cnt[sem]), r, w)

    def V(f, r, w):
        do("V", f, r, w)

    def ts(r, w, out, i, s1, o0, s2=None, o1=None):
        if o1 is None:
            V(lambda e: e.tensor_scalar(out, i, s1, None, o0), r, w)
        else:
            V(lambda e: e.tensor_scalar(out, i, s1, s2, o0, o1), r, w)

    def tt(r, w, out, a, b_, op):
        V(lambda e: e.tensor_tensor(out, a, b_, op), r, w)

    def cp(r, w, out, i):
        V(lambda e: e.tensor_copy(out, i), r, w)

    def red(r, w, out, i, op):
        V(lambda e: e.tensor_reduce(out, i, AxisListType.X, op), r, w)

    def fill(w, out, c, r=""):
        V(lambda e: e.memset(out, c), r, w)

    def scan(r, w, out, a, b_, o0, o1):
        V(lambda e: e.tensor_tensor_scan(out, a, b_, 0.0, o0, o1), r, w)

    def mm(r, w, out, l, r_, st=True, sp=True):
        do("P", lambda e: e.matmul(out, l, r_, st, sp), r, w)

    def act(r, w, out, i, fn, **k):
        do("S", lambda e: e.activation(out, i, fn, **k), r, w)

    def iota(w, out, pat, base=0, cm=0, small=True):
        if small:
            do("G", lambda e: e.iota(out, pat, base, cm, allow_small_or_imprecise_dtypes=True), "", w)
        else:
            do("G", lambda e: e.iota(out, pat, base, cm), "", w)

    def pick(r, w, out, i, pat, op, other, base, cm):
        do("G", lambda e: e.affine_select(out, i, pat, op, other, base, cm), r, w)

    def b(k, x, y):
        return T.PS[:, k * 512 + x:k * 512 + y]

    def hs(t, h, n=16):
        return t[:, h * n:h * n + n]

    def to_w(r, k, x, n, wt, src, c0, first=True, last=True):
        for q in range(16):
            mm(r, "ps%d" % k, b(k, x, x + n), wt[:, 15 - q:143 - q], src[:, c0 + q:c0 + 16 * n:16], first and q == 0, last and q == 15)

    off = [c for c in cores if topo.chip(c) != topo.chip(core)]
    near = [c for c in cores if topo.chip(c) == topo.chip(core) and c != core][0]
    far_e = list(topo.engines(core, off[0]))
    near_e = [e for e in topo.engines(core, near) if e not in far_e]
    ne = len(far_e) // len(off)
    lane = {c: far_e[i * ne:(i + 1) * ne] for i, c in enumerate(off)}
    lane[near] = near_e[:ne]
    ow = [cores.index(c) for c in off + [near, core]]
    low = [float(GAP * (o - 2)) for o in ow]
    arrive = ne * (len(cores) - 1)

    def send(local, parts, keys):
        keys = keys.split()
        need("G", deps("G", keys, []))
        tr = []
        for c, en, sem, src, dst in parts:
            rid, pid, _ = topo.addr(c)
            tr.append(RemoteDMATransfer(dst_ids=[DstId(rid=rid, pnc=pid)], dma_engine_mask=sum(1 << e for e in en),
                                        remote_sem=T.sem[sem], srcs=[src], dsts=[dst]))
            lastw[sem] = (sem, arrive)
        g.remote_dma_fused(tr, local_sem=T.sem[local])
        cnt[local] = cnt.get(local, 0) + ne * len(parts)
        mark("G", (local, cnt[local]), keys, [])

    dma("S", "ld0", [(T.XS[:, 0:512], T.s0[:])], "", "XS0")
    dma("Y", "ld2", [(T.OPS[:, 0:8192], T.opr[:])], "", "OPS")
    fill("F0", T.F0[:], 0)
    dma("S", "ld1", [(T.F0[0::16, :], T.f0[:]), (T.F0[1::16, :], T.f0[:])], "", "F0")
    dma("Y", "ld3", [(T.OPS[:, 8192:OW], T.opr[:, 0:OW - 8192])], "", "OPX")

    iota("TI", T.TI[:, 0:1], [[1, 1]], 0, 1, False)
    iota("CI", T.CI[:], [[1, 160]], small=False)
    iota("PW2", T.PW2[:], [[16, 32]])
    iota("RE0", T.RE0[:], [[0, 8], [16, 2]])
    iota("C4", T.C4[:], [[1, 8], [0, 16]], small=False)
    for j in range(8):
        iota("KMAT+", hs(T.KMAT, j, 32), [[0, 32]], KA[j])
    iota("CL", T.CL[:], [[0, 8], [1, 16]], 1)

    def C(k):
        return T.COL[:, k:k + 1]

    def TI(k):
        return T.TI[:, k:k + 1]
    ci = T.CI[:, 0:128]
    cw = T.CI[:, 0:143]
    for i in range(16):
        fill("wr+", T.WROW[:, i:i + 1], WTS[i])
    fill("ONE", T.ONE[:], 1.0)
    for k, sh, an in ((1, 0, 15), (2, 4, 7), (3, 4, 1), (4, 0, 7), (5, 3, 1)):
        ts("TI", "TI%d" % k, TI(k), TI(0), sh, A.logical_shift_right, an, A.bitwise_and)
    for k in (1, 2, 3):
        cp("TI%d" % k, "c%d" % k, C(k), TI(k))
    ts("CI c1", "wm", T.WROW[:, 16:32], T.CI[:, 0:16], C(1), A.is_equal)
    ts("c2", "c13", C(13), C(2), 16.0, A.mult, 15.0, A.add)
    tt("wr wm", "wx", T.WROW[:, 32:48], T.WROW[:, 0:16], T.WROW[:, 16:32], A.mult)
    ts("RE0 c1", "REP", T.REP[:], T.RE0[:], C(1), A.add)
    red("wx", "c7", C(7), T.WROW[:, 32:48], A.add)
    ts("c1", "c26", C(26), C(1), 0.0, A.is_equal)
    ts("CI c13 c7", "WMARK", T.WMARK[:, 0:143], cw, C(13), A.is_equal, C(7), A.mult)
    to_w("WMARK XS0", 7, 0, 32, T.WMARK, T.XS, 0)
    ts("c1", "c27", C(27), C(1), 1.0, A.is_equal, 4.0, A.mult)
    ts("c1", "c28", C(28), C(1), 15.0, A.is_equal, 4.0, A.mult)
    ts("c26 c28", "c20", C(20), C(26), 128.0, A.mult, C(28), A.add)
    ts("c27", "c21", C(21), C(27), -32.0, A.mult)
    ts("c26 c21", "c22", C(22), C(26), 4.0, A.mult, C(21), A.add)
    ts("c1", "c10", C(10), C(1), 4.5, A.is_lt)
    ts("c26 c10", "c9", C(9), C(26), 31.0, A.mult, C(10), A.add)
    cp("c7", "wi0", TI(8), C(7))
    ts("c9", "c11", C(11), C(9), 0.25, A.mult)
    ts("wi0", "wi1", TI(9), TI(8), 3, A.bitwise_and)
    ts("CI c13 c11", "WPC", T.WPC[:, 0:143], cw, C(13), A.is_equal, C(11), A.mult)
    ts("wi1", "c8", C(8), TI(9), -1.0 / 4096, A.mult, 1026.0 / 4096, A.add)
    ts("C4 c2", "BLK", T.BLK[:], T.C4[:], C(2), A.is_equal)
    ts("CI c13 c8", "WSUM", T.WSUM[:, 0:143], cw, C(13), A.is_equal, C(8), A.mult)
    ts("F0", "FL", T.FL[:], T.F0[:], 5, A.logical_shift_right)
    ts("F0 c27 c28", "ps6", b(6, 0, 512), T.F0[:], C(27), A.mult, C(28), A.add)
    ts("FL c22", "FA", T.FA[:], T.FL[:], C(22), A.mult)
    fill("XS1", T.XS[:, 512:1024], 0.0)
    tt("FA ps6", "XD0", T.XD[:, 0:512], T.FA[:], b(6, 0, 512), A.add)
    act("XS1 c20", "XD1", T.XD[:, 512:1024], T.XS[:, 512:1024], F.Identity, bias=C(20))
    act("XS1 c20", "FBz", T.FB[:, 512:528], T.XS[:, 512:528], F.Identity, bias=C(20))
    fill("lo hi last e U", T.ST[:], 0.0)
    fill("DL", T.DL[:], -71.0 / 8192)
    fill("last", T.ST[:, 6:9], 512.0)
    fill("U", T.ST[:, 10:11], 1023.0)
    cp("CI", "I3", T.I3[:, 0:3], T.CI[:, 0:3])
    ts("CI", "J3", T.I3[:, 4:7], T.CI[:, 0:3], 1.0, A.add)
    for i in range(4):
        fill("GO+", T.GO[:, i:i + 1], low[i])
    pick("ONE", "IDENT", T.IDENT[:], T.ONE[:, 0:128], [[-1, 128]], A.is_equal, 0.0, 0, 1)
    INEG, I45, IG, I16 = [hs(T.IK, k, 128) for k in range(4)]
    for nm, t, v in (("INEG", INEG, -1.0), ("I45", I45, 45.0), ("IG", IG, GAP * 4096.0), ("I16", I16, 16.0)):
        act("IDENT", nm, t, T.IDENT[:], F.Identity, scale=v)
    zero = ow.index(0)
    iota("BASE%d" % zero, hs(T.BASE, zero, 256), [[0, 256]])
    for i in range(4):
        iota("SCz+", T.SC[:, i * ST_:i * ST_ + 16], [[0, 16]])
        iota("P3z+", T.P3[:, i * ST_:i * ST_ + 16], [[0, 16]])
    iota("CHz", T.CH[:, 4096:CW], [[0, 16]])
    iota("KWX", T.KWX[:], [[16, 8], [0, 34]])
    iota("KKP", T.KKP[:], [[0, 4], [1, 128]])
    iota("C17", T.C17[:], [[17, 2], [0, 8]])
    iota("CN3", T.CN3[:], [[-256 * 17, 2], [0, 8]], -256)
    pick("ONE", "RS17", T.RS17[:], T.ONE[:], [[0, 16], [1, 17]], A.is_gt, 0.0, 0, 0)
    pick("BLK", "TRIU", T.TRIU[:], T.BLK[:], [[1, 128]], A.is_ge, 0.0, 0, -1)
    pick("BLK", "TRIL", T.TRIL[:], T.BLK[:], [[-1, 128]], A.is_gt, 0.0, 0, 1)
    for k in (2, 3):
        iota("BMz+", T.BML[:, rank * 4 + k::16], [[0, RO]])
    iota("KW8", T.KW8[:], [[16, 8], [0, 32]])
    iota("C8", T.C8[:], [[8, 4], [0, 8]])
    pick("ONE", "RS8", T.RS8[:], T.ONE[:, 0:256], [[0, 32], [1, 8]], A.is_gt, 0.0, 0, 0)
    for n in (0, 1):
        iota("FSz+", T.FS[:, n * 528 + 512:n * 528 + 528], [[0, 16]])

    LO, HI, LA, EE, UU = T.ST[:, 0:3], T.ST[:, 3:6], T.ST[:, 6:9], T.ST[:, 9:10], T.ST[:, 10:11]
    lt = {}

    def L(name, k=1):
        if name not in lt:
            lt[name] = (sum(v[1] for v in lt.values()), k)
        x, k = lt[name]
        return T.LT[:, x:x + k]

    def L1(name, i, n=1):
        x = lt[name][0] + i
        return T.LT[:, x:x + n]

    def derive(first):
        ts("I3 e", "oh", L("oh", 3), T.I3[:, 0:3], EE, A.is_equal)
        ts("J3 e", "oh1", L("oh1", 3), T.I3[:, 4:7], EE, A.is_equal)
        if not first:
            ts("oh e", "e1", L("e1"), L1("oh", 0), 97.0, A.mult, EE, A.add)
        ts("e", "e811", L("e811"), EE, 811.0, A.mult)
        if not first:
            ts("LANEG e1", "TLM", T.TLM[:], T.LANEG[:], -2.0, A.add, L("e1"), A.is_equal)
        tt("oh1 hi", "th", L("th", 3), L("oh1"), HI, A.mult)
        tt("oh lo", "ol", L("ol", 3), L("oh"), LO, A.mult)
        red("th", "th1", L("th1"), L("th"), A.add)
        ts("I3 e", "noh", L("noh", 3), T.I3[:, 0:3], EE, A.not_equal)
        red("ol", "loe", L("loe"), L("ol"), A.add)
        ts("oh th1", "thr", L("thr"), L1("oh", 0), 2000.0, A.mult, L("th1"), A.add)

    fill("slot", L("slot"), 0.0)
    derive(True)

    def more_constants():
        ts("GO", "t0", T.TAU[:, 0:4], T.GO[:], 512.0, A.add)
        ts("CI", "TA", T.TMPA[:, 0:32], T.CI[:, 0:32], 15.5, A.is_gt)
        ts("c1", "c12", C(12), C(1), 14.5, A.is_lt)
        ts("TA c3", "MH", T.MH[:], T.TMPA[:, 0:32], C(3), A.not_equal, 20000.0, A.mult)
        ts("CI c13 c12", "W15", T.W15[:, 0:143], cw, C(13), A.is_equal, C(12), A.mult)
        ts("CI c13", "W16", T.W16[:, 0:143], cw, C(13), A.is_equal)
        ts("TI4", "c14", C(14), TI(4), 34.0, A.mult, 16.0, A.add)
        ts("PW2 c1", "PWC", T.PWC[:], T.PW2[:], C(1), A.add)
        ts("TI5 c14", "REP2", T.REP2[:, 0:1], TI(5), 17.0, A.mult, C(14), A.add)
        ts("BLK c28", "TA", T.TMPA[:], T.BLK[:], C(28), A.mult, -0.09375, A.mult)
        tt("CL BLK", "LANEG", T.LANEG[:], T.CL[:], T.BLK[:], A.mult)
        tt("IDENT TA", "IM", T.IM[:], T.IDENT[:], T.TMPA[:], A.add)

    late = [lambda: ts("KWX c1", "KWX", T.KWX[:], T.KWX[:], C(1), A.add),
            lambda: fill("KWX", T.KWX[:, 16::17], -1024.0)]
    spare = [lambda: ts("KW8 c1", "KW8", T.KW8[:], T.KW8[:], C(1), A.add),
             lambda: fill("KW8", T.KW8[:, 7::8], -1024.0),
             lambda: ts("LANEG", "TL4", T.TL4[:], T.LANEG[:], 5.0, A.is_equal),
             lambda: ts("TRIL", "NTRIL", T.NTRIL[:], T.TRIL[:], -1.0, A.mult),
             lambda: ts("c28 c12", "c16", C(16), C(28), 128.0, A.mult, C(12), A.add),
             lambda: ts("CI c13 c16", "WE", T.WE[:, 0:143], cw, C(13), A.is_equal, C(16), A.mult),
             lambda: ts("TI4", "c17", C(17), TI(4), 32.0, A.mult, 7.0, A.add),
             lambda: ts("TI5 c17", "c18", C(18), TI(5), 8.0, A.mult, C(17), A.add),
             lambda: ts("CI c18", "REP3", T.REP3[:], T.CI[:, 0:2], 16.0, A.mult, C(18), A.add),
             lambda: ts("XS1 c20", "FXz+", T.FX[:, 512:528], T.XS[:, 512:528], C(20), A.add),
             lambda: ts("XS1 c20", "FXz+", T.FX[:, 1040:1056], T.XS[:, 512:528], C(20), A.add)]

    def pick3(name, x, i, j, sel):
        u, v = T.ST[:, x + i:x + i + 1], T.ST[:, x + j:x + j + 1]
        tt("last hi", name + "d", L(name + "d"), v, u, A.subtract)
        ts("last hi oh %sd" % name, name, L(name), L(name + "d"), sel, A.mult, u, A.add)

    def old_where():
        for n, (i, k) in enumerate(((0, 0), (2, 2))):
            pick3("sx%d" % n, 6, i, 1, L1("oh", k))
            pick3("hx%d" % n, 3, i, 1, L1("oh", k))
            ts("PWC sx%d" % n, "OFX%d" % n, hs(T.OFX, n, 32), T.PWC[:], L("sx%d" % n), A.add)
        ts("oh c2", "lc0", L("lc0"), L1("oh", 0), 32.0, A.mult, C(2), A.add)
        ts("noh", "lcx", L("lcx"), L1("noh", 2), 32.0, A.mult, 32.0, A.add)
        ts("e c2", "lc2", L("lc2"), EE, 32.0, A.mult, C(2), A.add)
        tt("lcx c2", "lc1", L("lc1"), L("lcx"), C(2), A.add)
        for n in range(3):
            ts("lc%d CI c11" % n, "LC%d" % n, hs(T.LC, n, 128), ci, L("lc%d" % n), A.is_equal, C(11), A.mult)

    def old_take(sk, dk, win):
        for n in (0, 1):
            act(dk + " OFX%d" % n, "FC%d" % n, hs(T.FC, n, 512), T.XD[:, 0:win].indirect(hs(T.OFX, n, 32)), F.Copy)
        act(sk + " OFX0", "FS0", T.FS[:, 0:512], T.XS[:, 0:win].indirect(hs(T.OFX, 0, 32)), F.Copy)

    def old_front(sk, win):
        cp(sk + " OFX1", "FS1", T.FS[:, 528:1040], T.XS[:, 0:win].indirect(hs(T.OFX, 1, 32)))
        for n in (0, 1):
            mm("TL4 FS%d" % n, "ps%d" % n, b(n, 0, 512), T.TL4[:], T.FS[:, n * 528:n * 528 + 512], True, False)
            mm("IM FC%d" % n, "ps%d" % n, b(n, 0, 512), T.IM[:], hs(T.FC, n, 512), False, True)
        for k, sel in enumerate((L1("oh", 0), L1("oh", 1), L1("oh", 2), L1("noh", 0), L1("noh", 2))):
            act("IDENT oh noh", "DG%d" % k, DG[k], T.IDENT[:], F.Identity, scale=sel)
        for n in (0, 1):
            ts("ps%d" % n, "FX%d" % n, T.FX[:, n * 528:n * 528 + 512], b(n, 0, 512), M4, A.add, M4, A.subtract)
            to_w("WPC FX%d" % n, 2 + n, 0, 32, T.WPC, T.FX, n * 528)
        for n in (0, 1):
            ts("ps%d hx%d" % (2 + n, n), "LV%d" % n, hs(T.LV, n, 32), b(2 + n, 0, 32), L("hx%d" % n), A.is_lt)
        for n in (0, 1):
            sv = hs(T.SV, n, 32)
            scan("RS8 LV%d" % n, "SV%d" % n, sv, T.RS8[:, 0:32], hs(T.LV, n, 32), A.mult, A.add)
            for c in range(8):
                mm("BLK SV%d" % n, "ps%d" % (6 + n), b(6 + n, c * 32, c * 32 + 32), T.BLK[:], sv)
            mm("BLK SV%d" % n, "ps%d" % (4 + n), b(4 + n, 0, 32), T.BLK[:], sv, True, False)
            mm("NTRIL LV%d" % n, "ps%d" % (4 + n), b(4 + n, 0, 32), T.NTRIL[:], hs(T.LV, n, 32), False, True)
            act("ps%d" % (4 + n), "P3X%d" % n, hs(T.P3X, n, 32), b(4 + n, 0, 32), F.Copy)
        for n in (0, 1):
            tt("ps%d KW8" % (6 + n), "I8%d" % n, hs(T.I8, n, 256), b(6 + n, 0, 256), T.KW8[:], A.is_le)
        for n in (0, 1):
            scan("RS8 I8%d" % n, "S8%d" % n, hs(T.S8, n, 256), T.RS8[:], hs(T.I8, n, 256), A.mult, A.add)
        for n in (0, 1):
            tt("S8%d REP3 C8" % n, "AX%d" % n, hs(T.AX, n, 32), hs(T.S8, n, 256).indirect(T.REP3[:]), T.C8[:], A.add)
        for n in (0, 1):
            cp("AX%d" % n, "OX%d" % n, hs(T.OX, n, 32), hs(T.AX, n, 32))

    DG = [hs(T.DG, k, 128) for k in range(5)]
    parts = ((1, 3, 0), (2, 0, 0), (2, 2, 1), (3, 4, 1))

    def old_back():
        for n in (0, 1):
            tt("P3X%d OX%d KKP" % (n, n), "I3X%d" % n, hs(T.I3X, n, 512), hs(T.P3X, n, 32).indirect(hs(T.OX, n, 32)), T.KKP[:], A.is_le)
            mm("I16 AX%d" % n, "ps%d" % (6 + n), b(6 + n, 0, 32), I16, hs(T.AX, n, 32), True, False)
            to_w("WE I3X%d" % n, 6 + n, 0, 32, T.WE, T.I3X, n * 512, False, True)

    def old_list(n):
        ts("ps%d" % (6 + n), "LX%d" % n, hs(T.LX, n, 32), b(6 + n, 0, 32), 512.0, A.min)
        if n == 0:
            act("FS0 FSz LX0", "CS0", hs(T.CS, 0, 512), hs(T.FS, 0, 528).indirect(hs(T.LX, 0, 32)), F.Copy)
        act("FX%d FXz LX%d" % (n, n), "CD%d" % n, hs(T.CD, n, 512), hs(T.FX, n, 528).indirect(hs(T.LX, n, 32)), F.Copy)

    def old_put():
        cp("FS1 FSz LX1", "CS1", hs(T.CS, 1, 512), hs(T.FS, 1, 528).indirect(hs(T.LX, 1, 32)))
        for i, (l, k, n) in enumerate(parts):
            mm("DG%d CS%d" % (k, n), "ps%d" % l, b(l, 0, 512), DG[k], hs(T.CS, n, 512), i != 2, False)
        for n in (0, 1):
            mm("LC%d CD%d" % (n, n), "ps4", b(4, 0, 512), hs(T.LC, n, 128), hs(T.CD, n, 512), n == 0, False)

    skeys, dkeys = ["XS0", "XS1"], ["XD0", "XD1"]
    for r in range(RO):
        win = (r + 2) * 512
        end = r + 1 == RO
        if r == 0:
            SS, FB, ssk, fbk, opk, OPS = T.XS[:, 0:512], T.XD, "XS0", "XD0 XD1", "OPS", T.OPS[:, 0:8192]
        else:
            SS, FB, ssk, fbk, opk, OPS = T.SS[:], T.FB, "SS", "FB FBz", "OPS OPX", T.OPS[:]
            cp(" ".join(skeys) + " OFS", "SS", SS, T.XS[:, 0:win].indirect(T.OFS[:]))
            to_w("WMN " + " ".join(skeys[-2:]), 7, 0, 32, T.WMN, T.XS, win - 512, False, True)
            act(" ".join(dkeys) + " OFS", "SF", T.SF[:], T.XD[:, 0:win].indirect(T.OFS[:]), F.Copy)
            mm("TLM SS", "ps6", b(6, 0, 512), T.TLM[:], SS, True, False)
            mm("IM SF", "ps6", b(6, 0, 512), T.IM[:], T.SF[:], False, True)
            act("ps6", "FA", T.FA[:], b(6, 0, 512), F.Identity, bias=M4)
            act("FA", "FB", T.FB[:, 0:512], T.FA[:], F.Identity, bias=-M4)
        sst = T.XS if r == 0 else T.SS
        u = [hs(T.UI, k, 32) for k in range(4)]
        cp("ps7", "u0", u[0], b(7, 0, 32))
        ts("u0", "u1", u[1], u[0], 4095, A.bitwise_and)
        tt("u1", "u2", u[2], u[1], u[1], A.mult)
        tt("u1 REP KMAT", "KU", T.KU[:], u[1].indirect(T.REP[:]), T.KMAT[:], A.mult)
        ts("u2", "u3", u[3], u[2], 4, A.logical_shift_right)
        tt("u3 REP KU", "OFP", T.OFP[:], u[3].indirect(T.REP[:]), T.KU[:], A.add)
        ts("OFP", "OFM", T.OFM[:], T.OFP[:], 8191, A.bitwise_and)
        ts("OFM e811", "OFU", T.OFU[:], T.OFM[:], L("e811"), A.add)
        to_w("WPC " + fbk, 7, 32, 32, T.WPC, FB, 0)
        if r == 0:
            more_constants()

        def opj(j, x=0, y=512):
            return OPS.indirect(T.OFU[:, j * 32 + x // 16:j * 32 + y // 16])

        def vg(j, x=0, y=512):
            tt(opk + " OFU " + ssk, "DY%d.%d" % (j, x), T.DY[:, j * 512 + x:j * 512 + y], opj(j, x, y), sst[:, x:y], A.subtract)

        def ab(j, x=0, y=512):
            if j < 6:
                act("DY%d.%d" % (j, x), "CH%d+" % j, T.CH[:, j * 512 + x:j * 512 + y], T.DY[:, j * 512 + x:j * 512 + y], F.Abs)
            else:
                act("ps%d" % (j - 2), "CH%d" % j, hs(T.CH, j, 512), b(j - 2, 0, 512), F.Abs)

        def sg(j):
            raw = hs(T.RAW, j - 6, 512)
            act(opk + " OFU", "RAW%d" % j, raw, opj(j), F.Copy)
            mm("INEG " + ssk, "ps%d" % (j - 2), b(j - 2, 0, 512), INEG, SS, True, False)
            mm("IDENT RAW%d" % j, "ps%d" % (j - 2), b(j - 2, 0, 512), T.IDENT[:], raw, False, True)

        def sums(k):
            mm("I45 DL", "ps%d" % k, b(k, 0, 64), I45, T.DL[:], True, False)
            for h in (0, 32):
                mm("IDENT PCW", "ps%d" % k, b(k, h, h + 32), T.IDENT[:], T.PCW[:], False, False)
            to_w("WSUM CH%d CH%d" % (2 * k, 2 * k + 1), k, 0, 64, T.WSUM, T.CH, k * 1024, False, True)

        def keys(k):
            pk, x, y = "ps%d" % k, b(k, 0, 64), b(k, 64, 128)
            kk, p0, p1 = hs(T.KK, k, 64), hs(T.PEN, k, 64), hs(T.PEN, 4 + k, 64)
            ts(pk, "F4%d" % k, hs(T.F4, k, 64), x, M2, A.add, M2, A.subtract)
            ts(pk, "KK%d" % k, kk, x, M0, A.add, M0, A.subtract)
            tt(pk + " F4%d" % k, "OO%d" % k, hs(T.OO, k, 64), x, hs(T.F4, k, 64), A.subtract)
            ts("KK%d loe" % k, "PEN%d" % k, p0, kk, L("loe"), A.is_lt, 8192.0, A.mult)
            ts("KK%d" % k, "PEM%d" % k, p1, kk, float(GAP), A.is_ge, 8192.0, A.mult)
            mm("IDENT KK%d" % k, pk, y, T.IDENT[:], kk, True, False)
            mm("IG OO%d" % k, pk, y, IG, hs(T.OO, k, 64), False, False)
            mm("IDENT PEN%d" % k, pk, y, T.IDENT[:], p0, False, False)
            mm("IDENT PEM%d" % k, pk, y, T.IDENT[:], p1, False, True)

        def key16(k):
            ts("ps%d" % k, "RR+", hs(T.RR, k, 64), b(k, 64, 128), -0.5 * GAP, A.add)
            mm("IDENT KK%d" % k, "ps6", b(6, k * 64, k * 64 + 64), T.IDENT[:], hs(T.KK, k, 64), True, False)
            mm("IDENT PEN%d" % k, "ps6", b(6, k * 64, k * 64 + 64), T.IDENT[:], hs(T.PEN, k, 64), False, True)

        vg(0), sg(6), ab(0), vg(1)
        ts("ps7 thr", "PP", T.PP[:], b(7, 32, 64), L("thr"), A.is_ge, 1023.0, A.mult)
        sg(7), ab(1), vg(2)
        tt("ps7 PP", "PCW", T.PCW[:], b(7, 32, 64), T.PP[:], A.max)
        sums(0), ab(6), ab(2), vg(3), ab(7), sums(3), ab(3), sums(1), vg(4), ab(4)
        vg(5, 0, 256), ab(5, 0, 256), vg(5, 256, 512), ab(5, 256, 512)
        if end:
            old_take(" ".join(skeys), " ".join(dkeys), win)
        keys(0), keys(3), sums(2), keys(1), key16(0), key16(3), key16(1), keys(2), key16(2)

        def col(t, i, s):
            return t[:, 4 * s + i:4 * s + i + 1]

        def count(i, k, src, key, w, out, scale, bias, rk=""):
            for n in range(4):
                mm("BLK " + key, "ps%d" % k, b(k, 128, 192), T.BLK[:], hs(src, 4 * i + n, 64), n == 0, n == 3)
            act("ps%d %s" % (k, rk), "JUNK%d %s" % (i, w), hs(T.JUNK, i, 64), b(k, 128, 192), F.Identity, bias=bias, scale=scale, accum_out=out)

        def on_s(i, s):
            return i in SSTEP and 1 <= s < 9

        def step(i, s):
            hi_, lo_ = (256.0 / 2 ** s, -256.0 / 2 ** s) if s < 9 else (0.0, -1.0)
            if on_s(i, s):
                n = int(hi_)
                act("ONE y%d.%d" % (i, s), "JUNK%d d%d.%d" % (4 + i, i, s), T.JUNK[:, 256 + i * 128:256 + i * 128 + n], T.ONE[:, 0:n], F.Sign,
                    scale=col(T.YY, i, s), accum_out=col(T.DEL, i, s))
            else:
                ts("y%d.%d" % (i, s), "d%d.%d" % (i, s), col(T.DEL, i, s), col(T.YY, i, s), hi_, A.min, lo_, A.max)

        def compare(i, s):
            io = hs(T.IN0, i, 256)
            if s == 0:
                ts("RR", "IN%d" % i, io, T.RR[:], low[i] + 512.0, A.is_lt)
            elif s == 10 and end:
                ts("RR TG", "IN%d" % i, io, T.RR[:], T.MM[:, 8 + i:9 + i], A.is_lt)
            else:
                ts("RR d%d.%d t%d" % (i, s - 1, s - 1), "IN%d" % i, io, T.RR[:], col(T.DEL, i, s - 1), A.subtract, col(T.TAU, i, s - 1), A.is_lt)
            if s < 10:
                count(i, i, T.IN0, "IN%d" % i, "y%d.%d" % (i, s), col(T.YY, i, s), -BIG, T.BB[:, i:i + 1] if ow[i] else BIG * 128.5 / 64, "BB%d" % i)
                if on_s(i, s):
                    step(i, s)

        def prefix(i):
            x = i * ST_ + 16
            scan("IN%d BASE%d SCz" % (i, i), "SC%d" % i, T.SC[:, x:x + 256], hs(T.IN0, i, 256), hs(T.BASE, i, 256), A.add, A.subtract)

        def level(s):
            dk = " ".join("d%d.%d" % (i, s - 1) for i in range(4))
            tt(dk + " t%d" % (s - 1), "t%d" % s, hs(T.TAU, s, 4), hs(T.TAU, s - 1, 4), hs(T.DEL, s - 1, 4), A.add)

        x = r * 16 + rank * 4
        own = T.BML[:, x:x + 4]
        bk = "BMb%d BMm%d bm%d" % (r, r, r)
        extra = [lambda: red("ps6", "MM0", T.MM[:, 0:1], b(6, 0, 256), A.min),
                 lambda: ts("MM0 MH", "MX", T.MX[:], T.MH[:], T.MM[:, 0:1], A.add),
                 lambda: V(lambda e: e.transpose(T.MXT[:], T.MX[:]), "MX", "MXT"),
                 lambda: red("MXT", "BMm%d" % r, T.BML[:, x + 1:x + 2], T.MXT[:], A.min)]
        bound = [lambda: level(10),
                 lambda: tt("t10 GO", "TB4", T.MM[:, 4:8], hs(T.TAU, 10, 4), T.GO[:], A.subtract),
                 lambda: red("TB4", "BMb%d" % r, T.BML[:, x:x + 1], T.MM[:, 4:8], A.min),
                 lambda: send("lsb", [(c, lane[c], "bm%d" % r, own, own) for c in lane], "BMb%d BMm%d BMz" % (r, r))]
        for n, i in enumerate([i for i in range(4) if ow[i]]):
            ts("RR", "BASE%d" % i, hs(T.BASE, i, 256), T.RR[:], low[i], A.is_lt)
            count(i, (4, 5, 7)[n], T.BASE, "BASE%d" % i, "BB%d" % i, T.BB[:, i:i + 1], BIG / 64, BIG * 128.5 / 4096)

        def place1(h):
            sck = "SC%d SC%d SCz" % (2 * h, 2 * h + 1)
            z = h * 544
            for c in range(8):
                mm("BLK " + sck, "ps%d" % (4 + h), b(4 + h, c * 34, c * 34 + 34), T.BLK[:], T.SC[:, z + 15:z + 544:16])
            to_w("W16 " + sck, 6 + h, 0, 34, T.W16, T.SC, z)
            act("ps%d" % (6 + h), "C2%d" % h, T.C2[:, h * 48:h * 48 + 34], b(6 + h, 0, 34), F.Copy)
            for i in (0, 1):
                y = z + i * ST_ + 16
                mm("TRIU " + sck, "ps%d" % h, b(h, i * 256, i * 256 + 256), T.TRIU[:], T.SC[:, y:y + 256], True, False)
                mm("TRIL " + sck, "ps%d" % h, b(h, i * 256, i * 256 + 256), T.TRIL[:], T.SC[:, y - 1:y + 255], False, True)
            for i in (0, 1):
                y = z + i * ST_ + 16
                act("ps%d P3z" % h, "P3%d+" % h, T.P3[:, y:y + 256], b(h, i * 256, i * 256 + 256), F.Copy)

        def place2(h):
            return [lambda: tt("ps%d KWX" % (4 + h), "IN1%d" % h, hs(T.IN1, h, 272), b(4 + h, 0, 272), T.KWX[:], A.is_le),
                    lambda: scan("RS17 IN1%d" % h, "S1%d" % h, hs(T.S1, h, 272), T.RS17[:], hs(T.IN1, h, 272), A.mult, A.add),
                    lambda: tt("S1%d REP2 C17" % h, "AW%d" % h, hs(T.AW, h), hs(T.S1, h, 272).indirect(T.REP2[:, 0:1]), T.C17[:], A.add),
                    lambda: cp("AW%d" % h, "OF2%d" % h, hs(T.OF2, h), hs(T.AW, h))]

        def place3(h):
            tt("C2%d OF2%d KKP" % (h, h), "IN2%d" % h, hs(T.IN2, h, 256), T.C2[:, h * 48:h * 48 + 34].indirect(hs(T.OF2, h)), T.KKP[:, 0:256], A.is_le)
            mm("I16 AW%d" % h, "ps%d" % (2 + h), b(2 + h, 0, 16), I16, hs(T.AW, h), True, False)
            to_w("W15 IN2%d" % h, 2 + h, 0, 16, T.W15, T.IN2, h * 256, False, True)

        def place4(h):
            cp("ps%d" % (2 + h), "OF3%d" % h, hs(T.OF3, h), b(2 + h, 0, 16))
            cp("ps%d" % (2 + h), "CF%d" % h, hs(T.CF, h), b(2 + h, 0, 16))
            tt("P3%d P3z OF3%d KKP" % (h, h), "IN3%d" % h, hs(T.IN3, h, 256), hs(T.P3, h, 544).indirect(hs(T.OF3, h)), T.KKP[:, 0:256], A.is_le)
            mm("IDENT CN3", "ps%d" % (4 + h), b(4 + h, 0, 16), T.IDENT[:], T.CN3[:], True, False)
            mm("I16 CF%d" % h, "ps%d" % (4 + h), b(4 + h, 0, 16), I16, hs(T.CF, h), False, False)
            to_w("W16 IN3%d" % h, 4 + h, 0, 16, T.W16, T.IN3, h * 256, False, True)

        xo = (r + 2) * 512 + rank * 128
        chk = " ".join("CH%d" % j for j in range(8)) + " CHz"
        fbw = FB[:, 0:528]

        def place5(h):
            cp("ps%d" % (4 + h), "LU%d" % h, hs(T.LU, h), b(4 + h, 0, 16))
            cp("ps%d" % (4 + h), "LI%d" % h, hs(T.LI, h), b(4 + h, 0, 16))
            if h == 0:
                cp(chk + " LU0", "MS0", T.MS[:, 0:256], T.CH[:].indirect(hs(T.LU, 0)))
            else:
                cp(chk + " LU1", "MS1", T.MS[:, 256:384], T.CH[:].indirect(hs(T.LU, 2, 8)))
            ts("LI%d" % h, "LJ%d" % h, hs(T.LI, 2 + h), hs(T.LI, h), 4607, A.bitwise_and)
            if h == 1:
                cp(chk + " LU1", "XSo%d" % r, T.XS[:, xo:xo + 128], T.CH[:].indirect(hs(T.LU, 3, 8)))
            ts("LJ%d" % h, "LCU%d" % h, hs(T.LCU, h), hs(T.LI, 2 + h), 512.0, A.min)
            if h == 0:
                act(fbk + " LCU0", "MD0", T.MD[:, 0:256], fbw.indirect(hs(T.LCU, 0)), F.Copy)
            else:
                act(fbk + " LCU1", "MD1", T.MD[:, 256:384], fbw.indirect(hs(T.LCU, 2, 8)), F.Copy)
                act(fbk + " LCU1", "XDo%d" % r, T.XD[:, xo:xo + 128], fbw.indirect(hs(T.LCU, 3, 8)), F.Copy)

        for s in range(11):
            if s == 10 and end:
                for i in range(4):
                    step(i, 9)
                while bound:
                    bound.pop(0)()
                old_front(" ".join(skeys), win)
                red(bk, "B", L("B"), T.BML[:, r * 16:r * 16 + 16:4], A.min)
                ts("GO B", "TG", T.MM[:, 8:12], T.GO[:], L("B"), A.add)
            if s == 10:
                for h in (0, 1):
                    for f in ([] if end else [lambda i: step(i, 9)]) + [lambda i: compare(i, 10), prefix]:
                        f(2 * h), f(2 * h + 1)
                    place1(h)
                break
            for i in range(4):
                if s and not on_s(i, s - 1):
                    step(i, s - 1)
                compare(i, s)
            if s:
                level(s)
            if late:
                late.pop(0)()
            if s > 3 and extra:
                extra.pop(0)()
        pa, pb = place2(0), place2(1)
        for f in (pa, bound, pa, bound, pa, pb, pa, bound, bound):
            if f:
                f.pop(0)()
        place3(0)
        pb[0](), pb[1]()
        tt("hi noh", "ha", L("ha", 3), HI, L("noh"), A.mult)
        pb[2]()
        tt("last oh1", "sl", L("sl", 2), T.ST[:, 6:8], L1("oh1", 1, 2), A.mult)
        place3(1)
        place4(0)
        place4(1)
        place5(0)
        send("lsa", [(c, lane[c], "ds%d" % r, hs(T.MS, i, 128), T.XS[:, xo:xo + 128]) for i, c in enumerate(off)], "MS0")
        place5(1)
        send("lsd", [(near, near_e[ne:2 * ne], "ds%d" % r, hs(T.MS, 2, 128), T.XS[:, xo:xo + 128])]
             + [(c, lane[c], "dd%d" % r, hs(T.MD, i, 128), T.XD[:, xo:xo + 128]) for i, c in enumerate(off + [near])], "MS1 MD0 MD1")
        if end:
            old_back()
            old_list(0)
        else:
            red(bk, "B", L("B"), T.BML[:, r * 16:r * 16 + 16:4], A.min)
        red(bk, "M", L("M"), T.BML[:, r * 16 + 1:r * 16 + 16:4], A.min)
        if not end:
            red("sl", "sb", L("sb"), L("sl"), A.add)
        tt("B U", "mn", L("mn"), L("B"), UU, A.min)
        ts("loe B", "x", L("x"), L("loe"), 1.0, A.add, L("B"), A.max)
        ts("M B oh", "k2", L("k2"), L("M"), L("B"), A.is_lt, L1("oh", 2), A.mult)
        ts("M mn oh", "nadv", L("nadv"), L("M"), L("mn"), A.is_ge, L1("oh", 2), A.max)
        ts("x U noh", "xu", L("xu"), L("x"), UU, A.is_ge, L1("noh", 0), A.mult)
        if end:
            old_list(1)
        else:
            tt("sb slot", "sd", L("sd"), L("sb"), L("slot"), A.subtract)
        ts("xu nadv k2", "back", L("back"), L("xu"), L("nadv"), A.mult, L("k2"), A.max)
        ts("nadv", "adv", L("adv"), L("nadv"), -1.0, A.mult, 1.0, A.add)
        if not end:
            act("WMARK nadv", "WMO", T.WMO[:, 0:143], T.WMARK[:, 0:143], F.Identity, scale=L("nadv"))
            ts("back sd slot", "so", L("so"), L("back"), L("sd"), A.mult, L("slot"), A.add)
            ts("adv", "an", L("an"), L("adv"), float((r + 2) * 512), A.mult)
            ts("PWC so", "OFO", T.OFO[:], T.PWC[:], L("so"), A.add)
            act("WMARK adv", "WMN", T.WMN[:, 0:143], T.WMARK[:, 0:143], F.Identity, scale=L("adv"))
            act(" ".join(skeys) + " OFO", "SO", T.SO[:], T.XS[:, 0:win].indirect(T.OFO[:]), F.Copy)
            ts("so nadv an", "slot", L("slot"), L("so"), L("nadv"), A.mult, L("an"), A.add)
            to_w("WMO SO", 7, 0, 32, T.WMO, T.SO, 0, True, False)
        ts("adv e back", "e", EE, L("adv"), EE, A.add, L("back"), A.subtract)
        if end:
            old_put()
        else:
            ts("PWC slot", "OFS", T.OFS[:], T.PWC[:], L("slot"), A.add)
        skeys += ["XSo%d" % r, "ds%d" % r]
        dkeys += ["XDo%d" % r, "dd%d" % r]
        ts("oh B", "hb", L("hb", 3), L("oh"), L("B"), A.mult)
        ts("k2 M", "uc", L("uc"), L("k2"), -4000.0, A.mult, L("M"), A.add)
        tt("lo noh", "lo0", L("lo0", 3), LO, L("noh"), A.mult)
        tt("ha hb", "hi", HI, L("ha"), L("hb"), A.add)
        ts("uc U", "U", UU, L("uc"), 4000.0, A.add, UU, A.min)
        if not end:
            ts("oh", "lb", L("lb", 3), L("oh"), float((r + 2) * 512), A.mult)
            tt("last noh", "la", L("la", 3), LA, L("noh"), A.mult)
        ts("adv loe", "al", L("al"), L("adv"), L("loe"), A.mult)
        ts("back", "nb", L("nb"), L("back"), -1.0, A.mult, 1.0, A.add)
        if not end:
            tt("la lb", "last", LA, L("la"), L("lb"), A.add)
        ts("I3 e", "oq", L("oq", 3), T.I3[:, 0:3], EE, A.is_equal)
        ts("adv back", "ch", L("ch"), L("adv"), L("back"), A.add)
        ts("x nadv nb", "y", L("y"), L("x"), L("nadv"), A.mult, L("nb"), A.mult)
        ts("oq back", "tb", L("tb", 3), L("oq"), L("back"), A.mult)
        ts("oq ch", "tk", L("tk", 3), L("oq"), L("ch"), A.mult)
        tt("al y", "z", L("z"), L("al"), L("y"), A.add)
        ts("tk", "tn", L("tn", 3), L("tk"), -1.0, A.mult, 1.0, A.add)
        ts("oh z", "oz", L("oz", 3), L("oh"), L("z"), A.mult)
        tt("lo0 oz", "l1", L("l1", 3), L("lo0"), L("oz"), A.add)
        ts("l1", "l2", L("l2", 3), L("l1"), 1.0, A.add)
        tt("l1 tn", "l3", L("l3", 3), L("l1"), L("tn"), A.mult)
        tt("l2 hi", "l4", L("l4", 3), L("l2"), HI, A.max)
        tt("l4 tb", "l5", L("l5", 3), L("l4"), L("tb"), A.mult)
        tt("l3 l5", "lo", LO, L("l3"), L("l5"), A.add)
        if not end:
            derive(False)
        if r + 2 == RO:
            old_where()
        for _ in range(2):
            if spare:
                spare.pop(0)()

    cp("lo hi", "YT", T.YT[:, 0:6], T.ST[:, 0:6])
    cp("e U", "YT+", T.YT[:, 6:8], T.ST[:, 9:11])
    dma("Y", "out", [(T.yt[:], T.YT[0::16, :])], "YT", "yt")
    xs, xd, sk, dk = hs(T.XS, NSLOT - 1, 512), hs(T.XD, NSLOT - 1, 512), " ".join(skeys[-2:]), " ".join(dkeys[-2:])
    mm("TL4 " + sk, "ps5", b(5, 0, 512), T.TL4[:], xs, True, False)
    for l in (1, 2, 3):
        mm("DG%d %s" % (l - 1, sk), "ps%d" % l, b(l, 0, 512), DG[l - 1], xs, False, True)
    mm("IM " + dk, "ps5", b(5, 0, 512), T.IM[:], xd, False, True)
    for l in (1, 2, 3):
        o = hs(T.OS, l - 1, 512)
        if l == 2:
            cp("ps2", "OS2", o, b(2, 0, 512))
        else:
            act("ps%d" % l, "OS%d" % l, o, b(l, 0, 512), F.Copy)
    dma("S", "out", [(T.yl[:], T.OS[:])], "OS1 OS2 OS3", "yl")
    fx = T.FX[:, 1056:1568]
    ts("ps5", "FX2", fx, b(5, 0, 512), M4, A.add, M4, A.subtract)
    mm("LC2 FX2", "ps4", b(4, 0, 512), hs(T.LC, 2, 128), fx, False, True)
    ts("ps4", "OV", T.OV[:], b(4, 0, 512), 1023.0, A.min)
    dma("Y", "out", [(T.yf[:, l * 512:l * 512 + 512], T.OV[32 * l:32 * l + 8, :]) for l in range(3)], "OV", "yf")
    need("G", list(cnt.items()) + [("%s%d" % (s, r), arrive) for s in ("bm", "ds", "dd") for r in range(RO)])
